import numpy as np
import ml_dtypes


def mxq(x, axis, fmt="e4m3"):
    dtype, down = {"e4m3": (ml_dtypes.float8_e4m3fn, 7), "e5m2": (ml_dtypes.float8_e5m2, 14)}[fmt]
    v = np.moveaxis(np.asarray(x, np.float32).astype(ml_dtypes.bfloat16).astype(np.float64), axis, -1)
    blocks = v.reshape(v.shape[:-1] + (-1, 32))
    amax = np.abs(blocks).max(-1, keepdims=True)
    byte = np.maximum(np.where(amax > 0, np.frexp(amax)[1] - 1 + 127, 0) - down, 1)
    scale = np.exp2(byte - 127.0)
    codes = (blocks / scale).astype(np.float32).astype(dtype).astype(np.float64)
    return np.moveaxis((codes * scale).reshape(v.shape), -1, axis)


WIDE = False


def mx_kscale(k):
    if not WIDE:
        return np.ones(k)
    levels = np.array([10, -10, 5, -5, 0])
    if k % 512:
        return np.exp2(np.random.permutation(np.resize(levels, k // 32))).repeat(32)
    a = np.empty((k // 512, 16))
    for p in range(k // 512):
        a[p, :8] = np.random.permutation(np.resize(levels, 8))
        for g in range(8):
            far = levels[np.abs(levels - a[p, g]) >= 10]
            a[p, g + 8] = far[np.random.randint(len(far))]
    return np.exp2(a.ravel()).repeat(32)


BF16 = ml_dtypes.bfloat16


def bf(x):
    return np.asarray(x, np.float32).astype(BF16)


def f64(x):
    return np.asarray(x).astype(np.float64)


T, D, F, S, C = 1024, 1024, 1024, 512, 16

GELU_A = np.sqrt(2.0 / np.pi)
GELU_B = 0.044715


def gelu(z):
    return 0.5 * z * (1.0 + np.tanh(GELU_A * (z + GELU_B * z * z * z)))


def draw0():
    s = mx_kscale(D)
    ts = mx_kscale(T)
    te = mx_kscale(T)
    return {"x": bf(np.random.standard_normal((T, D)) * s),
            "ws": bf(np.random.standard_normal((D, F)) / np.sqrt(D) / s[:, None]),
            "we": bf(np.random.standard_normal((D, F)) / np.sqrt(D) / s[:, None]),
            "bs": bf(0.3 * np.random.standard_normal(F)),
            "be": bf(0.3 * np.random.standard_normal(F)),
            "gs": bf(np.random.uniform(0.5, 1.5, T) * ts),
            "ge": bf(np.random.uniform(0.5, 1.5, T) * te),
            "ps": bf(np.random.standard_normal((S, T)) / np.sqrt(T) / ts),
            "pe": bf(np.random.standard_normal((S, T)) / np.sqrt(T) / te),
            "mix": bf(1.0 + 0.1 * np.random.standard_normal(F)),
            "v": bf(np.random.standard_normal(F) / np.sqrt(F // C)),
            "d": bf(0.3 * np.random.standard_normal(C))}


def core(x, ws, we, bs, be, gs, ge, ps, pe, mix, v, d):
    xq = mxq(f64(x), 1, "e4m3")
    hs = gelu((xq @ mxq(f64(ws), 0, "e4m3")) + f64(bs)) * f64(gs)[:, None]
    he = gelu((xq @ mxq(f64(we), 0, "e4m3")) + f64(be)) * f64(ge)[:, None]
    a = mxq(f64(ps), 1, "e4m3") @ mxq(hs, 0, "e4m3")
    b = mxq(f64(pe), 1, "e4m3") @ mxq(he, 0, "e4m3")
    emb = a + b + f64(mix) * a * b
    score = (emb * f64(v)).reshape(S, C, F // C).sum(axis=2) + f64(d)
    return emb, score


def e4m3fn_bytes(y):
    return np.clip(np.asarray(y, np.float64), -448.0, 448.0).astype(np.float32).astype(ml_dtypes.float8_e4m3fn).view(np.uint8)


def e4m3fn_values(b):
    return np.asarray(b, np.uint8).view(ml_dtypes.float8_e4m3fn).astype(np.float64)


def setup_inputs():
    d = draw0()
    x0 = np.asarray(d['x']).astype(np.float64)
    s = (np.max(np.abs(x0), axis=(0,), keepdims=True) / 448.0).astype(np.float32)
    out = {}
    for k, v in d.items():
        if k == 'x':
            out['x_bytes'] = e4m3fn_bytes(x0 / s.astype(np.float64))
            out['x_scale'] = s
        else:
            out[k] = v
    return out


def reference(x_bytes, x_scale, ws, we, bs, be, gs, ge, ps, pe, mix, v, d):
    return core(e4m3fn_values(x_bytes) * x_scale.astype(np.float64), ws, we, bs, be, gs, ge, ps, pe, mix, v, d)

@@ -1,0 +1,366 @@
+from contextlib import ExitStack
+
+import concourse.mybir as mybir
+from concourse.masks import make_identity
+
+T, D, F, S, C = 1024, 1024, 1024, 512, 16
+FLOPS = 2 * 2 * T * D * F + 2 * 2 * S * T * F
+
+F32 = mybir.dt.float32
+BF16 = mybir.dt.bfloat16
+U32 = mybir.dt.uint32
+U8 = mybir.dt.uint8
+FP8 = mybir.dt.float8_e4m3fn
+FP8X4 = mybir.dt.float8_e4m3fn_x4
+ACT = mybir.ActivationFunctionType
+ALU = mybir.AluOpType
+
+P = 128
+NI = F // P
+NR = 2 * NI
+WCH = 256
+
+
+def tile_endpoint_span_scoring_f4_kernel(
+    tc, x_bytes, x_scale, ws, we, bs, be, gs, ge, ps, pe, mix, v, d, out_0, out_1
+):
+    nc = tc.nc
+    with ExitStack() as ctx:
+        keep = ctx.enter_context(tc.tile_pool(name="keep", bufs=1))
+        stage = ctx.enter_context(tc.tile_pool(name="stage", bufs=3))
+        zpool = ctx.enter_context(tc.psum_pool(name="zpool", bufs=2))
+        tpool = ctx.enter_context(tc.psum_pool(name="tpool", bufs=3))
+        apool = ctx.enter_context(tc.psum_pool(name="apool", bufs=2))
+        bpool = ctx.enter_context(tc.psum_pool(name="bpool", bufs=1))
+
+        ident = keep.tile([P, P], F32, name="ident")
+        make_identity(nc, ident[:])
+
+        xb = [keep.tile([P, 4, D], U8, name=f"xb{h}", align_bytes=64) for h in range(2)]
+        xw = [keep.tile([P, 4, D], BF16, name=f"xw{h}", align_bytes=64) for h in range(2)]
+        xs = keep.tile([P, 2, 4], F32, name="xs")
+        xcodes = keep.tile([P, 2, T], U32, name="xcodes", align_bytes=64)
+        xscales = keep.tile([P, 2, T], U8, name="xscales", align_bytes=64)
+        praw = [keep.tile([P, 4, T], BF16, name=f"praw{e}", align_bytes=64) for e in range(2)]
+        pcodes = [keep.tile([P, 2, S], U32, name=f"pcodes{e}", align_bytes=64) for e in range(2)]
+        pscales = [keep.tile([P, 2, S], U8, name=f"pscales{e}", align_bytes=64) for e in range(2)]
+        wraw = [
+            [keep.tile([P, 2, 4, WCH], BF16, name=f"wraw{e}_{c}", align_bytes=64) for c in range(F // WCH)]
+            for e in range(2)
+        ]
+        sal = [keep.tile([P, 2, 4, 4], BF16, name=f"sal{e}") for e in range(2)]
+        rows = keep.tile([P, P], BF16, name="rows")
+        rows32 = keep.tile([P, P], F32, name="rows32")
+        cols = keep.tile([P, 4, NI], F32, name="cols")
+        vmat = keep.tile([P, NI, 2], F32, name="vmat")
+        dt_ = keep.tile([P, C], BF16, name="dt_")
+        score = keep.tile([P, 4, C], F32, name="score")
+        warm = keep.tile([P, 1], F32, name="warm")
+
+        xv = x_bytes.rearrange("(h p j) k -> h p j k", h=2, p=P, j=4)
+        wv = [w.rearrange("(g p j) f -> g p j f", g=2, p=P, j=4) for w in (ws, we)]
+        pv = [q.rearrange("(st r) t -> r st t", r=P) for q in (ps, pe)]
+
+        def load_w(e, c):
+            for g in range(2):
+                nc.sync.dma_start(out=wraw[e][c][:, g, :, :], in_=wv[e][g][:, :, c * WCH : (c + 1) * WCH])
+
+        nc.vector.memset(rows[:], 0.0)
+        nc.sync.dma_start(out=xb[0][:, 0:2, :], in_=xv[0][:, 0:2, :])
+        nc.sync.dma_start(out=xb[0][:, 2:4, :], in_=xv[0][:, 2:4, :])
+        nc.sync.dma_start(out=xs[:], in_=x_scale.rearrange("o (g p t) -> p (o g) t", p=P, t=4))
+        for q, vec in enumerate((bs, be, mix, v)):
+            nc.gpsimd.dma_start(out=rows[NI * q : NI * (q + 1), :], in_=vec.rearrange("(i f) -> i f", f=P))
+        for e, gv in enumerate((gs, ge)):
+            nc.gpsimd.dma_start(out=sal[e][:, :, 0, :], in_=gv.rearrange("(h m j) -> m h j", h=2, j=4))
+        nc.gpsimd.dma_start(out=dt_[:], in_=d.partition_broadcast(P))
+
+        def load_p(e):
+            for k in range(2):
+                nc.sync.dma_start(out=praw[e][:, 2 * k : 2 * k + 2, :], in_=pv[e][:, 2 * k : 2 * k + 2, :])
+
+        load_p(0)
+        load_w(0, 0)
+        nc.sync.dma_start(out=xb[1][:], in_=xv[1])
+        load_w(1, 0)
+        load_p(1)
+        for c in range(1, F // WCH):
+            load_w(0, c)
+            load_w(1, c)
+
+        nc.vector.memset(warm[:], 0.0)
+        nc.scalar.activation(out=warm[:], in_=warm[:], func=ACT.Gelu_apprx_tanh)
+
+        def cast_x(eng, h, j):
+            src = xb[h][:, j, :].bitcast(FP8)
+            if eng is nc.scalar:
+                nc.scalar.copy(out=xw[h][:, j, :], in_=src)
+            else:
+                nc.vector.tensor_copy(out=xw[h][:, j, :], in_=src)
+
+        def words_t(tp, src_words, u, col, base):
+            nc.tensor.transpose(tp[:, u, col : col + P], src_words[:, base + u : base + 256 : 2], ident[:])
+
+        def t_x(h, g, jp):
+            tp = tpool.tile([P, 2, 256], F32, name="tp")
+            for jj in range(2):
+                w = xw[h][:, 2 * jp + jj, :].bitcast(F32)
+                for u in range(2):
+                    words_t(tp, w, u, P * jj, 256 * g)
+            return tp
+
+        def prod_x(tp, h, g, xg, jp):
+            nc.vector.tensor_tensor(
+                out=xg[:, 256 * jp : 256 * (jp + 1), :].rearrange("p r (u e) -> p r u e", e=2),
+                in0=tp[:].rearrange("p u r -> p (u r)").bitcast(BF16).rearrange("p (u r e) -> p r u e", u=2, e=2),
+                in1=xs[:, g, :].unsqueeze(1).to_broadcast([P, 256, 4]).rearrange("p r (u e) -> p r u e", e=2),
+                op=ALU.mult,
+            )
+
+        def quant_x(h, g, xg):
+            nc.vector.quantize_mx(
+                out=xcodes[:, g, 512 * h : 512 * (h + 1)].bitcast(FP8X4),
+                scales=xscales[:, g, 512 * h : 512 * (h + 1)],
+                in_=xg[:].rearrange("p r q -> p (r q)"),
+            )
+
+        def t_p(e, h, sp):
+            tp = zpool.tile([P, 2, 256], F32, name="z")
+            for ss in range(2):
+                w = praw[e][:, 2 * sp + ss, :].bitcast(F32)
+                for u in range(2):
+                    words_t(tp, w, u, P * ss, 256 * h)
+            return tp
+
+        def out_p(tp, pg, sp):
+            nc.scalar.copy(
+                out=pg[:, 256 * sp : 256 * (sp + 1), :].rearrange("p r q -> p (r q)").bitcast(F32).rearrange("p (r u) -> p r u", u=2),
+                in_=tp[:].rearrange("p u r -> p r u"),
+            )
+
+        def quant_p(e, h, pg):
+            nc.vector.quantize_mx(
+                out=pcodes[e][:, h, :].bitcast(FP8X4),
+                scales=pscales[e][:, h, :],
+                in_=pg[:].rearrange("p r q -> p (r q)"),
+            )
+
+        wg, wq, z, gl, tph, hg, hq, av, bv, tv, uv, ev, tpe, tps = ({} for _ in range(14))
+
+        def inter_w(r):
+            i, e = divmod(r, 2)
+            c, o = divmod(i * P, WCH)
+            wg[r] = stage.tile([P, 2, P, 4], BF16, name="wg", align_bytes=64, bufs=4)
+            nc.scalar.copy(out=wg[r][:], in_=wraw[e][c][:, :, :, o : o + P].rearrange("p g t f -> p g f t"))
+
+        def quant_w(r):
+            cod = stage.tile([P, 2, P], U32, name="wcod", align_bytes=64, bufs=5)
+            sca = stage.tile([P, 2, P], U8, name="wsca", align_bytes=64, bufs=5)
+            nc.vector.quantize_mx(
+                out=cod[:].rearrange("p g f -> p (g f)").bitcast(FP8X4),
+                scales=sca[:].rearrange("p g f -> p (g f)"),
+                in_=wg.pop(r)[:].rearrange("p g f q -> p (g f q)"),
+            )
+            wq[r] = (cod, sca)
+
+        def mm1(r, h):
+            cod, sca = wq[r]
+            zt = zpool.tile([P, 512], F32, name="z")
+            for g in range(2):
+                nc.tensor.matmul_mx(
+                    out=zt[:],
+                    lhsT=cod[:, g, :].bitcast(FP8X4),
+                    lhsT_scale=sca[:, g, :],
+                    rhs=xcodes[:, g, 512 * h : 512 * (h + 1)].bitcast(FP8X4),
+                    rhs_scale=xscales[:, g, 512 * h : 512 * (h + 1)],
+                    start=(g == 0),
+                    stop=(g == 1),
+                )
+            z[r, h] = zt
+
+        def gelu(r, h):
+            i, e = divmod(r, 2)
+            gl[r, h] = stage.tile([P, 512], F32, name="gl", bufs=4)
+            nc.scalar.activation(
+                out=gl[r, h][:], in_=z.pop((r, h))[:], func=ACT.Gelu_apprx_tanh, bias=cols[:, e, i : i + 1]
+            )
+
+        def t_h(r, h):
+            tp = tpool.tile([P, 2, 256], F32, name="tp")
+            flat = tp[:].rearrange("p u r -> p (u r)")
+            src = gl.pop((r, h))
+            for j in range(4):
+                nc.tensor.transpose(flat[:, P * j : P * (j + 1)], src[:, P * j : P * (j + 1)], ident[:])
+            tph[r, h] = flat
+
+        def mult_h(r, h):
+            e = r % 2
+            if h == 0:
+                hg[r] = stage.tile([P, 2, P, 4], BF16, name="hg", align_bytes=64)
+            nc.vector.tensor_tensor(
+                out=hg[r][:, h, :, :],
+                in0=tph.pop((r, h)).rearrange("p (j f) -> p f j", j=4),
+                in1=sal[e][:, h, 0, :].unsqueeze(1).to_broadcast([P, P, 4]),
+                op=ALU.mult,
+            )
+
+        def quant_h(r):
+            cod = stage.tile([P, 2, P], U32, name="hcod", align_bytes=64, bufs=4)
+            sca = stage.tile([P, 2, P], U8, name="hsca", align_bytes=64, bufs=4)
+            nc.vector.quantize_mx(
+                out=cod[:].rearrange("p g f -> p (g f)").bitcast(FP8X4),
+                scales=sca[:].rearrange("p g f -> p (g f)"),
+                in_=hg.pop(r)[:].rearrange("p g f q -> p (g f q)"),
+            )
+            hq[r] = (cod, sca)
+
+        def mm2(r):
+            i, e = divmod(r, 2)
+            cod, sca = hq.pop(r)
+            if e == 0:
+                o = apool.tile([P, S], F32, name="a")
+                av[i] = o
+            else:
+                o = bpool.tile([P, S], F32, name="b")
+                bv[i] = o
+            for h in range(2):
+                nc.tensor.matmul_mx(
+                    out=o[:],
+                    lhsT=cod[:, h, :].bitcast(FP8X4),
+                    lhsT_scale=sca[:, h, :],
+                    rhs=pcodes[e][:, h, :].bitcast(FP8X4),
+                    rhs_scale=pscales[e][:, h, :],
+                    start=(h == 0),
+                    stop=(h == 1),
+                )
+
+        def emb_t(i):
+            tv[i] = stage.tile([P, S], F32, name="tv")
+            nc.scalar.activation(out=tv[i][:], in_=av[i][:], func=ACT.Identity, bias=1.0, scale=cols[:, 2, i : i + 1])
+
+        def emb_u(i):
+            uv[i] = stage.tile([P, S], F32, name="uv")
+            nc.vector.tensor_tensor(out=uv[i][:], in0=bv.pop(i)[:], in1=tv.pop(i)[:], op=ALU.mult)
+
+        def emb_e(i):
+            ev[i] = stage.tile([P, S], F32, name="ev")
+            nc.vector.tensor_tensor(out=ev[i][:], in0=av.pop(i)[:], in1=uv.pop(i)[:], op=ALU.add)
+
+        def t_emb(i):
+            tp = tpool.tile([P, 2, 256], F32, name="tp")
+            flat = tp[:].rearrange("p u r -> p (u r)")
+            for st in range(4):
+                nc.tensor.transpose(flat[:, P * st : P * (st + 1)], ev[i][:, P * st : P * (st + 1)], ident[:])
+            tpe[i] = flat
+            sc = bpool.tile([P, S], F32, name="b")
+            for st in range(4):
+                nc.tensor.matmul(
+                    out=sc[:, 2 * st : 2 * st + 2],
+                    lhsT=ev[i][:, P * st : P * (st + 1)],
+                    rhs=vmat[:, i, :],
+                    start=True,
+                    stop=True,
+                )
+            tps[i] = sc
+            ev.pop(i)
+
+        def out_score(i):
+            nc.vector.tensor_tensor(
+                out=score[:, :, 2 * i : 2 * i + 2],
+                in0=tps.pop(i)[:, 0:8].rearrange("p (st c) -> p st c", c=2),
+                in1=dt_[:, 2 * i : 2 * i + 2].unsqueeze(1).to_broadcast([P, 4, 2]),
+                op=ALU.add,
+            )
+
+        def out_emb(i):
+            eo = stage.tile([P, S], F32, name="eo")
+            nc.scalar.copy(out=eo[:], in_=tpe.pop(i))
+            nc.sync.dma_start(
+                out=out_0.rearrange("(st r) f -> r st f", r=P)[:, :, P * i : P * (i + 1)],
+                in_=eo[:].rearrange("p (st f) -> p st f", st=4),
+            )
+
+        with tc.manual_schedule():
+            def x_half(h, engs):
+                for j in range(4):
+                    cast_x(engs[j], h, j)
+                xg = [stage.tile([P, 512, 4], BF16, name=f"xg{g}", align_bytes=64) for g in range(2)]
+                for jp in range(2):
+                    tps_ = [t_x(h, g, jp) for g in range(2)]
+                    for g in range(2):
+                        prod_x(tps_[g], h, g, xg[g], jp)
+                return xg
+
+            def p_half(e, h):
+                pg = stage.tile([P, S, 4], BF16, name="pg", align_bytes=64, bufs=4)
+                for sp in range(2):
+                    out_p(t_p(e, h, sp), pg, sp)
+                return pg
+
+            xg = x_half(0, (nc.scalar, nc.vector, nc.scalar, nc.vector))
+            inter_w(0)
+            pgs = [p_half(0, h) for h in range(2)]
+            quant_x(0, 0, xg[0])
+            nc.vector.tensor_copy(out=rows32[:], in_=rows[:])
+            quant_x(0, 1, xg[1])
+            tpv = tpool.tile([P, 2, 256], F32, name="tp")
+            nc.tensor.transpose(tpv[:, 0, 0:P], rows32[:], ident[:])
+            quant_w(0)
+            mm1(0, 0)
+            nc.vector.memset(vmat[:], 0.0)
+            nc.vector.tensor_copy(out=cols[:].rearrange("p q i -> p (q i)"), in_=tpv[:, 0, 0:32])
+            xg = x_half(1, (nc.scalar,) * 4)
+            gelu(0, 0)
+            inter_w(1)
+            nc.vector.tensor_copy(out=vmat[0:64, :, 0], in_=cols[0:64, 3, :])
+            quant_x(1, 0, xg[0])
+            nc.vector.tensor_copy(out=vmat[64:128, :, 1], in_=cols[64:128, 3, :])
+            quant_x(1, 1, xg[1])
+            quant_w(1)
+            mm1(0, 1)
+            gelu(0, 1)
+            quant_p(0, 0, pgs[0])
+            inter_w(2)
+            quant_p(0, 1, pgs[1])
+            inter_w(3)
+            quant_w(2)
+
+            for n in range(1, NR + 6):
+                if n < NR:
+                    mm1(n, 0)
+                    mm1(n, 1)
+                if 0 <= n - 2 < NR:
+                    quant_h(n - 2)
+                if 0 <= n - 3 < NR:
+                    mm2(n - 3)
+                i, odd = divmod(n - 5, 2)
+                emb = odd == 0 and 0 <= i < NI
+                if emb:
+                    emb_u(i)
+                if 0 <= n - 1 < NR:
+                    t_h(n - 1, 0)
+                    t_h(n - 1, 1)
+                if n < NR:
+                    gelu(n, 0)
+                    gelu(n, 1)
+                if 0 <= n - 1 < NR:
+                    mult_h(n - 1, 0)
+                if emb:
+                    emb_e(i)
+                    t_emb(i)
+                if 0 <= n - 1 < NR:
+                    mult_h(n - 1, 1)
+                if n + 2 < NR:
+                    quant_w(n + 2)
+                if n % 2 == 0 and 0 <= (n - 4) // 2 < NI:
+                    emb_t((n - 4) // 2)
+                if emb:
+                    out_score(i)
+                    out_emb(i)
+                if n in (1, 2):
+                    pgs.append(p_half(1, n - 1))
+                if n in (2, 3):
+                    quant_p(1, n - 2, pgs[n])
+                if n + 3 < NR:
+                    inter_w(n + 3)
+            nc.sync.dma_start(out=out_1.rearrange("(st r) c -> r st c", r=P), in_=score[:])

@@ -19,6 +19,9 @@ P = 128
 NI = F // P
 NR = 2 * NI
 WCH = 256
+LEAD = 2
+LAG = 2
+SPARE = ("te", "sc", "a", "b")
 
 
 def tile_endpoint_span_scoring_f4_kernel(
@@ -28,339 +31,391 @@ def tile_endpoint_span_scoring_f4_kernel(
     with ExitStack() as ctx:
         keep = ctx.enter_context(tc.tile_pool(name="keep", bufs=1))
         stage = ctx.enter_context(tc.tile_pool(name="stage", bufs=3))
-        zpool = ctx.enter_context(tc.psum_pool(name="zpool", bufs=2))
-        tpool = ctx.enter_context(tc.psum_pool(name="tpool", bufs=3))
-        apool = ctx.enter_context(tc.psum_pool(name="apool", bufs=2))
-        bpool = ctx.enter_context(tc.psum_pool(name="bpool", bufs=1))
+        twin = ctx.enter_context(tc.psum_pool(name="twin", bufs=2))
+        lone = ctx.enter_context(tc.psum_pool(name="lone", bufs=1))
 
         ident = keep.tile([P, P], F32, name="ident")
         make_identity(nc, ident[:])
 
-        xb = [keep.tile([P, 4, D], U8, name=f"xb{h}", align_bytes=64) for h in range(2)]
-        xw = [keep.tile([P, 4, D], BF16, name=f"xw{h}", align_bytes=64) for h in range(2)]
+        xb = [keep.tile([P, 2, D], U8, name=f"xb{n}", align_bytes=64) for n in range(4)]
         xs = keep.tile([P, 2, 4], F32, name="xs")
-        xcodes = keep.tile([P, 2, T], U32, name="xcodes", align_bytes=64)
-        xscales = keep.tile([P, 2, T], U8, name="xscales", align_bytes=64)
-        praw = [keep.tile([P, 4, T], BF16, name=f"praw{e}", align_bytes=64) for e in range(2)]
-        pcodes = [keep.tile([P, 2, S], U32, name=f"pcodes{e}", align_bytes=64) for e in range(2)]
-        pscales = [keep.tile([P, 2, S], U8, name=f"pscales{e}", align_bytes=64) for e in range(2)]
-        wraw = [
-            [keep.tile([P, 2, 4, WCH], BF16, name=f"wraw{e}_{c}", align_bytes=64) for c in range(F // WCH)]
-            for e in range(2)
-        ]
-        sal = [keep.tile([P, 2, 4, 4], BF16, name=f"sal{e}") for e in range(2)]
+        xsc = [keep.tile([P, 512], F32, name=f"xsc{g}") for g in range(2)]
+        xcod = {(h, g): keep.tile([P, 512], U32, name=f"xcod{h}{g}", align_bytes=64) for h in range(2) for g in range(2)}
+        xsca = {(h, g): keep.tile([P, 512], U8, name=f"xsca{h}{g}", align_bytes=64) for h in range(2) for g in range(2)}
+        praw = {(e, sp): keep.tile([P, 2, T], BF16, name=f"praw{e}{sp}") for e in range(2) for sp in range(2)}
+        pcod = {(e, h): keep.tile([P, S], U32, name=f"pcod{e}{h}", align_bytes=64) for e in range(2) for h in range(2)}
+        psca = {(e, h): keep.tile([P, S], U8, name=f"psca{e}{h}", align_bytes=64) for e in range(2) for h in range(2)}
+        wraw = {
+            (e, c): keep.tile([P, 2, 4, WCH], BF16, name=f"wraw{e}{c}") for e in range(2) for c in range(F // WCH)
+        }
+        sal = [keep.tile([P, 2, 4], BF16, name=f"sal{e}") for e in range(2)]
         rows = keep.tile([P, P], BF16, name="rows")
         rows32 = keep.tile([P, P], F32, name="rows32")
         cols = keep.tile([P, 4, NI], F32, name="cols")
         vmat = keep.tile([P, NI, 2], F32, name="vmat")
-        dt_ = keep.tile([P, C], BF16, name="dt_")
+        dbias = keep.tile([P, C], BF16, name="dbias")
         score = keep.tile([P, 4, C], F32, name="score")
-        warm = keep.tile([P, 1], F32, name="warm")
 
         xv = x_bytes.rearrange("(h p j) k -> h p j k", h=2, p=P, j=4)
         wv = [w.rearrange("(g p j) f -> g p j f", g=2, p=P, j=4) for w in (ws, we)]
-        pv = [q.rearrange("(st r) t -> r st t", r=P) for q in (ps, pe)]
+        pv = [q.rearrange("(r st) t -> r st t", st=4) for q in (ps, pe)]
+
+        def load_x(n):
+            h, jp = divmod(n, 2)
+            nc.sync.dma_start(out=xb[n][:], in_=xv[h][:, 2 * jp : 2 * jp + 2, :])
 
         def load_w(e, c):
             for g in range(2):
-                nc.sync.dma_start(out=wraw[e][c][:, g, :, :], in_=wv[e][g][:, :, c * WCH : (c + 1) * WCH])
+                nc.sync.dma_start(out=wraw[e, c][:, g, :, :], in_=wv[e][g][:, :, c * WCH : (c + 1) * WCH])
 
-        nc.vector.memset(rows[:], 0.0)
-        nc.sync.dma_start(out=xb[0][:, 0:2, :], in_=xv[0][:, 0:2, :])
-        nc.sync.dma_start(out=xb[0][:, 2:4, :], in_=xv[0][:, 2:4, :])
-        nc.sync.dma_start(out=xs[:], in_=x_scale.rearrange("o (g p t) -> p (o g) t", p=P, t=4))
-        for q, vec in enumerate((bs, be, mix, v)):
-            nc.gpsimd.dma_start(out=rows[NI * q : NI * (q + 1), :], in_=vec.rearrange("(i f) -> i f", f=P))
-        for e, gv in enumerate((gs, ge)):
-            nc.gpsimd.dma_start(out=sal[e][:, :, 0, :], in_=gv.rearrange("(h m j) -> m h j", h=2, j=4))
-        nc.gpsimd.dma_start(out=dt_[:], in_=d.partition_broadcast(P))
+        def load_p(e, sp):
+            nc.sync.dma_start(out=praw[e, sp][:], in_=pv[e][:, 2 * sp : 2 * sp + 2, :])
 
-        def load_p(e):
-            for k in range(2):
-                nc.sync.dma_start(out=praw[e][:, 2 * k : 2 * k + 2, :], in_=pv[e][:, 2 * k : 2 * k + 2, :])
+        spare = []
 
-        load_p(0)
-        load_w(0, 0)
-        nc.sync.dma_start(out=xb[1][:], in_=xv[1])
-        load_w(1, 0)
-        load_p(1)
-        for c in range(1, F // WCH):
-            load_w(0, c)
-            load_w(1, c)
+        def spare_bank():
+            spare.append(SPARE[len(spare) % len(SPARE)])
+            return lone.tile([P, 512], F32, name=spare[-1])
 
-        nc.vector.memset(warm[:], 0.0)
-        nc.scalar.activation(out=warm[:], in_=warm[:], func=ACT.Gelu_apprx_tanh)
+        xw, xbank, xg, pbank, pg = {}, {}, {}, {}, {}
+        wg, wq, z, gl, tph, hg, hq, ab, tv, uv, ev, tpe, sc = ({} for n in range(13))
 
-        def cast_x(eng, h, j):
-            src = xb[h][:, j, :].bitcast(FP8)
-            if eng is nc.scalar:
-                nc.scalar.copy(out=xw[h][:, j, :], in_=src)
-            else:
-                nc.vector.tensor_copy(out=xw[h][:, j, :], in_=src)
-
-        def words_t(tp, src_words, u, col, base):
-            nc.tensor.transpose(tp[:, u, col : col + P], src_words[:, base + u : base + 256 : 2], ident[:])
-
-        def t_x(h, g, jp):
-            tp = tpool.tile([P, 2, 256], F32, name="tp")
-            for jj in range(2):
-                w = xw[h][:, 2 * jp + jj, :].bitcast(F32)
-                for u in range(2):
-                    words_t(tp, w, u, P * jj, 256 * g)
-            return tp
-
-        def prod_x(tp, h, g, xg, jp):
-            nc.vector.tensor_tensor(
-                out=xg[:, 256 * jp : 256 * (jp + 1), :].rearrange("p r (u e) -> p r u e", e=2),
-                in0=tp[:].rearrange("p u r -> p (u r)").bitcast(BF16).rearrange("p (u r e) -> p r u e", u=2, e=2),
-                in1=xs[:, g, :].unsqueeze(1).to_broadcast([P, 256, 4]).rearrange("p r (u e) -> p r u e", e=2),
-                op=ALU.mult,
-            )
-
-        def quant_x(h, g, xg):
-            nc.vector.quantize_mx(
-                out=xcodes[:, g, 512 * h : 512 * (h + 1)].bitcast(FP8X4),
-                scales=xscales[:, g, 512 * h : 512 * (h + 1)],
-                in_=xg[:].rearrange("p r q -> p (r q)"),
-            )
-
-        def t_p(e, h, sp):
-            tp = zpool.tile([P, 2, 256], F32, name="z")
-            for ss in range(2):
-                w = praw[e][:, 2 * sp + ss, :].bitcast(F32)
-                for u in range(2):
-                    words_t(tp, w, u, P * ss, 256 * h)
-            return tp
-
-        def out_p(tp, pg, sp):
+        def spread_scale(g):
+            bank = spare_bank()
+            for t in range(4):
+                nc.tensor.transpose(bank[:, P * t : P * (t + 1)], xs[:, g, t : t + 1].to_broadcast([P, P]), ident[:])
             nc.scalar.copy(
-                out=pg[:, 256 * sp : 256 * (sp + 1), :].rearrange("p r q -> p (r q)").bitcast(F32).rearrange("p (r u) -> p r u", u=2),
-                in_=tp[:].rearrange("p u r -> p r u"),
+                out=xsc[g][:].rearrange("p (n t) -> p n t", t=4), in_=bank[:].rearrange("p (t n) -> p n t", t=4)
             )
 
-        def quant_p(e, h, pg):
-            nc.vector.quantize_mx(
-                out=pcodes[e][:, h, :].bitcast(FP8X4),
-                scales=pscales[e][:, h, :],
-                in_=pg[:].rearrange("p r q -> p (r q)"),
+        def prod_x(n, g):
+            xw[n, g] = stage.tile([P, 512], BF16, name="xw", bufs=6)
+            src = xb[n // 2][:, n % 2, 512 * g : 512 * (g + 1)].bitcast(FP8)
+            nc.vector.tensor_tensor(out=xw[n, g][:], in0=src, in1=xsc[g][:], op=ALU.mult)
+
+        def turn_words(bank, half, words):
+            for u in range(2):
+                o = 256 * u + P * half
+                nc.tensor.transpose(bank[:, o : o + P], words[:, u:256:2], ident[:])
+
+        def copy_words(bank, name):
+            dst = stage.tile([P, 256, 4], BF16, name=name, align_bytes=64, bufs=8)
+            nc.scalar.copy(
+                out=dst[:].rearrange("p r q -> p (r q)").bitcast(F32).rearrange("p (r u) -> p r u", u=2),
+                in_=bank[:].rearrange("p (u r) -> p r u", u=2),
             )
+            return dst
 
-        wg, wq, z, gl, tph, hg, hq, av, bv, tv, uv, ev, tpe, tps = ({} for _ in range(14))
+        def quant(cod, sca, src):
+            nc.vector.quantize_mx(out=cod.bitcast(FP8X4), scales=sca, in_=src)
 
-        def inter_w(r):
+        def turn_x(n, g, name):
+            if n % 2 == 0:
+                xbank[n // 2, g] = twin.tile([P, 512], F32, name=name) if name else spare_bank()
+            turn_words(xbank[n // 2, g], n % 2, xw.pop((n, g))[:].bitcast(F32))
+
+        def copy_x(m, g):
+            xg[m, g] = copy_words(xbank.pop((m, g)), "xg")
+
+        def quant_x(m, g):
+            h, jp = divmod(m, 2)
+            span = slice(256 * jp, 256 * (jp + 1))
+            quant(xcod[h, g][:, span], xsca[h, g][:, span], xg.pop((m, g))[:].rearrange("p r q -> p (r q)"))
+
+        def turn_p(e, sp, h):
+            pbank[e, sp, h] = spare_bank()
+            for ss in range(2):
+                turn_words(pbank[e, sp, h], ss, praw[e, sp][:, ss, 512 * h : 512 * (h + 1)].bitcast(F32))
+
+        def copy_p(e, sp, h):
+            pg[e, sp, h] = copy_words(pbank.pop((e, sp, h)), "pg")
+
+        def quant_p(e, sp, h):
+            span = slice(256 * sp, 256 * (sp + 1))
+            quant(pcod[e, h][:, span], psca[e, h][:, span], pg.pop((e, sp, h))[:].rearrange("p r q -> p (r q)"))
+
+        def weave_w(r, on_vector):
             i, e = divmod(r, 2)
             c, o = divmod(i * P, WCH)
             wg[r] = stage.tile([P, 2, P, 4], BF16, name="wg", align_bytes=64, bufs=4)
-            nc.scalar.copy(out=wg[r][:], in_=wraw[e][c][:, :, :, o : o + P].rearrange("p g t f -> p g f t"))
+            src = wraw[e, c][:, :, :, o : o + P].rearrange("p g t f -> p g f t")
+            if on_vector:
+                nc.vector.tensor_copy(out=wg[r][:], in_=src)
+            else:
+                nc.scalar.copy(out=wg[r][:], in_=src)
 
         def quant_w(r):
-            cod = stage.tile([P, 2, P], U32, name="wcod", align_bytes=64, bufs=5)
-            sca = stage.tile([P, 2, P], U8, name="wsca", align_bytes=64, bufs=5)
-            nc.vector.quantize_mx(
-                out=cod[:].rearrange("p g f -> p (g f)").bitcast(FP8X4),
-                scales=sca[:].rearrange("p g f -> p (g f)"),
-                in_=wg.pop(r)[:].rearrange("p g f q -> p (g f q)"),
-            )
+            cod = stage.tile([P, 2 * P], U32, name="wcod", align_bytes=64, bufs=LEAD + 4)
+            sca = stage.tile([P, 2 * P], U8, name="wsca", align_bytes=64, bufs=LEAD + 4)
+            quant(cod[:], sca[:], wg.pop(r)[:].rearrange("p g f q -> p (g f q)"))
             wq[r] = (cod, sca)
 
-        def mm1(r, h):
+        def project(r, h):
             cod, sca = wq[r]
-            zt = zpool.tile([P, 512], F32, name="z")
+            z[r, h] = twin.tile([P, 512], F32, name="z")
             for g in range(2):
                 nc.tensor.matmul_mx(
-                    out=zt[:],
-                    lhsT=cod[:, g, :].bitcast(FP8X4),
-                    lhsT_scale=sca[:, g, :],
-                    rhs=xcodes[:, g, 512 * h : 512 * (h + 1)].bitcast(FP8X4),
-                    rhs_scale=xscales[:, g, 512 * h : 512 * (h + 1)],
+                    out=z[r, h][:],
+                    lhsT=cod[:, P * g : P * (g + 1)].bitcast(FP8X4),
+                    lhsT_scale=sca[:, P * g : P * (g + 1)],
+                    rhs=xcod[h, g][:].bitcast(FP8X4),
+                    rhs_scale=xsca[h, g][:],
                     start=(g == 0),
                     stop=(g == 1),
                 )
-            z[r, h] = zt
 
         def gelu(r, h):
             i, e = divmod(r, 2)
-            gl[r, h] = stage.tile([P, 512], F32, name="gl", bufs=4)
+            gl[r, h] = stage.tile([P, 512], F32, name="gl", bufs=6)
             nc.scalar.activation(
                 out=gl[r, h][:], in_=z.pop((r, h))[:], func=ACT.Gelu_apprx_tanh, bias=cols[:, e, i : i + 1]
             )
 
-        def t_h(r, h):
-            tp = tpool.tile([P, 2, 256], F32, name="tp")
-            flat = tp[:].rearrange("p u r -> p (u r)")
+        def turn_h(r, h):
+            tph[r, h] = twin.tile([P, 512], F32, name="tp")
             src = gl.pop((r, h))
             for j in range(4):
-                nc.tensor.transpose(flat[:, P * j : P * (j + 1)], src[:, P * j : P * (j + 1)], ident[:])
-            tph[r, h] = flat
+                nc.tensor.transpose(tph[r, h][:, P * j : P * (j + 1)], src[:, P * j : P * (j + 1)], ident[:])
 
-        def mult_h(r, h):
-            e = r % 2
-            if h == 0:
-                hg[r] = stage.tile([P, 2, P, 4], BF16, name="hg", align_bytes=64)
+        def weigh_h(r, h):
+            hg[r, h] = stage.tile([P, P, 4], BF16, name="hg", align_bytes=64, bufs=4)
             nc.vector.tensor_tensor(
-                out=hg[r][:, h, :, :],
-                in0=tph.pop((r, h)).rearrange("p (j f) -> p f j", j=4),
-                in1=sal[e][:, h, 0, :].unsqueeze(1).to_broadcast([P, P, 4]),
+                out=hg[r, h][:],
+                in0=tph.pop((r, h))[:].rearrange("p (j f) -> p f j", j=4),
+                in1=sal[r % 2][:, h, :].unsqueeze(1).to_broadcast([P, P, 4]),
                 op=ALU.mult,
             )
 
-        def quant_h(r):
-            cod = stage.tile([P, 2, P], U32, name="hcod", align_bytes=64, bufs=4)
-            sca = stage.tile([P, 2, P], U8, name="hsca", align_bytes=64, bufs=4)
-            nc.vector.quantize_mx(
-                out=cod[:].rearrange("p g f -> p (g f)").bitcast(FP8X4),
-                scales=sca[:].rearrange("p g f -> p (g f)"),
-                in_=hg.pop(r)[:].rearrange("p g f q -> p (g f q)"),
-            )
-            hq[r] = (cod, sca)
+        def quant_h(r, h):
+            cod = stage.tile([P, P], U32, name="hcod", align_bytes=64, bufs=LEAD + 8)
+            sca = stage.tile([P, P], U8, name="hsca", align_bytes=64, bufs=LEAD + 8)
+            quant(cod[:], sca[:], hg.pop((r, h))[:].rearrange("p f q -> p (f q)"))
+            hq[r, h] = (cod, sca)
 
-        def mm2(r):
-            i, e = divmod(r, 2)
-            cod, sca = hq.pop(r)
-            if e == 0:
-                o = apool.tile([P, S], F32, name="a")
-                av[i] = o
-            else:
-                o = bpool.tile([P, S], F32, name="b")
-                bv[i] = o
+        def gather(r, name=None):
+            e = r % 2
+            ab[r] = twin.tile([P, S], F32, name=name) if name else lone.tile([P, S], F32, name="ab"[e])
             for h in range(2):
+                cod, sca = hq.pop((r, h))
                 nc.tensor.matmul_mx(
-                    out=o[:],
-                    lhsT=cod[:, h, :].bitcast(FP8X4),
-                    lhsT_scale=sca[:, h, :],
-                    rhs=pcodes[e][:, h, :].bitcast(FP8X4),
-                    rhs_scale=pscales[e][:, h, :],
+                    out=ab[r][:],
+                    lhsT=cod[:].bitcast(FP8X4),
+                    lhsT_scale=sca[:],
+                    rhs=pcod[e, h][:].bitcast(FP8X4),
+                    rhs_scale=psca[e, h][:],
                     start=(h == 0),
                     stop=(h == 1),
                 )
 
-        def emb_t(i):
-            tv[i] = stage.tile([P, S], F32, name="tv")
-            nc.scalar.activation(out=tv[i][:], in_=av[i][:], func=ACT.Identity, bias=1.0, scale=cols[:, 2, i : i + 1])
-
-        def emb_u(i):
-            uv[i] = stage.tile([P, S], F32, name="uv")
-            nc.vector.tensor_tensor(out=uv[i][:], in0=bv.pop(i)[:], in1=tv.pop(i)[:], op=ALU.mult)
-
-        def emb_e(i):
-            ev[i] = stage.tile([P, S], F32, name="ev")
-            nc.vector.tensor_tensor(out=ev[i][:], in0=av.pop(i)[:], in1=uv.pop(i)[:], op=ALU.add)
-
-        def t_emb(i):
-            tp = tpool.tile([P, 2, 256], F32, name="tp")
-            flat = tp[:].rearrange("p u r -> p (u r)")
-            for st in range(4):
-                nc.tensor.transpose(flat[:, P * st : P * (st + 1)], ev[i][:, P * st : P * (st + 1)], ident[:])
-            tpe[i] = flat
-            sc = bpool.tile([P, S], F32, name="b")
-            for st in range(4):
-                nc.tensor.matmul(
-                    out=sc[:, 2 * st : 2 * st + 2],
-                    lhsT=ev[i][:, P * st : P * (st + 1)],
-                    rhs=vmat[:, i, :],
-                    start=True,
-                    stop=True,
-                )
-            tps[i] = sc
-            ev.pop(i)
-
-        def out_score(i):
-            nc.vector.tensor_tensor(
-                out=score[:, :, 2 * i : 2 * i + 2],
-                in0=tps.pop(i)[:, 0:8].rearrange("p (st c) -> p st c", c=2),
-                in1=dt_[:, 2 * i : 2 * i + 2].unsqueeze(1).to_broadcast([P, 4, 2]),
-                op=ALU.add,
+        def emb_factor(i):
+            tv[i] = stage.tile([P, S], F32, name="tv", bufs=2)
+            nc.scalar.activation(
+                out=tv[i][:], in_=ab[2 * i][:], func=ACT.Identity, bias=1.0, scale=cols[:, 2, i : i + 1]
             )
 
-        def out_emb(i):
-            eo = stage.tile([P, S], F32, name="eo")
-            nc.scalar.copy(out=eo[:], in_=tpe.pop(i))
+        def emb_product(i):
+            uv[i] = stage.tile([P, S], F32, name="uv", bufs=2)
+            nc.vector.tensor_tensor(out=uv[i][:], in0=ab.pop(2 * i + 1)[:], in1=tv.pop(i)[:], op=ALU.mult)
+
+        def emb_sum(i):
+            ev[i] = stage.tile([P, S], F32, name="ev", bufs=3)
+            nc.vector.tensor_tensor(out=ev[i][:], in0=ab.pop(2 * i)[:], in1=uv.pop(i)[:], op=ALU.add)
+
+        def turn_emb(i):
+            tpe[i] = lone.tile([P, S], F32, name="te")
+            for st in range(4):
+                nc.tensor.transpose(tpe[i][:, P * st : P * (st + 1)], ev[i][:, P * st : P * (st + 1)], ident[:])
+
+        def label_sums(i):
+            if i == 0:
+                sc[0] = lone.tile([P, 512], F32, name="sc")
+            src = ev.pop(i)
+            for st in range(4):
+                o = C * st + 2 * i
+                nc.tensor.matmul(
+                    out=sc[0][:, o : o + 2], lhsT=src[:, P * st : P * (st + 1)], rhs=vmat[:, i, :], start=True, stop=True
+                )
+
+        def store_emb(i):
+            eo = stage.tile([P, S], F32, name="eo", bufs=2)
+            nc.scalar.copy(out=eo[:], in_=tpe.pop(i)[:])
             nc.sync.dma_start(
-                out=out_0.rearrange("(st r) f -> r st f", r=P)[:, :, P * i : P * (i + 1)],
+                out=out_0.rearrange("(r st) f -> r st f", st=4)[:, :, P * i : P * (i + 1)],
                 in_=eo[:].rearrange("p (st f) -> p st f", st=4),
             )
 
+        def live(r):
+            return 0 <= r < NR
+
         with tc.manual_schedule():
-            def x_half(h, engs):
-                for j in range(4):
-                    cast_x(engs[j], h, j)
-                xg = [stage.tile([P, 512, 4], BF16, name=f"xg{g}", align_bytes=64) for g in range(2)]
-                for jp in range(2):
-                    tps_ = [t_x(h, g, jp) for g in range(2)]
-                    for g in range(2):
-                        prod_x(tps_[g], h, g, xg[g], jp)
-                return xg
-
-            def p_half(e, h):
-                pg = stage.tile([P, S, 4], BF16, name="pg", align_bytes=64, bufs=4)
-                for sp in range(2):
-                    out_p(t_p(e, h, sp), pg, sp)
-                return pg
-
-            xg = x_half(0, (nc.scalar, nc.vector, nc.scalar, nc.vector))
-            inter_w(0)
-            pgs = [p_half(0, h) for h in range(2)]
-            quant_x(0, 0, xg[0])
-            nc.vector.tensor_copy(out=rows32[:], in_=rows[:])
-            quant_x(0, 1, xg[1])
-            tpv = tpool.tile([P, 2, 256], F32, name="tp")
-            nc.tensor.transpose(tpv[:, 0, 0:P], rows32[:], ident[:])
-            quant_w(0)
-            mm1(0, 0)
+            nc.vector.memset(rows[:], 0.0)
             nc.vector.memset(vmat[:], 0.0)
-            nc.vector.tensor_copy(out=cols[:].rearrange("p q i -> p (q i)"), in_=tpv[:, 0, 0:32])
-            xg = x_half(1, (nc.scalar,) * 4)
-            gelu(0, 0)
-            inter_w(1)
-            nc.vector.tensor_copy(out=vmat[0:64, :, 0], in_=cols[0:64, 3, :])
-            quant_x(1, 0, xg[0])
-            nc.vector.tensor_copy(out=vmat[64:128, :, 1], in_=cols[64:128, 3, :])
-            quant_x(1, 1, xg[1])
-            quant_w(1)
-            mm1(0, 1)
-            gelu(0, 1)
-            quant_p(0, 0, pgs[0])
-            inter_w(2)
-            quant_p(0, 1, pgs[1])
-            inter_w(3)
-            quant_w(2)
+            nc.sync.dma_start(out=xs[:], in_=x_scale.rearrange("o (g p t) -> p (o g) t", p=P, t=4))
+            load_x(0)
+            for q, vec in enumerate((bs, be, mix, v)):
+                nc.scalar.dma_start(out=rows[NI * q : NI * (q + 1), :], in_=vec.rearrange("(i f) -> i f", f=P))
+            load_x(1)
+            load_w(0, 0)
+            load_w(1, 0)
+            load_p(0, 0)
+            load_x(2)
+            load_p(0, 1)
+            load_x(3)
+            load_p(1, 0)
+            load_p(1, 1)
+            for c in range(1, F // WCH):
+                load_w(0, c)
+                load_w(1, c)
+            for e, gv in enumerate((gs, ge)):
+                nc.gpsimd.dma_start(out=sal[e][:], in_=gv.rearrange("(h m j) -> m h j", h=2, j=4))
+            nc.gpsimd.dma_start(out=dbias[:], in_=d.partition_broadcast(P))
 
-            for n in range(1, NR + 6):
-                if n < NR:
-                    mm1(n, 0)
-                    mm1(n, 1)
-                if 0 <= n - 2 < NR:
-                    quant_h(n - 2)
-                if 0 <= n - 3 < NR:
-                    mm2(n - 3)
-                i, odd = divmod(n - 5, 2)
-                emb = odd == 0 and 0 <= i < NI
-                if emb:
-                    emb_u(i)
-                if 0 <= n - 1 < NR:
-                    t_h(n - 1, 0)
-                    t_h(n - 1, 1)
-                if n < NR:
-                    gelu(n, 0)
+            def x_turns(m, name):
+                for g in range(2):
+                    for n in (2 * m, 2 * m + 1):
+                        if (n, g) not in xw:
+                            prod_x(n, g)
+                        turn_x(n, g, name)
+
+            def x_copies(m):
+                for g in range(2):
+                    copy_x(m, g)
+
+            def p_turns(e, sp):
+                for h in range(2):
+                    turn_p(e, sp, h)
+
+            def p_copies(e, sp):
+                for h in range(2):
+                    copy_p(e, sp, h)
+
+            spread_scale(0)
+            spread_scale(1)
+            nc.scalar.copy(out=rows32[:], in_=rows[:])
+            x_turns(0, "tp")
+            small = spare_bank()
+            nc.tensor.transpose(small[:, 0:P], rows32[:], ident[:])
+            weave_w(0, False)
+            x_copies(0)
+            nc.scalar.copy(out=cols[:].rearrange("p q i -> p (q i)"), in_=small[:, 0 : 4 * NI])
+            x_turns(1, "z")
+            weave_w(1, False)
+            x_copies(1)
+            p_turns(0, 0)
+            quant_x(0, 0)
+            quant_x(0, 1)
+            quant_w(0)
+            prod_x(4, 0)
+            quant_x(1, 0)
+            prod_x(5, 0)
+            quant_x(1, 1)
+            quant_w(1)
+            p_copies(0, 0)
+            project(0, 0)
+            gelu(0, 0)
+            project(1, 0)
+            gelu(1, 0)
+            x_turns(2, "tp")
+            x_copies(2)
+            p_turns(0, 1)
+            x_turns(3, None)
+            x_copies(3)
+            turn_h(0, 0)
+            weave_w(2, True)
+            quant_x(2, 0)
+            quant_x(2, 1)
+            quant_w(2)
+            quant_x(3, 0)
+            quant_x(3, 1)
+            weave_w(3, True)
+            weigh_h(0, 0)
+            p_copies(0, 1)
+            quant_p(0, 0, 0)
+            quant_w(3)
+            quant_h(0, 0)
+            quant_p(0, 0, 1)
+
+            for n in range(NR - 1):
+                late, early = n - 1, n - 1 + LEAD
+                i, odd = divmod(n - LAG, 2)
+                if live(n + LEAD):
+                    project(n + LEAD, 0)
+                    gelu(n + LEAD, 0)
+                if live(n):
+                    project(n, 1)
                     gelu(n, 1)
-                if 0 <= n - 1 < NR:
-                    mult_h(n - 1, 0)
-                if emb:
-                    emb_e(i)
-                    t_emb(i)
-                if 0 <= n - 1 < NR:
-                    mult_h(n - 1, 1)
-                if n + 2 < NR:
-                    quant_w(n + 2)
-                if n % 2 == 0 and 0 <= (n - 4) // 2 < NI:
-                    emb_t((n - 4) // 2)
-                if emb:
-                    out_score(i)
-                    out_emb(i)
-                if n in (1, 2):
-                    pgs.append(p_half(1, n - 1))
-                if n in (2, 3):
-                    quant_p(1, n - 2, pgs[n])
-                if n + 3 < NR:
-                    inter_w(n + 3)
-            nc.sync.dma_start(out=out_1.rearrange("(st r) c -> r st c", r=P), in_=score[:])
+                if live(n - LAG):
+                    gather(n - LAG)
+                if live(late):
+                    turn_h(late, 1)
+                if live(early):
+                    turn_h(early, 0)
+                if n < 2:
+                    p_turns(1, n)
+                    p_copies(1, n)
+                if not odd and 1 <= i <= NI:
+                    turn_emb(i - 1)
+                if odd and 1 <= i <= NI:
+                    label_sums(i - 1)
+                if live(n - LAG):
+                    if odd:
+                        emb_product(i)
+                    else:
+                        emb_factor(i)
+                if live(late):
+                    weigh_h(late, 1)
+                if odd and live(n - LAG):
+                    emb_sum(i)
+                elif live(early):
+                    weigh_h(early, 0)
+                if live(late):
+                    quant_h(late, 1)
+                if n < 3:
+                    quant_p(*divmod(n + 1, 2), 0)
+                    quant_p(*divmod(n + 1, 2), 1)
+                if n == 2:
+                    nc.scalar.copy(out=vmat[0:64, :, 0], in_=cols[0:64, 3, :])
+                    nc.scalar.copy(out=vmat[64:128, :, 1], in_=cols[64:128, 3, :])
+                if odd and live(n - LAG) and live(early):
+                    weigh_h(early, 0)
+                if odd and 1 <= i <= NI:
+                    store_emb(i - 1)
+                if live(n + LEAD + 2):
+                    weave_w(n + LEAD + 2, n % 2 == 0)
+                if live(early):
+                    quant_h(early, 0)
+                if live(n + LEAD + 2):
+                    quant_w(n + LEAD + 2)
+
+            last = NR - 1
+            project(last, 1)
+            gelu(last, 1)
+            gather(last - 2)
+            turn_h(last - 1, 1)
+            turn_h(last, 1)
+            label_sums(NI - 3)
+            weigh_h(last - 1, 1)
+            weigh_h(last, 1)
+            quant_h(last - 1, 1)
+            store_emb(NI - 3)
+            emb_product(NI - 2)
+            quant_h(last, 1)
+            gather(last - 1, "z")
+            gather(last, "z")
+            emb_factor(NI - 1)
+            emb_sum(NI - 2)
+            turn_emb(NI - 2)
+            label_sums(NI - 2)
+            store_emb(NI - 2)
+            emb_product(NI - 1)
+            emb_sum(NI - 1)
+            turn_emb(NI - 1)
+            label_sums(NI - 1)
+            store_emb(NI - 1)
+            nc.vector.tensor_tensor(
+                out=score[:],
+                in0=sc[0][:, 0 : 4 * C].rearrange("p (st c) -> p st c", c=C),
+                in1=dbias[:].unsqueeze(1).to_broadcast([P, 4, C]),
+                op=ALU.add,
+            )
+            nc.sync.dma_start(out=out_1.rearrange("(r st) c -> r st c", st=4), in_=score[:])

@@ -52,7 +52,7 @@ def tile_endpoint_span_scoring_f4_kernel(
         rows = keep.tile([P, P], BF16, name="rows")
         rows32 = keep.tile([P, P], F32, name="rows32")
         cols = keep.tile([P, 4, NI], F32, name="cols")
-        vmat = keep.tile([P, NI, 2], F32, name="vmat")
+        dcol = keep.tile([P, NI], F32, name="dcol")
         dbias = keep.tile([P, C], BF16, name="dbias")
         score = keep.tile([P, 4, C], F32, name="score")
 
@@ -71,14 +71,17 @@ def tile_endpoint_span_scoring_f4_kernel(
         def load_p(e, sp):
             nc.sync.dma_start(out=praw[e, sp][:], in_=pv[e][:, 2 * sp : 2 * sp + 2, :])
 
+        def bank_of(name):
+            return (twin if name in ("z", "tp") else lone).tile([P, 512], F32, name=name)
+
         spare = []
 
         def spare_bank():
             spare.append(SPARE[len(spare) % len(SPARE)])
-            return lone.tile([P, 512], F32, name=spare[-1])
+            return bank_of(spare[-1])
 
         xw, xbank, xg, pbank, pg = {}, {}, {}, {}, {}
-        wg, wq, z, gl, tph, hg, hq, ab, tv, uv, ev, tpe, sc = ({} for n in range(13))
+        wg, wq, z, gl, tph, hg, hq, ab, tv, uv, ev, tpe, sc, vv = ({} for n in range(14))
 
         def spread_scale(g):
             bank = spare_bank()
@@ -111,7 +114,7 @@ def tile_endpoint_span_scoring_f4_kernel(
 
         def turn_x(n, g, name):
             if n % 2 == 0:
-                xbank[n // 2, g] = twin.tile([P, 512], F32, name=name) if name else spare_bank()
+                xbank[n // 2, g] = bank_of(name) if name else spare_bank()
             turn_words(xbank[n // 2, g], n % 2, xw.pop((n, g))[:].bitcast(F32))
 
         def copy_x(m, g):
@@ -134,15 +137,20 @@ def tile_endpoint_span_scoring_f4_kernel(
             span = slice(256 * sp, 256 * (sp + 1))
             quant(pcod[e, h][:, span], psca[e, h][:, span], pg.pop((e, sp, h))[:].rearrange("p r q -> p (r q)"))
 
-        def weave_w(r, on_vector):
+        def weave_w(r, engine):
             i, e = divmod(r, 2)
             c, o = divmod(i * P, WCH)
-            wg[r] = stage.tile([P, 2, P, 4], BF16, name="wg", align_bytes=64, bufs=4)
-            src = wraw[e, c][:, :, :, o : o + P].rearrange("p g t f -> p g f t")
-            if on_vector:
-                nc.vector.tensor_copy(out=wg[r][:], in_=src)
+            if r % 2 == 0 and r >= LEAD + 2:
+                wg[r] = stage.tile([P, 2, P, 4], BF16, name="wgp", align_bytes=64, bufs=1)
             else:
+                wg[r] = stage.tile([P, 2, P, 4], BF16, name="wg", align_bytes=64, bufs=3)
+            src = wraw[e, c][:, :, :, o : o + P].rearrange("p g t f -> p g f t")
+            if engine is nc.vector:
+                nc.vector.tensor_copy(out=wg[r][:], in_=src)
+            elif engine is nc.scalar:
                 nc.scalar.copy(out=wg[r][:], in_=src)
+            else:
+                nc.gpsimd.tensor_scalar(out=wg[r][:], in0=src, scalar1=1.0, scalar2=0.0, op0=ALU.mult, op1=ALU.add)
 
         def quant_w(r):
             cod = stage.tile([P, 2 * P], U32, name="wcod", align_bytes=64, bufs=LEAD + 4)
@@ -171,8 +179,8 @@ def tile_endpoint_span_scoring_f4_kernel(
                 out=gl[r, h][:], in_=z.pop((r, h))[:], func=ACT.Gelu_apprx_tanh, bias=cols[:, e, i : i + 1]
             )
 
-        def turn_h(r, h):
-            tph[r, h] = twin.tile([P, 512], F32, name="tp")
+        def turn_h(r, h, name="tp"):
+            tph[r, h] = bank_of(name)
             src = gl.pop((r, h))
             for j in range(4):
                 nc.tensor.transpose(tph[r, h][:, P * j : P * (j + 1)], src[:, P * j : P * (j + 1)], ident[:])
@@ -194,7 +202,7 @@ def tile_endpoint_span_scoring_f4_kernel(
 
         def gather(r, name=None):
             e = r % 2
-            ab[r] = twin.tile([P, S], F32, name=name) if name else lone.tile([P, S], F32, name="ab"[e])
+            ab[r] = bank_of(name or "ab"[e])
             for h in range(2):
                 cod, sca = hq.pop((r, h))
                 nc.tensor.matmul_mx(
@@ -221,20 +229,28 @@ def tile_endpoint_span_scoring_f4_kernel(
             ev[i] = stage.tile([P, S], F32, name="ev", bufs=3)
             nc.vector.tensor_tensor(out=ev[i][:], in0=ab.pop(2 * i)[:], in1=uv.pop(i)[:], op=ALU.add)
 
-        def turn_emb(i):
-            tpe[i] = lone.tile([P, S], F32, name="te")
+        def turn_emb(i, name="te"):
+            tpe[i] = bank_of(name)
             for st in range(4):
                 nc.tensor.transpose(tpe[i][:, P * st : P * (st + 1)], ev[i][:, P * st : P * (st + 1)], ident[:])
 
-        def label_sums(i):
-            if i == 0:
-                sc[0] = lone.tile([P, 512], F32, name="sc")
-            src = ev.pop(i)
+        def weigh_emb(i):
+            vv[i] = stage.tile([P, S], F32, name="vv", bufs=2)
+            nc.scalar.activation(out=vv[i][:], in_=ev.pop(i)[:], func=ACT.Identity, scale=cols[:, 3, i : i + 1], bias=dcol[:, i : i + 1])
+
+        def turn_weighted(i, name="sc"):
+            sc[i] = bank_of(name)
+            src = vv.pop(i)
             for st in range(4):
-                o = C * st + 2 * i
-                nc.tensor.matmul(
-                    out=sc[0][:, o : o + 2], lhsT=src[:, P * st : P * (st + 1)], rhs=vmat[:, i, :], start=True, stop=True
-                )
+                nc.tensor.transpose(sc[i][:, P * st : P * (st + 1)], src[:, P * st : P * (st + 1)], ident[:])
+
+        def label_sums(i):
+            nc.vector.tensor_reduce(
+                out=score[:, :, 2 * i : 2 * i + 2],
+                in_=sc.pop(i)[:].rearrange("p (st c f) -> p st c f", st=4, c=2),
+                op=ALU.add,
+                axis=mybir.AxisListType.X,
+            )
 
         def store_emb(i):
             eo = stage.tile([P, S], F32, name="eo", bufs=2)
@@ -249,7 +265,6 @@ def tile_endpoint_span_scoring_f4_kernel(
 
         with tc.manual_schedule():
             nc.vector.memset(rows[:], 0.0)
-            nc.vector.memset(vmat[:], 0.0)
             nc.sync.dma_start(out=xs[:], in_=x_scale.rearrange("o (g p t) -> p (o g) t", p=P, t=4))
             load_x(0)
             for q, vec in enumerate((bs, be, mix, v)):
@@ -295,11 +310,11 @@ def tile_endpoint_span_scoring_f4_kernel(
             x_turns(0, "tp")
             small = spare_bank()
             nc.tensor.transpose(small[:, 0:P], rows32[:], ident[:])
-            weave_w(0, False)
+            weave_w(0, nc.scalar)
             x_copies(0)
             nc.scalar.copy(out=cols[:].rearrange("p q i -> p (q i)"), in_=small[:, 0 : 4 * NI])
             x_turns(1, "z")
-            weave_w(1, False)
+            weave_w(1, nc.scalar)
             x_copies(1)
             p_turns(0, 0)
             quant_x(0, 0)
@@ -321,13 +336,13 @@ def tile_endpoint_span_scoring_f4_kernel(
             x_turns(3, None)
             x_copies(3)
             turn_h(0, 0)
-            weave_w(2, True)
+            weave_w(2, nc.vector)
             quant_x(2, 0)
             quant_x(2, 1)
             quant_w(2)
             quant_x(3, 0)
             quant_x(3, 1)
-            weave_w(3, True)
+            weave_w(3, nc.vector)
             weigh_h(0, 0)
             p_copies(0, 1)
             quant_p(0, 0, 0)
@@ -335,7 +350,7 @@ def tile_endpoint_span_scoring_f4_kernel(
             quant_h(0, 0)
             quant_p(0, 0, 1)
 
-            for n in range(NR - 1):
+            for n in range(NR - 2):
                 late, early = n - 1, n - 1 + LEAD
                 i, odd = divmod(n - LAG, 2)
                 if live(n + LEAD):
@@ -353,10 +368,11 @@ def tile_endpoint_span_scoring_f4_kernel(
                 if n < 2:
                     p_turns(1, n)
                     p_copies(1, n)
-                if not odd and 1 <= i <= NI:
+                if not odd and i >= 1:
                     turn_emb(i - 1)
-                if odd and 1 <= i <= NI:
-                    label_sums(i - 1)
+                    weigh_emb(i - 1)
+                if odd and i >= 1:
+                    turn_weighted(i - 1)
                 if live(n - LAG):
                     if odd:
                         emb_product(i)
@@ -370,52 +386,71 @@ def tile_endpoint_span_scoring_f4_kernel(
                     weigh_h(early, 0)
                 if live(late):
                     quant_h(late, 1)
+                if not odd and i >= 2:
+                    label_sums(i - 2)
                 if n < 3:
                     quant_p(*divmod(n + 1, 2), 0)
                     quant_p(*divmod(n + 1, 2), 1)
-                if n == 2:
-                    nc.scalar.copy(out=vmat[0:64, :, 0], in_=cols[0:64, 3, :])
-                    nc.scalar.copy(out=vmat[64:128, :, 1], in_=cols[64:128, 3, :])
                 if odd and live(n - LAG) and live(early):
                     weigh_h(early, 0)
                 if odd and 1 <= i <= NI:
                     store_emb(i - 1)
-                if live(n + LEAD + 2):
-                    weave_w(n + LEAD + 2, n % 2 == 0)
+                if live(n + LEAD + 2) and (n % 2 or n == 0):
+                    weave_w(n + LEAD + 2, nc.scalar if n >= 2 else nc.vector)
+                if n == 2:
+                    halves = dbias[:].rearrange("p (i c) -> p c i", c=2)
+                    for c in range(2):
+                        part = slice(64 * c, 64 * (c + 1))
+                        nc.scalar.activation(out=dcol[part, :], in_=halves[part, c, :], func=ACT.Copy, scale=1.0 / 64)
+                if odd and live(n + LEAD + 2):
+                    quant_w(n + LEAD + 2)
                 if live(early):
                     quant_h(early, 0)
-                if live(n + LEAD + 2):
+                if not odd and live(n + LEAD + 2):
                     quant_w(n + LEAD + 2)
+                if not odd and live(n + LEAD + 4):
+                    weave_w(n + LEAD + 4, nc.gpsimd)
 
             last = NR - 1
-            project(last, 1)
-            gelu(last, 1)
+            for r in (last - 1, last):
+                project(r, 1)
+                gelu(r, 1)
+            gather(last - 3)
+            turn_h(last - 2, 1)
+            turn_h(last, 0)
+            label_sums(NI - 4)
+            emb_factor(NI - 2)
+            weigh_h(last - 2, 1)
+            weigh_h(last, 0)
+            quant_h(last - 2, 1)
+            turn_emb(NI - 3)
+            weigh_emb(NI - 3)
+            turn_h(last - 1, 1, "z")
+            turn_h(last, 1, "z")
+            turn_weighted(NI - 3)
             gather(last - 2)
-            turn_h(last - 1, 1)
-            turn_h(last, 1)
-            label_sums(NI - 3)
             weigh_h(last - 1, 1)
+            quant_h(last, 0)
             weigh_h(last, 1)
             quant_h(last - 1, 1)
             store_emb(NI - 3)
             emb_product(NI - 2)
             quant_h(last, 1)
-            gather(last - 1, "z")
-            gather(last, "z")
+            gather(last - 1, "tp")
+            gather(last, "tp")
             emb_factor(NI - 1)
             emb_sum(NI - 2)
             turn_emb(NI - 2)
-            label_sums(NI - 2)
-            store_emb(NI - 2)
+            weigh_emb(NI - 2)
+            turn_weighted(NI - 2, "b")
             emb_product(NI - 1)
+            label_sums(NI - 3)
+            store_emb(NI - 2)
             emb_sum(NI - 1)
-            turn_emb(NI - 1)
-            label_sums(NI - 1)
+            label_sums(NI - 2)
+            turn_emb(NI - 1, "z")
+            weigh_emb(NI - 1)
+            turn_weighted(NI - 1, "z")
             store_emb(NI - 1)
-            nc.vector.tensor_tensor(
-                out=score[:],
-                in0=sc[0][:, 0 : 4 * C].rearrange("p (st c) -> p st c", c=C),
-                in1=dbias[:].unsqueeze(1).to_broadcast([P, 4, C]),
-                op=ALU.add,
-            )
+            label_sums(NI - 1)
             nc.sync.dma_start(out=out_1.rearrange("(r st) c -> r st c", st=4), in_=score[:])

@@ -19,9 +19,8 @@ P = 128
 NI = F // P
 NR = 2 * NI
 WCH = 256
-LEAD = 2
+LEAD = 3
 LAG = 2
-SPARE = ("te", "sc", "a", "b")
 
 
 def tile_endpoint_span_scoring_f4_kernel(
@@ -74,17 +73,11 @@ def tile_endpoint_span_scoring_f4_kernel(
         def bank_of(name):
             return (twin if name in ("z", "tp") else lone).tile([P, 512], F32, name=name)
 
-        spare = []
-
-        def spare_bank():
-            spare.append(SPARE[len(spare) % len(SPARE)])
-            return bank_of(spare[-1])
-
         xw, xbank, xg, pbank, pg = {}, {}, {}, {}, {}
         wg, wq, z, gl, tph, hg, hq, ab, tv, uv, ev, tpe, sc, vv = ({} for n in range(14))
 
         def spread_scale(g):
-            bank = spare_bank()
+            bank = bank_of("ab"[g])
             for t in range(4):
                 nc.tensor.transpose(bank[:, P * t : P * (t + 1)], xs[:, g, t : t + 1].to_broadcast([P, P]), ident[:])
             nc.scalar.copy(
@@ -114,7 +107,7 @@ def tile_endpoint_span_scoring_f4_kernel(
 
         def turn_x(n, g, name):
             if n % 2 == 0:
-                xbank[n // 2, g] = bank_of(name) if name else spare_bank()
+                xbank[n // 2, g] = bank_of(name)
             turn_words(xbank[n // 2, g], n % 2, xw.pop((n, g))[:].bitcast(F32))
 
         def copy_x(m, g):
@@ -125,8 +118,8 @@ def tile_endpoint_span_scoring_f4_kernel(
             span = slice(256 * jp, 256 * (jp + 1))
             quant(xcod[h, g][:, span], xsca[h, g][:, span], xg.pop((m, g))[:].rearrange("p r q -> p (r q)"))
 
-        def turn_p(e, sp, h):
-            pbank[e, sp, h] = spare_bank()
+        def turn_p(e, sp, h, name):
+            pbank[e, sp, h] = bank_of(name)
             for ss in range(2):
                 turn_words(pbank[e, sp, h], ss, praw[e, sp][:, ss, 512 * h : 512 * (h + 1)].bitcast(F32))
 
@@ -137,10 +130,15 @@ def tile_endpoint_span_scoring_f4_kernel(
             span = slice(256 * sp, 256 * (sp + 1))
             quant(pcod[e, h][:, span], psca[e, h][:, span], pg.pop((e, sp, h))[:].rearrange("p r q -> p (r q)"))
 
+        def warm_up(name="z"):
+            bank = bank_of(name)
+            twice = ident[:].unsqueeze(1).to_broadcast([P, 2, P])
+            nc.tensor.matmul(out=bank[:, 0 : 2 * P], lhsT=ident[:], rhs=twice, start=True, stop=True)
+
         def weave_w(r, engine):
             i, e = divmod(r, 2)
             c, o = divmod(i * P, WCH)
-            if r % 2 == 0 and r >= LEAD + 2:
+            if r % 2 == 1 and r >= LEAD + 2:
                 wg[r] = stage.tile([P, 2, P, 4], BF16, name="wgp", align_bytes=64, bufs=1)
             else:
                 wg[r] = stage.tile([P, 2, P, 4], BF16, name="wg", align_bytes=64, bufs=3)
@@ -174,7 +172,7 @@ def tile_endpoint_span_scoring_f4_kernel(
 
         def gelu(r, h):
             i, e = divmod(r, 2)
-            gl[r, h] = stage.tile([P, 512], F32, name="gl", bufs=6)
+            gl[r, h] = stage.tile([P, 512], F32, name="gl", bufs=LEAD + 4)
             nc.scalar.activation(
                 out=gl[r, h][:], in_=z.pop((r, h))[:], func=ACT.Gelu_apprx_tanh, bias=cols[:, e, i : i + 1]
             )
@@ -285,38 +283,37 @@ def tile_endpoint_span_scoring_f4_kernel(
                 nc.gpsimd.dma_start(out=sal[e][:], in_=gv.rearrange("(h m j) -> m h j", h=2, j=4))
             nc.gpsimd.dma_start(out=dbias[:], in_=d.partition_broadcast(P))
 
-            def x_turns(m, name):
-                for g in range(2):
-                    for n in (2 * m, 2 * m + 1):
-                        if (n, g) not in xw:
-                            prod_x(n, g)
-                        turn_x(n, g, name)
+            def x_turns(m, g, name):
+                for n in (2 * m, 2 * m + 1):
+                    if (n, g) not in xw:
+                        prod_x(n, g)
+                    turn_x(n, g, name)
 
-            def x_copies(m):
-                for g in range(2):
-                    copy_x(m, g)
-
-            def p_turns(e, sp):
-                for h in range(2):
-                    turn_p(e, sp, h)
-
-            def p_copies(e, sp):
-                for h in range(2):
-                    copy_p(e, sp, h)
-
+            warm_up()
             spread_scale(0)
             spread_scale(1)
+            warm_up()
             nc.scalar.copy(out=rows32[:], in_=rows[:])
-            x_turns(0, "tp")
-            small = spare_bank()
-            nc.tensor.transpose(small[:, 0:P], rows32[:], ident[:])
+            x_turns(0, 0, "tp")
+            warm_up()
             weave_w(0, nc.scalar)
-            x_copies(0)
+            copy_x(0, 0)
+            x_turns(0, 1, "tp")
+            copy_x(0, 1)
+            small = bank_of("te")
+            nc.tensor.transpose(small[:, 0:P], rows32[:], ident[:])
             nc.scalar.copy(out=cols[:].rearrange("p q i -> p (q i)"), in_=small[:, 0 : 4 * NI])
-            x_turns(1, "z")
+            warm_up()
             weave_w(1, nc.scalar)
-            x_copies(1)
-            p_turns(0, 0)
+            x_turns(1, 0, "z")
+            copy_x(1, 0)
+            turn_p(0, 0, 0, "a")
+            x_turns(1, 1, "z")
+            copy_x(1, 1)
+            warm_up("tp")
+            turn_p(0, 0, 1, "b")
+            turn_p(0, 1, 0, "te")
+            turn_p(0, 1, 1, "sc")
             quant_x(0, 0)
             quant_x(0, 1)
             quant_w(0)
@@ -325,30 +322,39 @@ def tile_endpoint_span_scoring_f4_kernel(
             prod_x(5, 0)
             quant_x(1, 1)
             quant_w(1)
-            p_copies(0, 0)
+            weave_w(2, nc.scalar)
+            copy_p(0, 0, 0)
             project(0, 0)
             gelu(0, 0)
+            x_turns(2, 0, "tp")
+            copy_x(2, 0)
+            weave_w(3, nc.scalar)
+            x_turns(2, 1, "a")
+            quant_w(2)
             project(1, 0)
+            copy_x(2, 1)
             gelu(1, 0)
-            x_turns(2, "tp")
-            x_copies(2)
-            p_turns(0, 1)
-            x_turns(3, None)
-            x_copies(3)
             turn_h(0, 0)
-            weave_w(2, nc.vector)
+            x_turns(3, 0, "tp")
+            project(2, 0)
+            copy_x(3, 0)
+            x_turns(3, 1, "a")
+            copy_x(3, 1)
+            gelu(2, 0)
+            weigh_h(0, 0)
+            turn_h(1, 0)
             quant_x(2, 0)
             quant_x(2, 1)
-            quant_w(2)
+            quant_w(3)
             quant_x(3, 0)
             quant_x(3, 1)
-            weave_w(3, nc.vector)
-            weigh_h(0, 0)
-            p_copies(0, 1)
-            quant_p(0, 0, 0)
-            quant_w(3)
+            copy_p(0, 0, 1)
+            copy_p(0, 1, 0)
+            weave_w(4, nc.vector)
+            weigh_h(1, 0)
+            quant_w(4)
             quant_h(0, 0)
-            quant_p(0, 0, 1)
+            quant_h(1, 0)
 
             for n in range(NR - 2):
                 late, early = n - 1, n - 1 + LEAD
@@ -365,9 +371,11 @@ def tile_endpoint_span_scoring_f4_kernel(
                     turn_h(late, 1)
                 if live(early):
                     turn_h(early, 0)
-                if n < 2:
-                    p_turns(1, n)
-                    p_copies(1, n)
+                if n == 0:
+                    copy_p(0, 1, 1)
+                for sp, h, name in ([(0, 0, "a"), (1, 0, "b")], [(0, 1, "te")], [(1, 1, "sc")])[n] if n < 3 else []:
+                    turn_p(1, sp, h, name)
+                    copy_p(1, sp, h)
                 if not odd and i >= 1:
                     turn_emb(i - 1)
                     weigh_emb(i - 1)
@@ -388,15 +396,16 @@ def tile_endpoint_span_scoring_f4_kernel(
                     quant_h(late, 1)
                 if not odd and i >= 2:
                     label_sums(i - 2)
-                if n < 3:
-                    quant_p(*divmod(n + 1, 2), 0)
-                    quant_p(*divmod(n + 1, 2), 1)
+                for e, sp, h in (
+                    [(0, 0, 0), (0, 1, 0)], [(0, 0, 1), (0, 1, 1), (1, 0, 0)], [(1, 1, 0), (1, 0, 1), (1, 1, 1)]
+                )[n] if n < 3 else []:
+                    quant_p(e, sp, h)
                 if odd and live(n - LAG) and live(early):
                     weigh_h(early, 0)
                 if odd and 1 <= i <= NI:
                     store_emb(i - 1)
                 if live(n + LEAD + 2) and (n % 2 or n == 0):
-                    weave_w(n + LEAD + 2, nc.scalar if n >= 2 else nc.vector)
+                    weave_w(n + LEAD + 2, nc.scalar if n else nc.vector)
                 if n == 2:
                     halves = dbias[:].rearrange("p (i c) -> p c i", c=2)
                     for c in range(2):
@@ -417,11 +426,9 @@ def tile_endpoint_span_scoring_f4_kernel(
                 gelu(r, 1)
             gather(last - 3)
             turn_h(last - 2, 1)
-            turn_h(last, 0)
             label_sums(NI - 4)
             emb_factor(NI - 2)
             weigh_h(last - 2, 1)
-            weigh_h(last, 0)
             quant_h(last - 2, 1)
             turn_emb(NI - 3)
             weigh_emb(NI - 3)
@@ -430,7 +437,6 @@ def tile_endpoint_span_scoring_f4_kernel(
             turn_weighted(NI - 3)
             gather(last - 2)
             weigh_h(last - 1, 1)
-            quant_h(last, 0)
             weigh_h(last, 1)
             quant_h(last - 1, 1)
             store_emb(NI - 3)

@@ -20,6 +20,7 @@ NI = F // P
 NR = 2 * NI
 WCH = 256
 LEAD = 3
+NV = 5
 LAG = 2
 
 
@@ -32,9 +33,9 @@ def tile_endpoint_span_scoring_f4_kernel(
         stage = ctx.enter_context(tc.tile_pool(name="stage", bufs=3))
         twin = ctx.enter_context(tc.psum_pool(name="twin", bufs=2))
         lone = ctx.enter_context(tc.psum_pool(name="lone", bufs=1))
+        trio = ctx.enter_context(tc.psum_pool(name="trio", bufs=3))
 
         ident = keep.tile([P, P], F32, name="ident")
-        make_identity(nc, ident[:])
 
         xb = [keep.tile([P, 2, D], U8, name=f"xb{n}", align_bytes=64) for n in range(4)]
         xs = keep.tile([P, 2, 4], F32, name="xs")
@@ -51,7 +52,9 @@ def tile_endpoint_span_scoring_f4_kernel(
         rows = keep.tile([P, P], BF16, name="rows")
         rows32 = keep.tile([P, P], F32, name="rows32")
         cols = keep.tile([P, 4, NI], F32, name="cols")
-        dcol = keep.tile([P, NI], F32, name="dcol")
+        sums = keep.tile([P, 4, C], F32, name="sums")
+        vrow = keep.tile([P, NV * P], BF16, name="vrow")
+        vmat = keep.tile([P, NI, 2], F32, name="vmat")
         dbias = keep.tile([P, C], BF16, name="dbias")
         score = keep.tile([P, 4, C], F32, name="score")
 
@@ -71,10 +74,10 @@ def tile_endpoint_span_scoring_f4_kernel(
             nc.sync.dma_start(out=praw[e, sp][:], in_=pv[e][:, 2 * sp : 2 * sp + 2, :])
 
         def bank_of(name):
-            return (twin if name in ("z", "tp") else lone).tile([P, 512], F32, name=name)
+            return {"z": twin, "tp": trio}.get(name, lone).tile([P, 512], F32, name=name)
 
         xw, xbank, xg, pbank, pg = {}, {}, {}, {}, {}
-        wg, wq, z, gl, tph, hg, hq, ab, tv, uv, ev, tpe, sc, vv = ({} for n in range(14))
+        wg, wq, z, gl, tph, hg, hq, ab, tv, uv, ev, tpe, eo, vv = ({} for n in range(14))
 
         def spread_scale(g):
             bank = bank_of("ab"[g])
@@ -129,11 +132,6 @@ def tile_endpoint_span_scoring_f4_kernel(
         def quant_p(e, sp, h):
             span = slice(256 * sp, 256 * (sp + 1))
             quant(pcod[e, h][:, span], psca[e, h][:, span], pg.pop((e, sp, h))[:].rearrange("p r q -> p (r q)"))
-
-        def warm_up(name="z"):
-            bank = bank_of(name)
-            twice = ident[:].unsqueeze(1).to_broadcast([P, 2, P])
-            nc.tensor.matmul(out=bank[:, 0 : 2 * P], lhsT=ident[:], rhs=twice, start=True, stop=True)
 
         def weave_w(r, engine):
             i, e = divmod(r, 2)
@@ -224,7 +222,7 @@ def tile_endpoint_span_scoring_f4_kernel(
             nc.vector.tensor_tensor(out=uv[i][:], in0=ab.pop(2 * i + 1)[:], in1=tv.pop(i)[:], op=ALU.mult)
 
         def emb_sum(i):
-            ev[i] = stage.tile([P, S], F32, name="ev", bufs=3)
+            ev[i] = stage.tile([P, S], F32, name="ev", bufs=4)
             nc.vector.tensor_tensor(out=ev[i][:], in0=ab.pop(2 * i)[:], in1=uv.pop(i)[:], op=ALU.add)
 
         def turn_emb(i, name="te"):
@@ -232,45 +230,59 @@ def tile_endpoint_span_scoring_f4_kernel(
             for st in range(4):
                 nc.tensor.transpose(tpe[i][:, P * st : P * (st + 1)], ev[i][:, P * st : P * (st + 1)], ident[:])
 
-        def weigh_emb(i):
-            vv[i] = stage.tile([P, S], F32, name="vv", bufs=2)
-            nc.scalar.activation(out=vv[i][:], in_=ev.pop(i)[:], func=ACT.Identity, scale=cols[:, 3, i : i + 1], bias=dcol[:, i : i + 1])
+        def copy_emb(i):
+            eo[i] = stage.tile([P, 4, P], F32, name="eo", bufs=4)
+            nc.scalar.copy(out=eo[i][:].rearrange("p st f -> p (st f)"), in_=tpe.pop(i)[:])
+            nc.sync.dma_start(out=out_0.rearrange("(r st) f -> r st f", st=4)[:, :, P * i : P * (i + 1)], in_=eo[i][:])
 
-        def turn_weighted(i, name="sc"):
-            sc[i] = bank_of(name)
-            src = vv.pop(i)
-            for st in range(4):
-                nc.tensor.transpose(sc[i][:, P * st : P * (st + 1)], src[:, P * st : P * (st + 1)], ident[:])
+        def weigh_emb(i, engine, name="vv"):
+            vv[i] = stage.tile([P, 4, P], F32, name=name, bufs=1)
+            row = vrow[:, P * i : P * (i + 1)].unsqueeze(1).to_broadcast([P, 4, P])
+            engine.tensor_tensor(out=vv[i][:], in0=eo[i][:], in1=row, op=ALU.mult)
 
         def label_sums(i):
             nc.vector.tensor_reduce(
-                out=score[:, :, 2 * i : 2 * i + 2],
-                in_=sc.pop(i)[:].rearrange("p (st c f) -> p st c f", st=4, c=2),
+                out=sums[:, :, 2 * i : 2 * i + 2],
+                in_=vv.pop(i)[:].rearrange("p st (c f) -> p st c f", c=2),
                 op=ALU.add,
                 axis=mybir.AxisListType.X,
             )
 
-        def store_emb(i):
-            eo = stage.tile([P, S], F32, name="eo", bufs=2)
-            nc.scalar.copy(out=eo[:], in_=tpe.pop(i)[:])
-            nc.sync.dma_start(
-                out=out_0.rearrange("(r st) f -> r st f", st=4)[:, :, P * i : P * (i + 1)],
-                in_=eo[:].rearrange("p (st f) -> p st f", st=4),
+        def label_matmuls(i):
+            if i == NV:
+                vv["bank"] = bank_of("tp")
+            for st in range(4):
+                o = C * st + 2 * i
+                nc.tensor.matmul(
+                    out=vv["bank"][:, o : o + 2],
+                    lhsT=ev[i][:, P * st : P * (st + 1)],
+                    rhs=vmat[:, i, :],
+                    start=True,
+                    stop=True,
+                )
+
+        def add_offsets(src, labels):
+            width = labels.stop - labels.start
+            nc.vector.tensor_tensor(
+                out=score[:, :, labels],
+                in0=src[:, :, labels],
+                in1=dbias[:, labels].unsqueeze(1).to_broadcast([P, 4, width]),
+                op=ALU.add,
             )
 
         def live(r):
             return 0 <= r < NR
 
         with tc.manual_schedule():
+            make_identity(nc, ident[:])
             nc.vector.memset(rows[:], 0.0)
+            nc.vector.memset(vmat[:], 0.0)
             nc.sync.dma_start(out=xs[:], in_=x_scale.rearrange("o (g p t) -> p (o g) t", p=P, t=4))
             load_x(0)
-            for q, vec in enumerate((bs, be, mix, v)):
-                nc.scalar.dma_start(out=rows[NI * q : NI * (q + 1), :], in_=vec.rearrange("(i f) -> i f", f=P))
             load_x(1)
             load_w(0, 0)
-            load_w(1, 0)
             load_p(0, 0)
+            load_w(1, 0)
             load_x(2)
             load_p(0, 1)
             load_x(3)
@@ -279,6 +291,9 @@ def tile_endpoint_span_scoring_f4_kernel(
             for c in range(1, F // WCH):
                 load_w(0, c)
                 load_w(1, c)
+            nc.sync.dma_start(out=vrow[:], in_=v[0 : NV * P].partition_broadcast(P))
+            for q, vec in enumerate((bs, be, mix, v)):
+                nc.gpsimd.dma_start(out=rows[NI * q : NI * (q + 1), :], in_=vec.rearrange("(i f) -> i f", f=P))
             for e, gv in enumerate((gs, ge)):
                 nc.gpsimd.dma_start(out=sal[e][:], in_=gv.rearrange("(h m j) -> m h j", h=2, j=4))
             nc.gpsimd.dma_start(out=dbias[:], in_=d.partition_broadcast(P))
@@ -289,54 +304,50 @@ def tile_endpoint_span_scoring_f4_kernel(
                         prod_x(n, g)
                     turn_x(n, g, name)
 
-            warm_up()
             spread_scale(0)
             spread_scale(1)
-            warm_up()
-            nc.scalar.copy(out=rows32[:], in_=rows[:])
             x_turns(0, 0, "tp")
-            warm_up()
             weave_w(0, nc.scalar)
             copy_x(0, 0)
             x_turns(0, 1, "tp")
+            turn_p(0, 0, 0, "a")
+            weave_w(2, nc.scalar)
             copy_x(0, 1)
-            small = bank_of("te")
-            nc.tensor.transpose(small[:, 0:P], rows32[:], ident[:])
-            nc.scalar.copy(out=cols[:].rearrange("p q i -> p (q i)"), in_=small[:, 0 : 4 * NI])
-            warm_up()
-            weave_w(1, nc.scalar)
             x_turns(1, 0, "z")
             copy_x(1, 0)
-            turn_p(0, 0, 0, "a")
+            turn_p(0, 0, 1, "b")
             x_turns(1, 1, "z")
             copy_x(1, 1)
-            warm_up("tp")
-            turn_p(0, 0, 1, "b")
+            nc.scalar.copy(out=rows32[:], in_=rows[:])
+            weave_w(1, nc.scalar)
             turn_p(0, 1, 0, "te")
-            turn_p(0, 1, 1, "sc")
+            small = bank_of("tp")
+            nc.tensor.transpose(small[:, 0:P], rows32[:], ident[:])
+            nc.scalar.copy(out=cols[:].rearrange("p q i -> p (q i)"), in_=small[:, 0 : 4 * NI])
             quant_x(0, 0)
             quant_x(0, 1)
             quant_w(0)
-            prod_x(4, 0)
             quant_x(1, 0)
-            prod_x(5, 0)
+            prod_x(4, 0)
             quant_x(1, 1)
+            prod_x(5, 0)
             quant_w(1)
-            weave_w(2, nc.scalar)
             copy_p(0, 0, 0)
             project(0, 0)
             gelu(0, 0)
             x_turns(2, 0, "tp")
             copy_x(2, 0)
-            weave_w(3, nc.scalar)
+            turn_p(0, 1, 1, "tp")
+            copy_p(0, 1, 1)
+            project(1, 0)
             x_turns(2, 1, "a")
             quant_w(2)
-            project(1, 0)
-            copy_x(2, 1)
             gelu(1, 0)
+            copy_x(2, 1)
+            weave_w(3, nc.scalar)
             turn_h(0, 0)
-            x_turns(3, 0, "tp")
             project(2, 0)
+            x_turns(3, 0, "tp")
             copy_x(3, 0)
             x_turns(3, 1, "a")
             copy_x(3, 1)
@@ -354,9 +365,8 @@ def tile_endpoint_span_scoring_f4_kernel(
             weigh_h(1, 0)
             quant_w(4)
             quant_h(0, 0)
-            quant_h(1, 0)
 
-            for n in range(NR - 2):
+            for n in range(NR - LEAD):
                 late, early = n - 1, n - 1 + LEAD
                 i, odd = divmod(n - LAG, 2)
                 if live(n + LEAD):
@@ -371,16 +381,11 @@ def tile_endpoint_span_scoring_f4_kernel(
                     turn_h(late, 1)
                 if live(early):
                     turn_h(early, 0)
-                if n == 0:
-                    copy_p(0, 1, 1)
-                for sp, h, name in ([(0, 0, "a"), (1, 0, "b")], [(0, 1, "te")], [(1, 1, "sc")])[n] if n < 3 else []:
+                for sp, h, name in ([(0, 0, "a"), (1, 0, "b")], [(0, 1, "te")], [(1, 1, "te")])[n] if n < 3 else []:
                     turn_p(1, sp, h, name)
                     copy_p(1, sp, h)
-                if not odd and i >= 1:
-                    turn_emb(i - 1)
-                    weigh_emb(i - 1)
                 if odd and i >= 1:
-                    turn_weighted(i - 1)
+                    turn_emb(i - 1)
                 if live(n - LAG):
                     if odd:
                         emb_product(i)
@@ -394,69 +399,81 @@ def tile_endpoint_span_scoring_f4_kernel(
                     weigh_h(early, 0)
                 if live(late):
                     quant_h(late, 1)
-                if not odd and i >= 2:
-                    label_sums(i - 2)
+                if live(early - 1):
+                    quant_h(early - 1, 0)
                 for e, sp, h in (
                     [(0, 0, 0), (0, 1, 0)], [(0, 0, 1), (0, 1, 1), (1, 0, 0)], [(1, 1, 0), (1, 0, 1), (1, 1, 1)]
                 )[n] if n < 3 else []:
                     quant_p(e, sp, h)
+                if not odd and i >= 2:
+                    copy_emb(i - 2)
+                if live(n + LEAD + 2):
+                    if odd or n == 0:
+                        weave_w(n + LEAD + 2, nc.scalar if n else nc.vector)
+                    quant_w(n + LEAD + 2)
+                if n == 4:
+                    nc.scalar.copy(out=vmat[0:64, :, 0], in_=cols[0:64, 3, :])
+                    nc.scalar.copy(out=vmat[64:128, :, 1], in_=cols[64:128, 3, :])
+                if odd and i >= 3:
+                    label_sums(i - 3)
+                if odd and i >= 2:
+                    weigh_emb(i - 2, nc.gpsimd if i >= 3 else nc.vector)
                 if odd and live(n - LAG) and live(early):
                     weigh_h(early, 0)
-                if odd and 1 <= i <= NI:
-                    store_emb(i - 1)
-                if live(n + LEAD + 2) and (n % 2 or n == 0):
-                    weave_w(n + LEAD + 2, nc.scalar if n else nc.vector)
-                if n == 2:
-                    halves = dbias[:].rearrange("p (i c) -> p c i", c=2)
-                    for c in range(2):
-                        part = slice(64 * c, 64 * (c + 1))
-                        nc.scalar.activation(out=dcol[part, :], in_=halves[part, c, :], func=ACT.Copy, scale=1.0 / 64)
-                if odd and live(n + LEAD + 2):
-                    quant_w(n + LEAD + 2)
-                if live(early):
-                    quant_h(early, 0)
-                if not odd and live(n + LEAD + 2):
-                    quant_w(n + LEAD + 2)
                 if not odd and live(n + LEAD + 4):
                     weave_w(n + LEAD + 4, nc.gpsimd)
 
             last = NR - 1
-            for r in (last - 1, last):
+            label_sums(NV - 3)
+            weigh_emb(NV - 2, nc.gpsimd)
+            for r in (last - 2, last - 1):
                 project(r, 1)
                 gelu(r, 1)
-            gather(last - 3)
+            gather(last - 4)
+            turn_h(last - 3, 1)
+            turn_h(last, 0)
+            turn_emb(NI - 4)
+            emb_product(NI - 3)
+            weigh_h(last - 3, 1)
+            emb_sum(NI - 3)
+            quant_h(last - 3, 1)
+            quant_h(last - 1, 0)
+            project(last, 1)
+            gelu(last, 1)
+            copy_emb(NI - 4)
             turn_h(last - 2, 1)
-            label_sums(NI - 4)
+            weigh_h(last, 0)
+            turn_h(last - 1, 1)
+            gather(last - 3)
             emb_factor(NI - 2)
             weigh_h(last - 2, 1)
-            quant_h(last - 2, 1)
+            turn_h(last, 1)
             turn_emb(NI - 3)
-            weigh_emb(NI - 3)
-            turn_h(last - 1, 1, "z")
-            turn_h(last, 1, "z")
-            turn_weighted(NI - 3)
-            gather(last - 2)
+            copy_emb(NI - 3)
             weigh_h(last - 1, 1)
+            quant_h(last - 2, 1)
+            quant_h(last, 0)
+            gather(last - 2)
             weigh_h(last, 1)
             quant_h(last - 1, 1)
-            store_emb(NI - 3)
+            gather(last - 1, "z")
+            emb_factor(NI - 1)
             emb_product(NI - 2)
             quant_h(last, 1)
-            gather(last - 1, "tp")
-            gather(last, "tp")
-            emb_factor(NI - 1)
+            gather(last, "z")
+            label_matmuls(NI - 3)
             emb_sum(NI - 2)
             turn_emb(NI - 2)
-            weigh_emb(NI - 2)
-            turn_weighted(NI - 2, "b")
+            label_matmuls(NI - 2)
             emb_product(NI - 1)
-            label_sums(NI - 3)
-            store_emb(NI - 2)
+            copy_emb(NI - 2)
             emb_sum(NI - 1)
-            label_sums(NI - 2)
-            turn_emb(NI - 1, "z")
-            weigh_emb(NI - 1)
-            turn_weighted(NI - 1, "z")
-            store_emb(NI - 1)
-            label_sums(NI - 1)
+            weigh_emb(NV - 1, nc.vector, "vt")
+            label_sums(NV - 2)
+            turn_emb(NI - 1, "b")
+            label_matmuls(NI - 1)
+            copy_emb(NI - 1)
+            label_sums(NV - 1)
+            add_offsets(vv["bank"][:, 0 : 4 * C].rearrange("p (st c) -> p st c", c=C), slice(2 * NV, C))
+            add_offsets(sums, slice(0, 2 * NV))
             nc.sync.dma_start(out=out_1.rearrange("(r st) c -> r st c", st=4), in_=score[:])

@@ -97,13 +97,11 @@ def tile_endpoint_span_scoring_f4_kernel(
                 o = 256 * u + P * half
                 nc.tensor.transpose(bank[:, o : o + P], words[:, u:256:2], ident[:])
 
-        def copy_words(bank, name):
-            dst = stage.tile([P, 256, 4], BF16, name=name, align_bytes=64, bufs=8)
+        def copy_words(bank, dst):
             nc.scalar.copy(
-                out=dst[:].rearrange("p r q -> p (r q)").bitcast(F32).rearrange("p (r u) -> p r u", u=2),
+                out=dst.rearrange("p r q -> p (r q)").bitcast(F32).rearrange("p (r u) -> p r u", u=2),
                 in_=bank[:].rearrange("p (u r) -> p r u", u=2),
             )
-            return dst
 
         def quant(cod, sca, src):
             nc.vector.quantize_mx(out=cod.bitcast(FP8X4), scales=sca, in_=src)
@@ -114,7 +112,8 @@ def tile_endpoint_span_scoring_f4_kernel(
             turn_words(xbank[n // 2, g], n % 2, xw.pop((n, g))[:].bitcast(F32))
 
         def copy_x(m, g):
-            xg[m, g] = copy_words(xbank.pop((m, g)), "xg")
+            xg[m, g] = stage.tile([P, 256, 4], BF16, name="xg", align_bytes=64, bufs=6)
+            copy_words(xbank.pop((m, g)), xg[m, g][:])
 
         def quant_x(m, g):
             h, jp = divmod(m, 2)
@@ -127,16 +126,17 @@ def tile_endpoint_span_scoring_f4_kernel(
                 turn_words(pbank[e, sp, h], ss, praw[e, sp][:, ss, 512 * h : 512 * (h + 1)].bitcast(F32))
 
         def copy_p(e, sp, h):
-            pg[e, sp, h] = copy_words(pbank.pop((e, sp, h)), "pg")
+            if (e, h) not in pg:
+                pg[e, h] = stage.tile([P, S, 4], BF16, name="pg", align_bytes=64, bufs=4)
+            copy_words(pbank.pop((e, sp, h)), pg[e, h][:, 256 * sp : 256 * (sp + 1), :])
 
-        def quant_p(e, sp, h):
-            span = slice(256 * sp, 256 * (sp + 1))
-            quant(pcod[e, h][:, span], psca[e, h][:, span], pg.pop((e, sp, h))[:].rearrange("p r q -> p (r q)"))
+        def quant_p(e, h):
+            quant(pcod[e, h][:], psca[e, h][:], pg.pop((e, h))[:].rearrange("p r q -> p (r q)"))
 
         def weave_w(r, engine):
             i, e = divmod(r, 2)
             c, o = divmod(i * P, WCH)
-            if r % 2 == 1 and r >= LEAD + 2:
+            if r >= LEAD + 2 and (r % 2 or r == LEAD + 3):
                 wg[r] = stage.tile([P, 2, P, 4], BF16, name="wgp", align_bytes=64, bufs=1)
             else:
                 wg[r] = stage.tile([P, 2, P, 4], BF16, name="wg", align_bytes=64, bufs=3)
@@ -181,20 +181,28 @@ def tile_endpoint_span_scoring_f4_kernel(
             for j in range(4):
                 nc.tensor.transpose(tph[r, h][:, P * j : P * (j + 1)], src[:, P * j : P * (j + 1)], ident[:])
 
-        def weigh_h(r, h):
-            hg[r, h] = stage.tile([P, P, 4], BF16, name="hg", align_bytes=64, bufs=4)
+        def weigh_h(r, h, mate=None):
+            if mate in hg:
+                hg[r, h] = (hg[mate][0], 1)
+            else:
+                width = 1 if mate is None else 2
+                hg[r, h] = (stage.tile([P, width, P, 4], BF16, name="hg", align_bytes=64, bufs=4), 0)
+            tile, slot = hg[r, h]
             nc.vector.tensor_tensor(
-                out=hg[r, h][:],
+                out=tile[:, slot],
                 in0=tph.pop((r, h))[:].rearrange("p (j f) -> p f j", j=4),
                 in1=sal[r % 2][:, h, :].unsqueeze(1).to_broadcast([P, P, 4]),
                 op=ALU.mult,
             )
 
-        def quant_h(r, h):
-            cod = stage.tile([P, P], U32, name="hcod", align_bytes=64, bufs=LEAD + 8)
-            sca = stage.tile([P, P], U8, name="hsca", align_bytes=64, bufs=LEAD + 8)
-            quant(cod[:], sca[:], hg.pop((r, h))[:].rearrange("p f q -> p (f q)"))
-            hq[r, h] = (cod, sca)
+        def quant_h(*units):
+            width = P * len(units)
+            cod = stage.tile([P, width], U32, name="hcod", align_bytes=64, bufs=LEAD + 6)
+            sca = stage.tile([P, width], U8, name="hsca", align_bytes=64, bufs=LEAD + 6)
+            quant(cod[:], sca[:], hg[units[0]][0][:].rearrange("p s f q -> p (s f q)"))
+            for unit in units:
+                slot = hg.pop(unit)[1]
+                hq[unit] = (cod[:, P * slot : P * (slot + 1)], sca[:, P * slot : P * (slot + 1)])
 
         def gather(r, name=None):
             e = r % 2
@@ -203,8 +211,8 @@ def tile_endpoint_span_scoring_f4_kernel(
                 cod, sca = hq.pop((r, h))
                 nc.tensor.matmul_mx(
                     out=ab[r][:],
-                    lhsT=cod[:].bitcast(FP8X4),
-                    lhsT_scale=sca[:],
+                    lhsT=cod.bitcast(FP8X4),
+                    lhsT_scale=sca,
                     rhs=pcod[e, h][:].bitcast(FP8X4),
                     rhs_scale=psca[e, h][:],
                     start=(h == 0),
@@ -280,6 +288,8 @@ def tile_endpoint_span_scoring_f4_kernel(
             nc.sync.dma_start(out=xs[:], in_=x_scale.rearrange("o (g p t) -> p (o g) t", p=P, t=4))
             load_x(0)
             load_x(1)
+            for q, vec in enumerate((bs, be, mix, v)):
+                nc.scalar.dma_start(out=rows[NI * q : NI * (q + 1), :], in_=vec.rearrange("(i f) -> i f", f=P))
             load_w(0, 0)
             load_p(0, 0)
             load_w(1, 0)
@@ -292,8 +302,6 @@ def tile_endpoint_span_scoring_f4_kernel(
                 load_w(0, c)
                 load_w(1, c)
             nc.sync.dma_start(out=vrow[:], in_=v[0 : NV * P].partition_broadcast(P))
-            for q, vec in enumerate((bs, be, mix, v)):
-                nc.gpsimd.dma_start(out=rows[NI * q : NI * (q + 1), :], in_=vec.rearrange("(i f) -> i f", f=P))
             for e, gv in enumerate((gs, ge)):
                 nc.gpsimd.dma_start(out=sal[e][:], in_=gv.rearrange("(h m j) -> m h j", h=2, j=4))
             nc.gpsimd.dma_start(out=dbias[:], in_=d.partition_broadcast(P))
@@ -306,9 +314,13 @@ def tile_endpoint_span_scoring_f4_kernel(
 
             spread_scale(0)
             spread_scale(1)
+            nc.scalar.copy(out=rows32[:], in_=rows[:])
             x_turns(0, 0, "tp")
             weave_w(0, nc.scalar)
             copy_x(0, 0)
+            small = bank_of("te")
+            nc.tensor.transpose(small[:, 0:P], rows32[:], ident[:])
+            nc.scalar.copy(out=cols[:].rearrange("p q i -> p (q i)"), in_=small[:, 0 : 4 * NI])
             x_turns(0, 1, "tp")
             turn_p(0, 0, 0, "a")
             weave_w(2, nc.scalar)
@@ -318,12 +330,9 @@ def tile_endpoint_span_scoring_f4_kernel(
             turn_p(0, 0, 1, "b")
             x_turns(1, 1, "z")
             copy_x(1, 1)
-            nc.scalar.copy(out=rows32[:], in_=rows[:])
             weave_w(1, nc.scalar)
             turn_p(0, 1, 0, "te")
-            small = bank_of("tp")
-            nc.tensor.transpose(small[:, 0:P], rows32[:], ident[:])
-            nc.scalar.copy(out=cols[:].rearrange("p q i -> p (q i)"), in_=small[:, 0 : 4 * NI])
+            turn_p(0, 1, 1, "tp")
             quant_x(0, 0)
             quant_x(0, 1)
             quant_w(0)
@@ -331,45 +340,48 @@ def tile_endpoint_span_scoring_f4_kernel(
             prod_x(4, 0)
             quant_x(1, 1)
             prod_x(5, 0)
+            prod_x(4, 1)
             quant_w(1)
             copy_p(0, 0, 0)
             project(0, 0)
             gelu(0, 0)
             x_turns(2, 0, "tp")
             copy_x(2, 0)
-            turn_p(0, 1, 1, "tp")
             copy_p(0, 1, 1)
             project(1, 0)
+            weave_w(3, nc.scalar)
             x_turns(2, 1, "a")
             quant_w(2)
-            gelu(1, 0)
-            copy_x(2, 1)
-            weave_w(3, nc.scalar)
             turn_h(0, 0)
             project(2, 0)
+            gelu(1, 0)
+            copy_x(2, 1)
             x_turns(3, 0, "tp")
             copy_x(3, 0)
-            x_turns(3, 1, "a")
+            x_turns(3, 1, "tp")
             copy_x(3, 1)
             gelu(2, 0)
-            weigh_h(0, 0)
+            weigh_h(0, 0, (1, 0))
+            quant_w(3)
+            project(3, 0)
+            gelu(3, 0)
             turn_h(1, 0)
+            turn_p(1, 0, 0, "tp")
             quant_x(2, 0)
             quant_x(2, 1)
-            quant_w(3)
             quant_x(3, 0)
             quant_x(3, 1)
             copy_p(0, 0, 1)
             copy_p(0, 1, 0)
             weave_w(4, nc.vector)
-            weigh_h(1, 0)
+            weigh_h(1, 0, (0, 0))
             quant_w(4)
-            quant_h(0, 0)
+            quant_h((0, 0), (1, 0))
 
             for n in range(NR - LEAD):
                 late, early = n - 1, n - 1 + LEAD
                 i, odd = divmod(n - LAG, 2)
-                if live(n + LEAD):
+                if n and live(n + LEAD):
                     project(n + LEAD, 0)
                     gelu(n + LEAD, 0)
                 if live(n):
@@ -381,7 +393,9 @@ def tile_endpoint_span_scoring_f4_kernel(
                     turn_h(late, 1)
                 if live(early):
                     turn_h(early, 0)
-                for sp, h, name in ([(0, 0, "a"), (1, 0, "b")], [(0, 1, "te")], [(1, 1, "te")])[n] if n < 3 else []:
+                if n == 0:
+                    copy_p(1, 0, 0)
+                for sp, h, name in ([(1, 0, "a"), (0, 1, "b")], [(1, 1, "te")])[n] if n < 2 else []:
                     turn_p(1, sp, h, name)
                     copy_p(1, sp, h)
                 if odd and i >= 1:
@@ -392,23 +406,19 @@ def tile_endpoint_span_scoring_f4_kernel(
                     else:
                         emb_factor(i)
                 if live(late):
-                    weigh_h(late, 1)
+                    weigh_h(late, 1, (early - 1, 0))
                 if odd and live(n - LAG):
                     emb_sum(i)
-                elif live(early):
-                    weigh_h(early, 0)
+                if n < 3:
+                    quant_p(*((0, 0), (0, 1), (1, 1))[n])
                 if live(late):
-                    quant_h(late, 1)
-                if live(early - 1):
-                    quant_h(early - 1, 0)
-                for e, sp, h in (
-                    [(0, 0, 0), (0, 1, 0)], [(0, 0, 1), (0, 1, 1), (1, 0, 0)], [(1, 1, 0), (1, 0, 1), (1, 1, 1)]
-                )[n] if n < 3 else []:
-                    quant_p(e, sp, h)
+                    quant_h((early - 1, 0), (late, 1))
+                if n == 1:
+                    quant_p(1, 0)
                 if not odd and i >= 2:
                     copy_emb(i - 2)
                 if live(n + LEAD + 2):
-                    if odd or n == 0:
+                    if n in (0, 2) or (odd and n > 1):
                         weave_w(n + LEAD + 2, nc.scalar if n else nc.vector)
                     quant_w(n + LEAD + 2)
                 if n == 4:
@@ -418,10 +428,10 @@ def tile_endpoint_span_scoring_f4_kernel(
                     label_sums(i - 3)
                 if odd and i >= 2:
                     weigh_emb(i - 2, nc.gpsimd if i >= 3 else nc.vector)
-                if odd and live(n - LAG) and live(early):
-                    weigh_h(early, 0)
+                if live(early):
+                    weigh_h(early, 0, (late + 1, 1))
                 if not odd and live(n + LEAD + 4):
-                    weave_w(n + LEAD + 4, nc.gpsimd)
+                    weave_w(n + LEAD + (4 if n else 3), nc.gpsimd)
 
             last = NR - 1
             label_sums(NV - 3)
@@ -434,32 +444,30 @@ def tile_endpoint_span_scoring_f4_kernel(
             turn_h(last, 0)
             turn_emb(NI - 4)
             emb_product(NI - 3)
-            weigh_h(last - 3, 1)
+            weigh_h(last - 3, 1, (last - 1, 0))
             emb_sum(NI - 3)
-            quant_h(last - 3, 1)
-            quant_h(last - 1, 0)
+            quant_h((last - 1, 0), (last - 3, 1))
             project(last, 1)
             gelu(last, 1)
             copy_emb(NI - 4)
             turn_h(last - 2, 1)
-            weigh_h(last, 0)
+            weigh_h(last, 0, (last - 2, 1))
             turn_h(last - 1, 1)
             gather(last - 3)
             emb_factor(NI - 2)
-            weigh_h(last - 2, 1)
+            weigh_h(last - 2, 1, (last, 0))
             turn_h(last, 1)
             turn_emb(NI - 3)
             copy_emb(NI - 3)
             weigh_h(last - 1, 1)
-            quant_h(last - 2, 1)
-            quant_h(last, 0)
+            quant_h((last, 0), (last - 2, 1))
             gather(last - 2)
             weigh_h(last, 1)
-            quant_h(last - 1, 1)
+            quant_h((last - 1, 1))
             gather(last - 1, "z")
             emb_factor(NI - 1)
             emb_product(NI - 2)
-            quant_h(last, 1)
+            quant_h((last, 1))
             gather(last, "z")
             label_matmuls(NI - 3)
             emb_sum(NI - 2)

@@ -39,7 +39,6 @@ def tile_endpoint_span_scoring_f4_kernel(
 
         xb = [keep.tile([P, 2, D], U8, name=f"xb{n}", align_bytes=64) for n in range(4)]
         xs = keep.tile([P, 2, 4], F32, name="xs")
-        xsc = [keep.tile([P, 512], F32, name=f"xsc{g}") for g in range(2)]
         xcod = {(h, g): keep.tile([P, 512], U32, name=f"xcod{h}{g}", align_bytes=64) for h in range(2) for g in range(2)}
         xsca = {(h, g): keep.tile([P, 512], U8, name=f"xsca{h}{g}", align_bytes=64) for h in range(2) for g in range(2)}
         praw = {(e, sp): keep.tile([P, 2, T], BF16, name=f"praw{e}{sp}") for e in range(2) for sp in range(2)}
@@ -79,26 +78,22 @@ def tile_endpoint_span_scoring_f4_kernel(
         xw, xbank, xg, pbank, pg = {}, {}, {}, {}, {}
         wg, wq, z, gl, tph, hg, hq, ab, tv, uv, ev, tpe, eo, vv = ({} for n in range(14))
 
-        def spread_scale(g):
-            bank = bank_of("ab"[g])
-            for t in range(4):
-                nc.tensor.transpose(bank[:, P * t : P * (t + 1)], xs[:, g, t : t + 1].to_broadcast([P, P]), ident[:])
-            nc.scalar.copy(
-                out=xsc[g][:].rearrange("p (n t) -> p n t", t=4), in_=bank[:].rearrange("p (t n) -> p n t", t=4)
-            )
-
-        def prod_x(n, g):
+        def cast_x(n, g, engine):
             xw[n, g] = stage.tile([P, 512], BF16, name="xw", bufs=6)
             src = xb[n // 2][:, n % 2, 512 * g : 512 * (g + 1)].bitcast(FP8)
-            nc.vector.tensor_tensor(out=xw[n, g][:], in0=src, in1=xsc[g][:], op=ALU.mult)
+            if engine is nc.vector:
+                nc.vector.tensor_copy(out=xw[n, g][:], in_=src)
+            else:
+                nc.scalar.copy(out=xw[n, g][:], in_=src)
 
         def turn_words(bank, half, words):
             for u in range(2):
                 o = 256 * u + P * half
                 nc.tensor.transpose(bank[:, o : o + P], words[:, u:256:2], ident[:])
 
-        def copy_words(bank, dst):
-            nc.scalar.copy(
+        def copy_words(bank, dst, engine):
+            move = nc.vector.tensor_copy if engine is nc.vector else nc.scalar.copy
+            move(
                 out=dst.rearrange("p r q -> p (r q)").bitcast(F32).rearrange("p (r u) -> p r u", u=2),
                 in_=bank[:].rearrange("p (u r) -> p r u", u=2),
             )
@@ -111,9 +106,14 @@ def tile_endpoint_span_scoring_f4_kernel(
                 xbank[n // 2, g] = bank_of(name)
             turn_words(xbank[n // 2, g], n % 2, xw.pop((n, g))[:].bitcast(F32))
 
-        def copy_x(m, g):
+        def scale_x(m, g):
             xg[m, g] = stage.tile([P, 256, 4], BF16, name="xg", align_bytes=64, bufs=6)
-            copy_words(xbank.pop((m, g)), xg[m, g][:])
+            nc.vector.tensor_tensor(
+                out=xg[m, g][:].rearrange("p r (u e) -> p r u e", e=2),
+                in0=xbank.pop((m, g))[:].bitcast(BF16).rearrange("p (u r e) -> p r u e", u=2, e=2),
+                in1=xs[:, g, :].unsqueeze(1).to_broadcast([P, 256, 4]).rearrange("p r (u e) -> p r u e", e=2),
+                op=ALU.mult,
+            )
 
         def quant_x(m, g):
             h, jp = divmod(m, 2)
@@ -125,10 +125,10 @@ def tile_endpoint_span_scoring_f4_kernel(
             for ss in range(2):
                 turn_words(pbank[e, sp, h], ss, praw[e, sp][:, ss, 512 * h : 512 * (h + 1)].bitcast(F32))
 
-        def copy_p(e, sp, h):
+        def copy_p(e, sp, h, engine=nc.scalar):
             if (e, h) not in pg:
                 pg[e, h] = stage.tile([P, S, 4], BF16, name="pg", align_bytes=64, bufs=4)
-            copy_words(pbank.pop((e, sp, h)), pg[e, h][:, 256 * sp : 256 * (sp + 1), :])
+            copy_words(pbank.pop((e, sp, h)), pg[e, h][:, 256 * sp : 256 * (sp + 1), :], engine)
 
         def quant_p(e, h):
             quant(pcod[e, h][:], psca[e, h][:], pg.pop((e, h))[:].rearrange("p r q -> p (r q)"))
@@ -136,7 +136,7 @@ def tile_endpoint_span_scoring_f4_kernel(
         def weave_w(r, engine):
             i, e = divmod(r, 2)
             c, o = divmod(i * P, WCH)
-            if r >= LEAD + 2 and (r % 2 or r == LEAD + 3):
+            if r % 2 or r == 2:
                 wg[r] = stage.tile([P, 2, P, 4], BF16, name="wgp", align_bytes=64, bufs=1)
             else:
                 wg[r] = stage.tile([P, 2, P, 4], BF16, name="wg", align_bytes=64, bufs=3)
@@ -285,119 +285,115 @@ def tile_endpoint_span_scoring_f4_kernel(
             make_identity(nc, ident[:])
             nc.vector.memset(rows[:], 0.0)
             nc.vector.memset(vmat[:], 0.0)
-            nc.sync.dma_start(out=xs[:], in_=x_scale.rearrange("o (g p t) -> p (o g) t", p=P, t=4))
             load_x(0)
+            nc.sync.dma_start(out=xs[:], in_=x_scale.rearrange("o (g p t) -> p (o g) t", p=P, t=4))
             load_x(1)
             for q, vec in enumerate((bs, be, mix, v)):
                 nc.scalar.dma_start(out=rows[NI * q : NI * (q + 1), :], in_=vec.rearrange("(i f) -> i f", f=P))
             load_w(0, 0)
-            load_p(0, 0)
-            load_w(1, 0)
             load_x(2)
-            load_p(0, 1)
             load_x(3)
+            load_w(1, 0)
+            load_p(0, 0)
+            load_p(0, 1)
+            for e, gv in enumerate((gs, ge)):
+                nc.sync.dma_start(out=sal[e][:], in_=gv.rearrange("(h m j) -> m h j", h=2, j=4))
+            load_w(0, 1)
+            load_w(1, 1)
             load_p(1, 0)
             load_p(1, 1)
-            for c in range(1, F // WCH):
+            for c in range(2, F // WCH):
                 load_w(0, c)
                 load_w(1, c)
             nc.sync.dma_start(out=vrow[:], in_=v[0 : NV * P].partition_broadcast(P))
-            for e, gv in enumerate((gs, ge)):
-                nc.gpsimd.dma_start(out=sal[e][:], in_=gv.rearrange("(h m j) -> m h j", h=2, j=4))
-            nc.gpsimd.dma_start(out=dbias[:], in_=d.partition_broadcast(P))
+            nc.sync.dma_start(out=dbias[:], in_=d.partition_broadcast(P))
 
             def x_turns(m, g, name):
                 for n in (2 * m, 2 * m + 1):
-                    if (n, g) not in xw:
-                        prod_x(n, g)
+                    cast_x(n, g, nc.vector if n == 1 else nc.scalar)
                     turn_x(n, g, name)
 
-            spread_scale(0)
-            spread_scale(1)
-            nc.scalar.copy(out=rows32[:], in_=rows[:])
             x_turns(0, 0, "tp")
-            weave_w(0, nc.scalar)
-            copy_x(0, 0)
-            small = bank_of("te")
-            nc.tensor.transpose(small[:, 0:P], rows32[:], ident[:])
-            nc.scalar.copy(out=cols[:].rearrange("p q i -> p (q i)"), in_=small[:, 0 : 4 * NI])
             x_turns(0, 1, "tp")
-            turn_p(0, 0, 0, "a")
-            weave_w(2, nc.scalar)
-            copy_x(0, 1)
-            x_turns(1, 0, "z")
-            copy_x(1, 0)
-            turn_p(0, 0, 1, "b")
+            weave_w(0, nc.gpsimd)
+            weave_w(2, nc.gpsimd)
+            scale_x(0, 0)
+            x_turns(1, 0, "tp")
+            scale_x(0, 1)
             x_turns(1, 1, "z")
-            copy_x(1, 1)
-            weave_w(1, nc.scalar)
-            turn_p(0, 1, 0, "te")
-            turn_p(0, 1, 1, "tp")
-            quant_x(0, 0)
-            quant_x(0, 1)
-            quant_w(0)
-            quant_x(1, 0)
-            prod_x(4, 0)
-            quant_x(1, 1)
-            prod_x(5, 0)
-            prod_x(4, 1)
-            quant_w(1)
-            copy_p(0, 0, 0)
-            project(0, 0)
-            gelu(0, 0)
+            scale_x(1, 0)
+            scale_x(1, 1)
+            nc.scalar.copy(out=rows32[:], in_=rows[:])
             x_turns(2, 0, "tp")
-            copy_x(2, 0)
-            copy_p(0, 1, 1)
-            project(1, 0)
-            weave_w(3, nc.scalar)
-            x_turns(2, 1, "a")
-            quant_w(2)
-            turn_h(0, 0)
-            project(2, 0)
-            gelu(1, 0)
-            copy_x(2, 1)
+            small = bank_of("a")
+            nc.tensor.transpose(small[:, 0:P], rows32[:], ident[:])
+            x_turns(2, 1, "tp")
+            nc.scalar.copy(out=cols[:].rearrange("p q i -> p (q i)"), in_=small[:, 0 : 4 * NI])
+            turn_p(0, 0, 0, "a")
             x_turns(3, 0, "tp")
-            copy_x(3, 0)
-            x_turns(3, 1, "tp")
-            copy_x(3, 1)
+            turn_p(0, 0, 1, "b")
+            for m in range(2):
+                quant_x(m, 0)
+                quant_x(m, 1)
+            quant_w(0)
+            quant_w(2)
+            weave_w(1, nc.gpsimd)
+            project(0, 0)
+            x_turns(3, 1, "te")
+            copy_p(0, 0, 0)
+            copy_p(0, 0, 1)
+            gelu(0, 0)
+            weave_w(4, nc.scalar)
+            turn_p(0, 1, 0, "a")
+            project(2, 0)
+            turn_p(0, 1, 1, "b")
+            copy_p(0, 1, 0)
             gelu(2, 0)
-            weigh_h(0, 0, (1, 0))
-            quant_w(3)
-            project(3, 0)
-            gelu(3, 0)
-            turn_h(1, 0)
-            turn_p(1, 0, 0, "tp")
+            copy_p(0, 1, 1)
+            weave_w(6, nc.scalar)
+            scale_x(2, 0)
+            scale_x(2, 1)
+            turn_h(0, 0)
+            turn_p(1, 0, 0, "a")
             quant_x(2, 0)
             quant_x(2, 1)
+            quant_w(1)
+            weave_w(3, nc.gpsimd)
+            project(1, 0)
+            gelu(1, 0)
+            turn_h(2, 0)
+            turn_p(1, 1, 0, "b")
+            scale_x(3, 0)
+            scale_x(3, 1)
             quant_x(3, 0)
             quant_x(3, 1)
-            copy_p(0, 0, 1)
-            copy_p(0, 1, 0)
-            weave_w(4, nc.vector)
-            weigh_h(1, 0, (0, 0))
             quant_w(4)
-            quant_h((0, 0), (1, 0))
+            quant_w(3)
+            weave_w(5, nc.gpsimd)
+            weigh_h(0, 0, (2, 0))
+            weigh_h(2, 0, (0, 0))
+            copy_p(1, 0, 0, nc.vector)
+            copy_p(1, 1, 0, nc.vector)
 
             for n in range(NR - LEAD):
-                late, early = n - 1, n - 1 + LEAD
+                late, early = n - 1, n - 1 + LEAD if n else 1
+                before = early - 1 if n != 1 else 1
                 i, odd = divmod(n - LAG, 2)
-                if n and live(n + LEAD):
-                    project(n + LEAD, 0)
-                    gelu(n + LEAD, 0)
-                if live(n):
-                    project(n, 1)
-                    gelu(n, 1)
+                project(n, 1)
+                gelu(n, 1)
+                project(n + LEAD, 0)
+                gelu(n + LEAD, 0)
                 if live(n - LAG):
                     gather(n - LAG)
                 if live(late):
                     turn_h(late, 1)
                 if live(early):
                     turn_h(early, 0)
-                if n == 0:
-                    copy_p(1, 0, 0)
-                for sp, h, name in ([(1, 0, "a"), (0, 1, "b")], [(1, 1, "te")])[n] if n < 2 else []:
-                    turn_p(1, sp, h, name)
-                    copy_p(1, sp, h)
+                if n == 1:
+                    weave_w(n + LEAD + 3, nc.scalar)
+                if n < 2:
+                    turn_p(1, n, 1, "ab"[n])
+                    copy_p(1, n, 1)
                 if odd and i >= 1:
                     turn_emb(i - 1)
                 if live(n - LAG):
@@ -406,20 +402,21 @@ def tile_endpoint_span_scoring_f4_kernel(
                     else:
                         emb_factor(i)
                 if live(late):
-                    weigh_h(late, 1, (early - 1, 0))
+                    weigh_h(late, 1, (before, 0))
                 if odd and live(n - LAG):
                     emb_sum(i)
-                if n < 3:
-                    quant_p(*((0, 0), (0, 1), (1, 1))[n])
+                if n == 0:
+                    weigh_h(early, 0, (late + 1, 1))
+                    quant_h((0, 0), (2, 0))
+                for e, h in ([(0, 0), (0, 1)], [(1, 0)], [(1, 1)])[n] if n < 3 else []:
+                    quant_p(e, h)
                 if live(late):
-                    quant_h((early - 1, 0), (late, 1))
-                if n == 1:
-                    quant_p(1, 0)
+                    quant_h((before, 0), (late, 1))
                 if not odd and i >= 2:
                     copy_emb(i - 2)
                 if live(n + LEAD + 2):
-                    if n in (0, 2) or (odd and n > 1):
-                        weave_w(n + LEAD + 2, nc.scalar if n else nc.vector)
+                    if odd and n > 1:
+                        weave_w(n + LEAD + 2, nc.scalar)
                     quant_w(n + LEAD + 2)
                 if n == 4:
                     nc.scalar.copy(out=vmat[0:64, :, 0], in_=cols[0:64, 3, :])
@@ -428,10 +425,10 @@ def tile_endpoint_span_scoring_f4_kernel(
                     label_sums(i - 3)
                 if odd and i >= 2:
                     weigh_emb(i - 2, nc.gpsimd if i >= 3 else nc.vector)
-                if live(early):
+                if n:
                     weigh_h(early, 0, (late + 1, 1))
-                if not odd and live(n + LEAD + 4):
-                    weave_w(n + LEAD + (4 if n else 3), nc.gpsimd)
+                if n and not odd and live(n + LEAD + 4):
+                    weave_w(n + LEAD + 4, nc.gpsimd)
 
             last = NR - 1
             label_sums(NV - 3)

@@ -37,7 +37,7 @@ def tile_endpoint_span_scoring_f4_kernel(
 
         ident = keep.tile([P, P], F32, name="ident")
 
-        xb = [keep.tile([P, 2, D], U8, name=f"xb{n}", align_bytes=64) for n in range(4)]
+        xb = {(m, g): keep.tile([P, 2, 512], U8, name=f"xb{m}{g}", align_bytes=64) for m in range(4) for g in range(2)}
         xs = keep.tile([P, 2, 4], F32, name="xs")
         xcod = {(h, g): keep.tile([P, 512], U32, name=f"xcod{h}{g}", align_bytes=64) for h in range(2) for g in range(2)}
         xsca = {(h, g): keep.tile([P, 512], U8, name=f"xsca{h}{g}", align_bytes=64) for h in range(2) for g in range(2)}
@@ -61,9 +61,9 @@ def tile_endpoint_span_scoring_f4_kernel(
         wv = [w.rearrange("(g p j) f -> g p j f", g=2, p=P, j=4) for w in (ws, we)]
         pv = [q.rearrange("(r st) t -> r st t", st=4) for q in (ps, pe)]
 
-        def load_x(n):
-            h, jp = divmod(n, 2)
-            nc.sync.dma_start(out=xb[n][:], in_=xv[h][:, 2 * jp : 2 * jp + 2, :])
+        def load_x(m, g):
+            h, jp = divmod(m, 2)
+            nc.sync.dma_start(out=xb[m, g][:], in_=xv[h][:, 2 * jp : 2 * jp + 2, 512 * g : 512 * (g + 1)])
 
         def load_w(e, c):
             for g in range(2):
@@ -80,7 +80,7 @@ def tile_endpoint_span_scoring_f4_kernel(
 
         def cast_x(n, g, engine):
             xw[n, g] = stage.tile([P, 512], BF16, name="xw", bufs=6)
-            src = xb[n // 2][:, n % 2, 512 * g : 512 * (g + 1)].bitcast(FP8)
+            src = xb[n // 2, g][:, n % 2, :].bitcast(FP8)
             if engine is nc.vector:
                 nc.vector.tensor_copy(out=xw[n, g][:], in_=src)
             else:
@@ -136,8 +136,8 @@ def tile_endpoint_span_scoring_f4_kernel(
         def weave_w(r, engine):
             i, e = divmod(r, 2)
             c, o = divmod(i * P, WCH)
-            if r % 2 or r == 2:
-                wg[r] = stage.tile([P, 2, P, 4], BF16, name="wgp", align_bytes=64, bufs=1)
+            if r % 2 or r in (2, 6):
+                wg[r] = stage.tile([P, 2, P, 4], BF16, name="wgp" if r < 6 else "wgq", align_bytes=64, bufs=1)
             else:
                 wg[r] = stage.tile([P, 2, P, 4], BF16, name="wg", align_bytes=64, bufs=3)
             src = wraw[e, c][:, :, :, o : o + P].rearrange("p g t f -> p g f t")
@@ -285,22 +285,26 @@ def tile_endpoint_span_scoring_f4_kernel(
             make_identity(nc, ident[:])
             nc.vector.memset(rows[:], 0.0)
             nc.vector.memset(vmat[:], 0.0)
-            load_x(0)
+            load_x(0, 0)
+            load_x(0, 1)
             nc.sync.dma_start(out=xs[:], in_=x_scale.rearrange("o (g p t) -> p (o g) t", p=P, t=4))
-            load_x(1)
-            for q, vec in enumerate((bs, be, mix, v)):
-                nc.scalar.dma_start(out=rows[NI * q : NI * (q + 1), :], in_=vec.rearrange("(i f) -> i f", f=P))
+            load_x(1, 0)
+            load_x(1, 1)
             load_w(0, 0)
-            load_x(2)
-            load_x(3)
-            load_w(1, 0)
+            load_x(2, 0)
+            load_x(2, 1)
             load_p(0, 0)
+            load_x(3, 0)
+            load_x(3, 1)
+            for q, vec in enumerate((bs, be, mix, v)):
+                nc.sync.dma_start(out=rows[NI * q : NI * (q + 1), :], in_=vec.rearrange("(i f) -> i f", f=P))
             load_p(0, 1)
+            load_w(1, 0)
+            load_w(0, 1)
             for e, gv in enumerate((gs, ge)):
                 nc.sync.dma_start(out=sal[e][:], in_=gv.rearrange("(h m j) -> m h j", h=2, j=4))
-            load_w(0, 1)
-            load_w(1, 1)
             load_p(1, 0)
+            load_w(1, 1)
             load_p(1, 1)
             for c in range(2, F // WCH):
                 load_w(0, c)
@@ -323,15 +327,17 @@ def tile_endpoint_span_scoring_f4_kernel(
             x_turns(1, 1, "z")
             scale_x(1, 0)
             scale_x(1, 1)
-            nc.scalar.copy(out=rows32[:], in_=rows[:])
+            turn_p(0, 0, 0, "a")
             x_turns(2, 0, "tp")
-            small = bank_of("a")
+            nc.scalar.copy(out=rows32[:], in_=rows[:])
+            turn_p(0, 0, 1, "b")
+            small = bank_of("te")
             nc.tensor.transpose(small[:, 0:P], rows32[:], ident[:])
             x_turns(2, 1, "tp")
             nc.scalar.copy(out=cols[:].rearrange("p q i -> p (q i)"), in_=small[:, 0 : 4 * NI])
-            turn_p(0, 0, 0, "a")
+            turn_p(0, 1, 1, "z")
             x_turns(3, 0, "tp")
-            turn_p(0, 0, 1, "b")
+            turn_p(0, 1, 0, "te")
             for m in range(2):
                 quant_x(m, 0)
                 quant_x(m, 1)
@@ -339,22 +345,20 @@ def tile_endpoint_span_scoring_f4_kernel(
             quant_w(2)
             weave_w(1, nc.gpsimd)
             project(0, 0)
-            x_turns(3, 1, "te")
-            copy_p(0, 0, 0)
-            copy_p(0, 0, 1)
-            gelu(0, 0)
-            weave_w(4, nc.scalar)
-            turn_p(0, 1, 0, "a")
-            project(2, 0)
-            turn_p(0, 1, 1, "b")
-            copy_p(0, 1, 0)
-            gelu(2, 0)
-            copy_p(0, 1, 1)
-            weave_w(6, nc.scalar)
             scale_x(2, 0)
+            x_turns(3, 1, "tp")
+            copy_p(0, 1, 1)
+            copy_p(0, 0, 0)
+            gelu(0, 0)
+            project(2, 0)
+            copy_p(0, 0, 1)
+            weave_w(4, nc.scalar)
+            gelu(2, 0)
+            copy_p(0, 1, 0)
             scale_x(2, 1)
-            turn_h(0, 0)
             turn_p(1, 0, 0, "a")
+            turn_h(0, 0)
+            turn_p(1, 0, 1, "b")
             quant_x(2, 0)
             quant_x(2, 1)
             quant_w(1)
@@ -362,7 +366,6 @@ def tile_endpoint_span_scoring_f4_kernel(
             project(1, 0)
             gelu(1, 0)
             turn_h(2, 0)
-            turn_p(1, 1, 0, "b")
             scale_x(3, 0)
             scale_x(3, 1)
             quant_x(3, 0)
@@ -372,8 +375,6 @@ def tile_endpoint_span_scoring_f4_kernel(
             weave_w(5, nc.gpsimd)
             weigh_h(0, 0, (2, 0))
             weigh_h(2, 0, (0, 0))
-            copy_p(1, 0, 0, nc.vector)
-            copy_p(1, 1, 0, nc.vector)
 
             for n in range(NR - LEAD):
                 late, early = n - 1, n - 1 + LEAD if n else 1
@@ -389,11 +390,15 @@ def tile_endpoint_span_scoring_f4_kernel(
                     turn_h(late, 1)
                 if live(early):
                     turn_h(early, 0)
-                if n == 1:
+                if n == 0:
+                    turn_p(1, 1, 0, "te")
+                    copy_p(1, 0, 0)
                     weave_w(n + LEAD + 3, nc.scalar)
-                if n < 2:
-                    turn_p(1, n, 1, "ab"[n])
-                    copy_p(1, n, 1)
+                    copy_p(1, 1, 0)
+                if n == 1:
+                    turn_p(1, 1, 1, "a")
+                    copy_p(1, 1, 1)
+                    copy_p(1, 0, 1)
                 if odd and i >= 1:
                     turn_emb(i - 1)
                 if live(n - LAG):
@@ -415,7 +420,7 @@ def tile_endpoint_span_scoring_f4_kernel(
                 if not odd and i >= 2:
                     copy_emb(i - 2)
                 if live(n + LEAD + 2):
-                    if odd and n > 1:
+                    if n > 1 and odd:
                         weave_w(n + LEAD + 2, nc.scalar)
                     quant_w(n + LEAD + 2)
                 if n == 4:
@@ -427,6 +432,8 @@ def tile_endpoint_span_scoring_f4_kernel(
                     weigh_emb(i - 2, nc.gpsimd if i >= 3 else nc.vector)
                 if n:
                     weigh_h(early, 0, (late + 1, 1))
+                if n == 1:
+                    weave_w(n + LEAD + 3, nc.gpsimd)
                 if n and not odd and live(n + LEAD + 4):
                     weave_w(n + LEAD + 4, nc.gpsimd)
 

@@ -19,9 +19,7 @@ P = 128
 NI = F // P
 NR = 2 * NI
 WCH = 256
-LEAD = 3
-NV = 5
-LAG = 2
+NV = 7
 
 
 def tile_endpoint_span_scoring_f4_kernel(
@@ -31,13 +29,12 @@ def tile_endpoint_span_scoring_f4_kernel(
     with ExitStack() as ctx:
         keep = ctx.enter_context(tc.tile_pool(name="keep", bufs=1))
         stage = ctx.enter_context(tc.tile_pool(name="stage", bufs=3))
-        twin = ctx.enter_context(tc.psum_pool(name="twin", bufs=2))
-        lone = ctx.enter_context(tc.psum_pool(name="lone", bufs=1))
-        trio = ctx.enter_context(tc.psum_pool(name="trio", bufs=3))
+        psum = ctx.enter_context(tc.psum_pool(name="psum", bufs=1))
 
         ident = keep.tile([P, P], F32, name="ident")
 
-        xb = {(m, g): keep.tile([P, 2, 512], U8, name=f"xb{m}{g}", align_bytes=64) for m in range(4) for g in range(2)}
+        xb = {(m, g): keep.tile([P, 2, 512], U8, name=f"xb{m}{g}", align_bytes=64) for m in range(2) for g in range(2)}
+        xc = {m: keep.tile([P, 2, D], U8, name=f"xc{m}", align_bytes=64) for m in range(2, 4)}
         xs = keep.tile([P, 2, 4], F32, name="xs")
         xcod = {(h, g): keep.tile([P, 512], U32, name=f"xcod{h}{g}", align_bytes=64) for h in range(2) for g in range(2)}
         xsca = {(h, g): keep.tile([P, 512], U8, name=f"xsca{h}{g}", align_bytes=64) for h in range(2) for g in range(2)}
@@ -53,7 +50,7 @@ def tile_endpoint_span_scoring_f4_kernel(
         cols = keep.tile([P, 4, NI], F32, name="cols")
         sums = keep.tile([P, 4, C], F32, name="sums")
         vrow = keep.tile([P, NV * P], BF16, name="vrow")
-        vmat = keep.tile([P, NI, 2], F32, name="vmat")
+        vmat = keep.tile([P, 2], F32, name="vmat")
         dbias = keep.tile([P, C], BF16, name="dbias")
         score = keep.tile([P, 4, C], F32, name="score")
 
@@ -62,8 +59,10 @@ def tile_endpoint_span_scoring_f4_kernel(
         pv = [q.rearrange("(r st) t -> r st t", st=4) for q in (ps, pe)]
 
         def load_x(m, g):
-            h, jp = divmod(m, 2)
-            nc.sync.dma_start(out=xb[m, g][:], in_=xv[h][:, 2 * jp : 2 * jp + 2, 512 * g : 512 * (g + 1)])
+            nc.sync.dma_start(out=xb[m, g][:], in_=xv[0][:, 2 * m : 2 * m + 2, 512 * g : 512 * (g + 1)])
+
+        def load_x_rows(m):
+            nc.sync.dma_start(out=xc[m][:], in_=xv[1][:, 2 * m - 4 : 2 * m - 2, :])
 
         def load_w(e, c):
             for g in range(2):
@@ -72,141 +71,153 @@ def tile_endpoint_span_scoring_f4_kernel(
         def load_p(e, sp):
             nc.sync.dma_start(out=praw[e, sp][:], in_=pv[e][:, 2 * sp : 2 * sp + 2, :])
 
-        def bank_of(name):
-            return {"z": twin, "tp": trio}.get(name, lone).tile([P, 512], F32, name=name)
+        def bank_of(b):
+            return psum.tile([P, 512], F32, name=f"bank{b}")
 
         xw, xbank, xg, pbank, pg = {}, {}, {}, {}, {}
-        wg, wq, z, gl, tph, hg, hq, ab, tv, uv, ev, tpe, eo, vv = ({} for n in range(14))
+        wg, wq, z, gl, tph, hg, hq, ab, tv, uv, av, ev, tpe, eo, vv = ({} for n in range(15))
 
         def cast_x(n, g, engine):
-            xw[n, g] = stage.tile([P, 512], BF16, name="xw", bufs=6)
-            src = xb[n // 2, g][:, n % 2, :].bitcast(FP8)
+            xw[n, g] = stage.tile([P, 512], BF16, name="xw", bufs=8)
+            raw = xb[n // 2, g][:, n % 2, :] if n < 4 else xc[n // 2][:, n % 2, 512 * g : 512 * (g + 1)]
             if engine is nc.vector:
-                nc.vector.tensor_copy(out=xw[n, g][:], in_=src)
+                nc.vector.tensor_copy(out=xw[n, g][:], in_=raw.bitcast(FP8))
             else:
-                nc.scalar.copy(out=xw[n, g][:], in_=src)
+                nc.scalar.copy(out=xw[n, g][:], in_=raw.bitcast(FP8))
 
         def turn_words(bank, half, words):
             for u in range(2):
                 o = 256 * u + P * half
                 nc.tensor.transpose(bank[:, o : o + P], words[:, u:256:2], ident[:])
 
-        def copy_words(bank, dst, engine):
-            move = nc.vector.tensor_copy if engine is nc.vector else nc.scalar.copy
-            move(
-                out=dst.rearrange("p r q -> p (r q)").bitcast(F32).rearrange("p (r u) -> p r u", u=2),
-                in_=bank[:].rearrange("p (u r) -> p r u", u=2),
-            )
-
         def quant(cod, sca, src):
             nc.vector.quantize_mx(out=cod.bitcast(FP8X4), scales=sca, in_=src)
 
-        def turn_x(n, g, name):
-            if n % 2 == 0:
-                xbank[n // 2, g] = bank_of(name)
-            turn_words(xbank[n // 2, g], n % 2, xw.pop((n, g))[:].bitcast(F32))
+        def turn_x(m, g, b):
+            xbank[m, g] = bank_of(b)
+            for half in range(2):
+                turn_words(xbank[m, g], half, xw.pop((2 * m + half, g))[:].bitcast(F32))
 
         def scale_x(m, g):
-            xg[m, g] = stage.tile([P, 256, 4], BF16, name="xg", align_bytes=64, bufs=6)
+            h, jp = divmod(m, 2)
+            if jp == 0:
+                xg[h, g] = stage.tile([P, 512, 4], BF16, name=f"xg{h}{g}", align_bytes=64, bufs=1)
             nc.vector.tensor_tensor(
-                out=xg[m, g][:].rearrange("p r (u e) -> p r u e", e=2),
+                out=xg[h, g][:, 256 * jp : 256 * (jp + 1), :].rearrange("p r (u e) -> p r u e", e=2),
                 in0=xbank.pop((m, g))[:].bitcast(BF16).rearrange("p (u r e) -> p r u e", u=2, e=2),
                 in1=xs[:, g, :].unsqueeze(1).to_broadcast([P, 256, 4]).rearrange("p r (u e) -> p r u e", e=2),
                 op=ALU.mult,
             )
 
-        def quant_x(m, g):
-            h, jp = divmod(m, 2)
-            span = slice(256 * jp, 256 * (jp + 1))
-            quant(xcod[h, g][:, span], xsca[h, g][:, span], xg.pop((m, g))[:].rearrange("p r q -> p (r q)"))
+        def quant_x(h, g):
+            quant(xcod[h, g][:], xsca[h, g][:], xg.pop((h, g))[:].rearrange("p r q -> p (r q)"))
 
-        def turn_p(e, sp, h, name):
-            pbank[e, sp, h] = bank_of(name)
+        def turn_p(e, sp, h, b):
+            pbank[e, sp, h] = bank_of(b)
             for ss in range(2):
                 turn_words(pbank[e, sp, h], ss, praw[e, sp][:, ss, 512 * h : 512 * (h + 1)].bitcast(F32))
 
-        def copy_p(e, sp, h, engine=nc.scalar):
+        def copy_p(e, sp, h):
             if (e, h) not in pg:
                 pg[e, h] = stage.tile([P, S, 4], BF16, name="pg", align_bytes=64, bufs=4)
-            copy_words(pbank.pop((e, sp, h)), pg[e, h][:, 256 * sp : 256 * (sp + 1), :], engine)
+            dst = pg[e, h][:, 256 * sp : 256 * (sp + 1), :]
+            nc.scalar.copy(
+                out=dst.rearrange("p r q -> p (r q)").bitcast(F32).rearrange("p (r u) -> p r u", u=2),
+                in_=pbank.pop((e, sp, h))[:].rearrange("p (u r) -> p r u", u=2),
+            )
 
         def quant_p(e, h):
             quant(pcod[e, h][:], psca[e, h][:], pg.pop((e, h))[:].rearrange("p r q -> p (r q)"))
 
-        def weave_w(r, engine):
+        def weave_w(e, c):
+            wg[e, c] = stage.tile([P, 2, WCH, 4], BF16, name=("wg", "wh")[e], align_bytes=64, bufs=1)
+            src = wraw[e, c][:].rearrange("p g t f -> p g f t")
+            nc.gpsimd.tensor_scalar(out=wg[e, c][:], in0=src, scalar1=1.0, scalar2=0.0, op0=ALU.mult, op1=ALU.add)
+
+        def quant_w(e, c):
+            cod = stage.tile([P, 2, WCH], U32, name="wcod", align_bytes=64, bufs=4)
+            sca = stage.tile([P, 2, WCH], U8, name="wsca", align_bytes=64, bufs=4)
+            flat = "p g f -> p (g f)"
+            quant(cod[:].rearrange(flat), sca[:].rearrange(flat), wg.pop((e, c))[:].rearrange("p g f q -> p (g f q)"))
+            for o in range(2):
+                wq[4 * c + 2 * o + e] = (cod[:, :, P * o : P * (o + 1)], sca[:, :, P * o : P * (o + 1)])
+
+        def w_tile(width, name="wg"):
+            return stage.tile([P, width, 2, P, 4], BF16, name=name, align_bytes=64, bufs=1)
+
+        def weave(r, engine, tile, slot):
             i, e = divmod(r, 2)
             c, o = divmod(i * P, WCH)
-            if r % 2 or r in (2, 6):
-                wg[r] = stage.tile([P, 2, P, 4], BF16, name="wgp" if r < 6 else "wgq", align_bytes=64, bufs=1)
-            else:
-                wg[r] = stage.tile([P, 2, P, 4], BF16, name="wg", align_bytes=64, bufs=3)
+            wg[r] = (tile, slot)
             src = wraw[e, c][:, :, :, o : o + P].rearrange("p g t f -> p g f t")
-            if engine is nc.vector:
-                nc.vector.tensor_copy(out=wg[r][:], in_=src)
-            elif engine is nc.scalar:
-                nc.scalar.copy(out=wg[r][:], in_=src)
+            if engine is nc.scalar:
+                nc.scalar.copy(out=tile[:, slot], in_=src)
             else:
-                nc.gpsimd.tensor_scalar(out=wg[r][:], in0=src, scalar1=1.0, scalar2=0.0, op0=ALU.mult, op1=ALU.add)
+                nc.gpsimd.tensor_scalar(out=tile[:, slot], in0=src, scalar1=1.0, scalar2=0.0, op0=ALU.mult, op1=ALU.add)
 
-        def quant_w(r):
-            cod = stage.tile([P, 2 * P], U32, name="wcod", align_bytes=64, bufs=LEAD + 4)
-            sca = stage.tile([P, 2 * P], U8, name="wsca", align_bytes=64, bufs=LEAD + 4)
-            quant(cod[:], sca[:], wg.pop(r)[:].rearrange("p g f q -> p (g f q)"))
-            wq[r] = (cod, sca)
+        def quant_rounds(*rounds):
+            width = len(rounds)
+            cod = stage.tile([P, width, 2, P], U32, name="wcod", align_bytes=64, bufs=4)
+            sca = stage.tile([P, width, 2, P], U8, name="wsca", align_bytes=64, bufs=4)
+            flat = "p e g f -> p (e g f)"
+            quant(cod[:].rearrange(flat), sca[:].rearrange(flat), wg[rounds[0]][0][:].rearrange("p e g f q -> p (e g f q)"))
+            for r in rounds:
+                slot = wg.pop(r)[1]
+                wq[r] = (cod[:, slot], sca[:, slot])
 
-        def project(r, h):
+        def project(unit, b):
+            r, h = unit
             cod, sca = wq[r]
-            z[r, h] = twin.tile([P, 512], F32, name="z")
+            z[unit] = bank_of(b)
             for g in range(2):
                 nc.tensor.matmul_mx(
-                    out=z[r, h][:],
-                    lhsT=cod[:, P * g : P * (g + 1)].bitcast(FP8X4),
-                    lhsT_scale=sca[:, P * g : P * (g + 1)],
+                    out=z[unit][:],
+                    lhsT=cod[:, g, :].bitcast(FP8X4),
+                    lhsT_scale=sca[:, g, :],
                     rhs=xcod[h, g][:].bitcast(FP8X4),
                     rhs_scale=xsca[h, g][:],
                     start=(g == 0),
                     stop=(g == 1),
                 )
 
-        def gelu(r, h):
-            i, e = divmod(r, 2)
-            gl[r, h] = stage.tile([P, 512], F32, name="gl", bufs=LEAD + 4)
+        def gelu(unit):
+            i, e = divmod(unit[0], 2)
+            gl[unit] = stage.tile([P, 512], F32, name="gl", bufs=8)
             nc.scalar.activation(
-                out=gl[r, h][:], in_=z.pop((r, h))[:], func=ACT.Gelu_apprx_tanh, bias=cols[:, e, i : i + 1]
+                out=gl[unit][:], in_=z.pop(unit)[:], func=ACT.Gelu_apprx_tanh, bias=cols[:, e, i : i + 1]
             )
 
-        def turn_h(r, h, name="tp"):
-            tph[r, h] = bank_of(name)
-            src = gl.pop((r, h))
+        def turn_h(unit, b):
+            tph[unit] = bank_of(b)
+            src = gl.pop(unit)
             for j in range(4):
-                nc.tensor.transpose(tph[r, h][:, P * j : P * (j + 1)], src[:, P * j : P * (j + 1)], ident[:])
+                nc.tensor.transpose(tph[unit][:, P * j : P * (j + 1)], src[:, P * j : P * (j + 1)], ident[:])
 
-        def weigh_h(r, h, mate=None):
-            if mate in hg:
-                hg[r, h] = (hg[mate][0], 1)
-            else:
-                width = 1 if mate is None else 2
-                hg[r, h] = (stage.tile([P, width, P, 4], BF16, name="hg", align_bytes=64, bufs=4), 0)
-            tile, slot = hg[r, h]
+        def weigh_h(unit, tile, slot):
+            r, h = unit
+            hg[unit] = (tile, slot)
             nc.vector.tensor_tensor(
                 out=tile[:, slot],
-                in0=tph.pop((r, h))[:].rearrange("p (j f) -> p f j", j=4),
+                in0=tph.pop(unit)[:].rearrange("p (j f) -> p f j", j=4),
                 in1=sal[r % 2][:, h, :].unsqueeze(1).to_broadcast([P, P, 4]),
                 op=ALU.mult,
             )
 
+        def h_tile(width, name="hg", bufs=3):
+            return stage.tile([P, width, P, 4], BF16, name=name, align_bytes=64, bufs=bufs)
+
         def quant_h(*units):
             width = P * len(units)
-            cod = stage.tile([P, width], U32, name="hcod", align_bytes=64, bufs=LEAD + 6)
-            sca = stage.tile([P, width], U8, name="hsca", align_bytes=64, bufs=LEAD + 6)
+            cod = stage.tile([P, width], U32, name="hcod", align_bytes=64, bufs=5)
+            sca = stage.tile([P, width], U8, name="hsca", align_bytes=64, bufs=5)
             quant(cod[:], sca[:], hg[units[0]][0][:].rearrange("p s f q -> p (s f q)"))
             for unit in units:
                 slot = hg.pop(unit)[1]
                 hq[unit] = (cod[:, P * slot : P * (slot + 1)], sca[:, P * slot : P * (slot + 1)])
 
-        def gather(r, name=None):
+        def gather(r, b):
             e = r % 2
-            ab[r] = bank_of(name or "ab"[e])
+            ab[r] = bank_of(b)
             for h in range(2):
                 cod, sca = hq.pop((r, h))
                 nc.tensor.matmul_mx(
@@ -226,27 +237,50 @@ def tile_endpoint_span_scoring_f4_kernel(
             )
 
         def emb_product(i):
-            uv[i] = stage.tile([P, S], F32, name="uv", bufs=2)
+            uv[i] = stage.tile([P, S], F32, name="uv", bufs=3)
             nc.vector.tensor_tensor(out=uv[i][:], in0=ab.pop(2 * i + 1)[:], in1=tv.pop(i)[:], op=ALU.mult)
 
         def emb_sum(i):
-            ev[i] = stage.tile([P, S], F32, name="ev", bufs=4)
+            ev[i] = stage.tile([P, S], F32, name="ev", bufs=2)
             nc.vector.tensor_tensor(out=ev[i][:], in0=ab.pop(2 * i)[:], in1=uv.pop(i)[:], op=ALU.add)
 
-        def turn_emb(i, name="te"):
-            tpe[i] = bank_of(name)
+        def copy_a(i):
+            av[i] = stage.tile([P, S], F32, name="av", bufs=2)
+            nc.scalar.copy(out=av[i][:], in_=ab.pop(2 * i)[:])
+
+        def turn_emb(i, b):
+            tpe[i] = bank_of(b)
+            src = ev.pop(i)
             for st in range(4):
-                nc.tensor.transpose(tpe[i][:, P * st : P * (st + 1)], ev[i][:, P * st : P * (st + 1)], ident[:])
+                nc.tensor.transpose(tpe[i][:, P * st : P * (st + 1)], src[:, P * st : P * (st + 1)], ident[:])
+
+        def turn_term(i, term, first):
+            for st in range(4):
+                nc.tensor.matmul(
+                    out=tpe[i][:, P * st : P * (st + 1)],
+                    lhsT=term[:, P * st : P * (st + 1)],
+                    rhs=ident[:],
+                    is_transpose=True,
+                    start=first and st == 0,
+                    stop=not first and st == 3,
+                )
 
         def copy_emb(i):
-            eo[i] = stage.tile([P, 4, P], F32, name="eo", bufs=4)
-            nc.scalar.copy(out=eo[i][:].rearrange("p st f -> p (st f)"), in_=tpe.pop(i)[:])
+            eo[i] = stage.tile([P, 4, P], F32, name="eo", bufs=6)
+            nc.scalar.copy(out=eo[i][:].rearrange("p st f -> p (st f)"), in_=tpe[i][:])
             nc.sync.dma_start(out=out_0.rearrange("(r st) f -> r st f", st=4)[:, :, P * i : P * (i + 1)], in_=eo[i][:])
 
-        def weigh_emb(i, engine, name="vv"):
-            vv[i] = stage.tile([P, 4, P], F32, name=name, bufs=1)
+        def weigh_emb(i, name="vv", bufs=3):
+            vv[i] = stage.tile([P, 4, P], F32, name=name, align_bytes=64, bufs=bufs)
             row = vrow[:, P * i : P * (i + 1)].unsqueeze(1).to_broadcast([P, 4, P])
-            engine.tensor_tensor(out=vv[i][:], in0=eo[i][:], in1=row, op=ALU.mult)
+            nc.gpsimd.tensor_tensor(out=vv[i][:], in0=eo[i][:], in1=row, op=ALU.mult)
+
+        def weigh_bank(i):
+            vv[i] = stage.tile([P, 4, P], F32, name="vv", align_bytes=64, bufs=3)
+            row = vrow[:, P * i : P * (i + 1)].unsqueeze(1).to_broadcast([P, 4, P])
+            nc.vector.tensor_tensor(
+                out=vv[i][:], in0=tpe[i][:].rearrange("p (st f) -> p st f", st=4), in1=row, op=ALU.mult
+            )
 
         def label_sums(i):
             nc.vector.tensor_reduce(
@@ -256,17 +290,15 @@ def tile_endpoint_span_scoring_f4_kernel(
                 axis=mybir.AxisListType.X,
             )
 
-        def label_matmuls(i):
-            if i == NV:
-                vv["bank"] = bank_of("tp")
+        def label_matmuls(i, term, first=False, last=False):
             for st in range(4):
                 o = C * st + 2 * i
                 nc.tensor.matmul(
                     out=vv["bank"][:, o : o + 2],
-                    lhsT=ev[i][:, P * st : P * (st + 1)],
-                    rhs=vmat[:, i, :],
-                    start=True,
-                    stop=True,
+                    lhsT=term[:, P * st : P * (st + 1)],
+                    rhs=vmat[:],
+                    start=first and st == 0,
+                    stop=last and st == 3,
                 )
 
         def add_offsets(src, labels):
@@ -278,214 +310,199 @@ def tile_endpoint_span_scoring_f4_kernel(
                 op=ALU.add,
             )
 
-        def live(r):
-            return 0 <= r < NR
-
         with tc.manual_schedule():
             make_identity(nc, ident[:])
             nc.vector.memset(rows[:], 0.0)
             nc.vector.memset(vmat[:], 0.0)
             load_x(0, 0)
-            load_x(0, 1)
-            nc.sync.dma_start(out=xs[:], in_=x_scale.rearrange("o (g p t) -> p (o g) t", p=P, t=4))
             load_x(1, 0)
+            nc.sync.dma_start(out=xs[:], in_=x_scale.rearrange("o (g p t) -> p (o g) t", p=P, t=4))
+            load_x(0, 1)
             load_x(1, 1)
             load_w(0, 0)
-            load_x(2, 0)
-            load_x(2, 1)
+            load_x_rows(2)
+            load_x_rows(3)
+            load_w(1, 0)
             load_p(0, 0)
-            load_x(3, 0)
-            load_x(3, 1)
             for q, vec in enumerate((bs, be, mix, v)):
                 nc.sync.dma_start(out=rows[NI * q : NI * (q + 1), :], in_=vec.rearrange("(i f) -> i f", f=P))
             load_p(0, 1)
-            load_w(1, 0)
-            load_w(0, 1)
+            load_p(1, 0)
+            load_p(1, 1)
             for e, gv in enumerate((gs, ge)):
                 nc.sync.dma_start(out=sal[e][:], in_=gv.rearrange("(h m j) -> m h j", h=2, j=4))
-            load_p(1, 0)
+            load_w(0, 1)
             load_w(1, 1)
-            load_p(1, 1)
             for c in range(2, F // WCH):
                 load_w(0, c)
                 load_w(1, c)
             nc.sync.dma_start(out=vrow[:], in_=v[0 : NV * P].partition_broadcast(P))
             nc.sync.dma_start(out=dbias[:], in_=d.partition_broadcast(P))
 
-            def x_turns(m, g, name):
-                for n in (2 * m, 2 * m + 1):
-                    cast_x(n, g, nc.vector if n == 1 else nc.scalar)
-                    turn_x(n, g, name)
-
-            x_turns(0, 0, "tp")
-            x_turns(0, 1, "tp")
-            weave_w(0, nc.gpsimd)
-            weave_w(2, nc.gpsimd)
-            scale_x(0, 0)
-            x_turns(1, 0, "tp")
-            scale_x(0, 1)
-            x_turns(1, 1, "z")
-            scale_x(1, 0)
-            scale_x(1, 1)
-            turn_p(0, 0, 0, "a")
-            x_turns(2, 0, "tp")
+            pieces = [(0, 0), (1, 0), (0, 1), (1, 1), (2, 0), (3, 0), (2, 1), (3, 1)]
+            for n, (m, g) in enumerate(pieces):
+                cast_x(2 * m, g, nc.scalar)
+                cast_x(2 * m + 1, g, nc.vector if n < 2 else nc.scalar)
+                turn_x(m, g, n % 4)
+                if n == 3:
+                    weave_w(0, 0)
+                    weave_w(1, 0)
+                if n >= 1:
+                    scale_x(*pieces[n - 1])
             nc.scalar.copy(out=rows32[:], in_=rows[:])
-            turn_p(0, 0, 1, "b")
-            small = bank_of("te")
+            scale_x(*pieces[-1])
+            turn_p(0, 0, 0, 4)
+            small = bank_of(0)
             nc.tensor.transpose(small[:, 0:P], rows32[:], ident[:])
-            x_turns(2, 1, "tp")
-            nc.scalar.copy(out=cols[:].rearrange("p q i -> p (q i)"), in_=small[:, 0 : 4 * NI])
-            turn_p(0, 1, 1, "z")
-            x_turns(3, 0, "tp")
-            turn_p(0, 1, 0, "te")
-            for m in range(2):
-                quant_x(m, 0)
-                quant_x(m, 1)
-            quant_w(0)
-            quant_w(2)
-            weave_w(1, nc.gpsimd)
-            project(0, 0)
-            scale_x(2, 0)
-            x_turns(3, 1, "tp")
-            copy_p(0, 1, 1)
+            for n in range(1, 4):
+                turn_p(0, n // 2, n % 2, 4 + n)
+            turn_p(1, 0, 0, 1)
             copy_p(0, 0, 0)
-            gelu(0, 0)
-            project(2, 0)
-            copy_p(0, 0, 1)
-            weave_w(4, nc.scalar)
-            gelu(2, 0)
-            copy_p(0, 1, 0)
-            scale_x(2, 1)
-            turn_p(1, 0, 0, "a")
-            turn_h(0, 0)
-            turn_p(1, 0, 1, "b")
-            quant_x(2, 0)
-            quant_x(2, 1)
-            quant_w(1)
-            weave_w(3, nc.gpsimd)
-            project(1, 0)
-            gelu(1, 0)
-            turn_h(2, 0)
-            scale_x(3, 0)
-            scale_x(3, 1)
-            quant_x(3, 0)
-            quant_x(3, 1)
-            quant_w(4)
-            quant_w(3)
-            weave_w(5, nc.gpsimd)
-            weigh_h(0, 0, (2, 0))
-            weigh_h(2, 0, (0, 0))
+            nc.scalar.copy(out=cols[:].rearrange("p q i -> p (q i)"), in_=small[:, 0 : 4 * NI])
+            for n in range(1, 4):
+                copy_p(0, n // 2, n % 2)
+            quant_x(0, 0)
+            quant_w(0, 0)
+            quant_x(0, 1)
+            quant_x(1, 0)
+            quant_x(1, 1)
+            quant_w(1, 0)
+            quant_p(0, 0)
+            quant_p(0, 1)
+            pair = w_tile(2, "wh")
+            weave(4, nc.gpsimd, pair, 0)
+            weave(5, nc.gpsimd, pair, 1)
+            first = [(0, 0), (2, 0), (0, 1), (2, 1), (1, 0), (1, 1)]
+            for unit, b in zip(first, (2, 3, 0, 4, 5, 6)):
+                project(unit, b)
+                gelu(unit)
+            tiles = [h_tile(2), h_tile(4)]
+            slots = [(0, 0), (1, 0), (0, 1), (1, 1), (1, 2), (1, 3)]
+            turn_h(first[0], 7)
+            turn_h(first[1], 2)
+            turn_p(1, 0, 1, 3)
+            turn_h(first[2], 0)
+            turn_h(first[3], 4)
+            for n in range(4):
+                weigh_h(first[n], tiles[slots[n][0]], slots[n][1])
+            weave(6, nc.scalar, w_tile(1, "wg"), 0)
+            units = [(r, h) for r in (3, 4) for h in range(2)]
+            for unit, b in zip(units[:2], (5, 6)):
+                project(unit, b)
+                gelu(unit)
+            copy_p(1, 0, 0)
+            copy_p(1, 0, 1)
+            quant_rounds(4, 5)
+            quant_h((0, 0), (0, 1))
+            pair = w_tile(2, "wh")
+            weave(7, nc.gpsimd, pair, 0)
+            for n, b in zip((4, 5), (7, 2)):
+                turn_h(first[n], b)
+                weigh_h(first[n], tiles[slots[n][0]], slots[n][1])
+            turn_p(1, 1, 0, 0)
+            turn_p(1, 1, 1, 4)
+            copy_p(1, 1, 0)
+            for unit, b in zip(units[2:], (1, 3)):
+                project(unit, b)
+            gelu(units[2])
+            copy_p(1, 1, 1)
+            gelu(units[3])
+            quant_rounds(6)
+            quant_h((2, 0), (2, 1), (1, 0), (1, 1))
+            quant_p(1, 0)
+            quant_p(1, 1)
+            gather(0, 5)
+            emb_factor(0)
+            weave(8, nc.scalar, pair, 1)
+            tile = h_tile(4)
+            for n, b in enumerate((7, 0, 4, 3)):
+                turn_h(units[n], b)
+            weigh_h(units[0], tile, 0)
+            done = units
 
-            for n in range(NR - LEAD):
-                late, early = n - 1, n - 1 + LEAD if n else 1
-                before = early - 1 if n != 1 else 1
-                i, odd = divmod(n - LAG, 2)
-                project(n, 1)
-                gelu(n, 1)
-                project(n + LEAD, 0)
-                gelu(n + LEAD, 0)
-                if live(n - LAG):
-                    gather(n - LAG)
-                if live(late):
-                    turn_h(late, 1)
-                if live(early):
-                    turn_h(early, 0)
-                if n == 0:
-                    turn_p(1, 1, 0, "te")
-                    copy_p(1, 0, 0)
-                    weave_w(n + LEAD + 3, nc.scalar)
-                    copy_p(1, 1, 0)
-                if n == 1:
-                    turn_p(1, 1, 1, "a")
-                    copy_p(1, 1, 1)
-                    copy_p(1, 0, 1)
-                if odd and i >= 1:
-                    turn_emb(i - 1)
-                if live(n - LAG):
-                    if odd:
-                        emb_product(i)
-                    else:
-                        emb_factor(i)
-                if live(late):
-                    weigh_h(late, 1, (before, 0))
-                if odd and live(n - LAG):
-                    emb_sum(i)
-                if n == 0:
-                    weigh_h(early, 0, (late + 1, 1))
-                    quant_h((0, 0), (2, 0))
-                for e, h in ([(0, 0), (0, 1)], [(1, 0)], [(1, 1)])[n] if n < 3 else []:
-                    quant_p(e, h)
-                if live(late):
-                    quant_h((before, 0), (late, 1))
-                if not odd and i >= 2:
-                    copy_emb(i - 2)
-                if live(n + LEAD + 2):
-                    if n > 1 and odd:
-                        weave_w(n + LEAD + 2, nc.scalar)
-                    quant_w(n + LEAD + 2)
-                if n == 4:
-                    nc.scalar.copy(out=vmat[0:64, :, 0], in_=cols[0:64, 3, :])
-                    nc.scalar.copy(out=vmat[64:128, :, 1], in_=cols[64:128, 3, :])
-                if odd and i >= 3:
-                    label_sums(i - 3)
-                if odd and i >= 2:
-                    weigh_emb(i - 2, nc.gpsimd if i >= 3 else nc.vector)
-                if n:
-                    weigh_h(early, 0, (late + 1, 1))
-                if n == 1:
-                    weave_w(n + LEAD + 3, nc.gpsimd)
-                if n and not odd and live(n + LEAD + 4):
-                    weave_w(n + LEAD + 4, nc.gpsimd)
+            for i in range(5):
+                r = 2 * i + 5
+                units = [(r + n, h) for n in range(2) for h in range(2)]
+                gather(2 * i + 1, 6)
+                weigh_h(done[1], tile, 1)
+                if i >= 2:
+                    label_sums(i - 2)
+                emb_product(i)
+                weigh_h(done[2], tile, 2)
+                emb_sum(i)
+                weigh_h(done[3], tile, 3)
+                for unit, b in zip(units, (1, 2, 7, 1)):
+                    project(unit, b)
+                    gelu(unit)
+                gather(2 * i + 2, 5)
+                emb_factor(i + 1)
+                quant_rounds(*range(r + 2, min(r + 4, NR)))
+                quant_h(*done)
+                turn_h(units[0], 0)
+                turn_emb(i, 7)
+                copy_emb(i)
+                if r + 4 < NR:
+                    rounds = range(r + 4, min(r + 6, NR))
+                    pair = w_tile(len(rounds), "wh")
+                    for n, q in enumerate(rounds):
+                        weave(q, nc.scalar if n else nc.gpsimd, pair, n)
+                weigh_emb(i)
+                if i == 3:
+                    nc.scalar.copy(out=vmat[0:64, 0:1], in_=cols[0:64, 3, NI - 1 : NI])
+                    nc.scalar.copy(out=vmat[64:128, 1:2], in_=cols[64:128, 3, NI - 1 : NI])
+                turn_h(units[1], 3)
+                turn_h(units[2], 4)
+                tile = h_tile(4)
+                weigh_h(units[0], tile, 0)
+                turn_h(units[3], 0)
+                done = units
 
-            last = NR - 1
-            label_sums(NV - 3)
-            weigh_emb(NV - 2, nc.gpsimd)
-            for r in (last - 2, last - 1):
-                project(r, 1)
-                gelu(r, 1)
-            gather(last - 4)
-            turn_h(last - 3, 1)
-            turn_h(last, 0)
-            turn_emb(NI - 4)
-            emb_product(NI - 3)
-            weigh_h(last - 3, 1, (last - 1, 0))
-            emb_sum(NI - 3)
-            quant_h((last - 1, 0), (last - 3, 1))
-            project(last, 1)
-            gelu(last, 1)
-            copy_emb(NI - 4)
-            turn_h(last - 2, 1)
-            weigh_h(last, 0, (last - 2, 1))
-            turn_h(last - 1, 1)
-            gather(last - 3)
-            emb_factor(NI - 2)
-            weigh_h(last - 2, 1, (last, 0))
-            turn_h(last, 1)
-            turn_emb(NI - 3)
-            copy_emb(NI - 3)
-            weigh_h(last - 1, 1)
-            quant_h((last, 0), (last - 2, 1))
-            gather(last - 2)
-            weigh_h(last, 1)
-            quant_h((last - 1, 1))
-            gather(last - 1, "z")
-            emb_factor(NI - 1)
-            emb_product(NI - 2)
-            quant_h((last, 1))
-            gather(last, "z")
-            label_matmuls(NI - 3)
-            emb_sum(NI - 2)
-            turn_emb(NI - 2)
-            label_matmuls(NI - 2)
-            emb_product(NI - 1)
-            copy_emb(NI - 2)
-            emb_sum(NI - 1)
-            weigh_emb(NV - 1, nc.vector, "vt")
-            label_sums(NV - 2)
-            turn_emb(NI - 1, "b")
-            label_matmuls(NI - 1)
-            copy_emb(NI - 1)
-            label_sums(NV - 1)
+            project((15, 0), 1)
+            gelu((15, 0))
+            gather(11, 6)
+            project((15, 1), 2)
+            gelu((15, 1))
+            weigh_h(done[1], tile, 1)
+            weigh_h(done[2], tile, 2)
+            label_sums(3)
+            emb_product(5)
+            weigh_h(done[3], tile, 3)
+            gather(12, 7)
+            emb_factor(6)
+            copy_a(6)
+            turn_h((15, 0), 3)
+            turn_h((15, 1), 4)
+            emb_sum(5)
+            quant_h(*done)
+            tile = h_tile(2, "hl", 1)
+            weigh_h((15, 0), tile, 0)
+            weigh_h((15, 1), tile, 1)
+            turn_emb(5, 6)
+            copy_emb(5)
+            gather(14, 2)
+            gather(13, 0)
+            emb_factor(7)
+            copy_a(7)
+            tpe[6] = bank_of(5)
+            turn_term(6, av[6], True)
+            label_sums(4)
+            quant_h((15, 0), (15, 1))
+            weigh_emb(5, "hl", 1)
+            emb_product(6)
+            gather(15, 1)
+            tpe[7] = bank_of(7)
+            turn_term(6, uv[6], False)
+            turn_term(7, av[7], True)
+            copy_emb(6)
+            emb_product(7)
+            turn_term(7, uv[7], False)
+            copy_emb(7)
+            vv["bank"] = bank_of(3)
+            label_matmuls(7, av[7], first=True)
+            label_matmuls(7, uv[7], last=True)
+            weigh_bank(6)
+            label_sums(5)
+            label_sums(6)
             add_offsets(vv["bank"][:, 0 : 4 * C].rearrange("p (st c) -> p st c", c=C), slice(2 * NV, C))
             add_offsets(sums, slice(0, 2 * NV))
             nc.sync.dma_start(out=out_1.rearrange("(r st) c -> r st c", st=4), in_=score[:])

@@ -145,13 +145,13 @@ def tile_endpoint_span_scoring_f4_kernel(
         def w_tile(width, name="wg"):
             return stage.tile([P, width, 2, P, 4], BF16, name=name, align_bytes=64, bufs=1)
 
-        def weave(r, engine, tile, slot):
+        def weave(r, engine, tile, slot, passes=slice(0, 2)):
             i, e = divmod(r, 2)
             c, o = divmod(i * P, WCH)
             wg[r] = (tile, slot)
-            src = wraw[e, c][:, :, :, o : o + P].rearrange("p g t f -> p g f t")
+            src = wraw[e, c][:, passes, :, o : o + P].rearrange("p g t f -> p g f t")
             if engine is nc.scalar:
-                nc.scalar.copy(out=tile[:, slot], in_=src)
+                nc.scalar.copy(out=tile[:, slot, passes], in_=src)
             else:
                 nc.gpsimd.tensor_scalar(out=tile[:, slot], in0=src, scalar1=1.0, scalar2=0.0, op0=ALU.mult, op1=ALU.add)
 
@@ -182,7 +182,7 @@ def tile_endpoint_span_scoring_f4_kernel(
 
         def gelu(unit):
             i, e = divmod(unit[0], 2)
-            gl[unit] = stage.tile([P, 512], F32, name="gl", bufs=8)
+            gl[unit] = stage.tile([P, 512], F32, name="gl", bufs=7)
             nc.scalar.activation(
                 out=gl[unit][:], in_=z.pop(unit)[:], func=ACT.Gelu_apprx_tanh, bias=cols[:, e, i : i + 1]
             )
@@ -245,7 +245,7 @@ def tile_endpoint_span_scoring_f4_kernel(
             nc.vector.tensor_tensor(out=ev[i][:], in0=ab.pop(2 * i)[:], in1=uv.pop(i)[:], op=ALU.add)
 
         def copy_a(i):
-            av[i] = stage.tile([P, S], F32, name="av", bufs=2)
+            av[i] = stage.tile([P, S], F32, name="av", bufs=3)
             nc.scalar.copy(out=av[i][:], in_=ab.pop(2 * i)[:])
 
         def turn_emb(i, b):
@@ -322,8 +322,8 @@ def tile_endpoint_span_scoring_f4_kernel(
             load_w(0, 0)
             load_x_rows(2)
             load_x_rows(3)
-            load_w(1, 0)
             load_p(0, 0)
+            load_w(1, 0)
             for q, vec in enumerate((bs, be, mix, v)):
                 nc.sync.dma_start(out=rows[NI * q : NI * (q + 1), :], in_=vec.rearrange("(i f) -> i f", f=P))
             load_p(0, 1)
@@ -349,18 +349,23 @@ def tile_endpoint_span_scoring_f4_kernel(
                     weave_w(1, 0)
                 if n >= 1:
                     scale_x(*pieces[n - 1])
+                if n in (5, 6):
+                    turn_p(0, 0, n - 5, n - 1)
             nc.scalar.copy(out=rows32[:], in_=rows[:])
             scale_x(*pieces[-1])
-            turn_p(0, 0, 0, 4)
             small = bank_of(0)
             nc.tensor.transpose(small[:, 0:P], rows32[:], ident[:])
-            for n in range(1, 4):
-                turn_p(0, n // 2, n % 2, 4 + n)
-            turn_p(1, 0, 0, 1)
-            copy_p(0, 0, 0)
+            for h in range(2):
+                copy_p(0, 0, h)
+                turn_p(0, 1, h, 6 + h)
             nc.scalar.copy(out=cols[:].rearrange("p q i -> p (q i)"), in_=small[:, 0 : 4 * NI])
-            for n in range(1, 4):
-                copy_p(0, n // 2, n % 2)
+            for h in range(2):
+                copy_p(0, 1, h)
+                turn_p(1, 0, h, (1, 4)[h])
+            turn_p(1, 1, 0, 5)
+            for h in range(2):
+                copy_p(1, 0, h)
+            copy_p(1, 1, 0)
             quant_x(0, 0)
             quant_w(0, 0)
             quant_x(0, 1)
@@ -369,139 +374,147 @@ def tile_endpoint_span_scoring_f4_kernel(
             quant_w(1, 0)
             quant_p(0, 0)
             quant_p(0, 1)
+            quant_p(1, 0)
             pair = w_tile(2, "wh")
             weave(4, nc.gpsimd, pair, 0)
             weave(5, nc.gpsimd, pair, 1)
             first = [(0, 0), (2, 0), (0, 1), (2, 1), (1, 0), (1, 1)]
-            for unit, b in zip(first, (2, 3, 0, 4, 5, 6)):
+            for unit, b in zip(first[:4], (0, 2, 3, 6)):
                 project(unit, b)
                 gelu(unit)
             tiles = [h_tile(2), h_tile(4)]
             slots = [(0, 0), (1, 0), (0, 1), (1, 1), (1, 2), (1, 3)]
-            turn_h(first[0], 7)
-            turn_h(first[1], 2)
-            turn_p(1, 0, 1, 3)
-            turn_h(first[2], 0)
-            turn_h(first[3], 4)
-            for n in range(4):
-                weigh_h(first[n], tiles[slots[n][0]], slots[n][1])
-            weave(6, nc.scalar, w_tile(1, "wg"), 0)
-            units = [(r, h) for r in (3, 4) for h in range(2)]
-            for unit, b in zip(units[:2], (5, 6)):
+            turn_p(1, 1, 1, 7)
+            turn_h(first[0], 1)
+            for unit, b in zip(first[4:], (4, 5)):
                 project(unit, b)
                 gelu(unit)
-            copy_p(1, 0, 0)
-            copy_p(1, 0, 1)
+            for n, b in zip((1, 2, 3), (0, 2, 3)):
+                turn_h(first[n], b)
+            for n in range(4):
+                weigh_h(first[n], tiles[slots[n][0]], slots[n][1])
+            copy_p(1, 1, 1)
+            weave(6, nc.scalar, w_tile(1, "wg"), 0)
+            units = [(r, h) for r in (3, 4) for h in range(2)]
+            for unit, b in zip(units[:2], (6, 1)):
+                project(unit, b)
+                gelu(unit)
             quant_rounds(4, 5)
             quant_h((0, 0), (0, 1))
-            pair = w_tile(2, "wh")
-            weave(7, nc.gpsimd, pair, 0)
-            for n, b in zip((4, 5), (7, 2)):
+            for n, b in zip((4, 5), (4, 7)):
                 turn_h(first[n], b)
                 weigh_h(first[n], tiles[slots[n][0]], slots[n][1])
-            turn_p(1, 1, 0, 0)
-            turn_p(1, 1, 1, 4)
-            copy_p(1, 1, 0)
-            for unit, b in zip(units[2:], (1, 3)):
+            for unit, b in zip(units[2:], (0, 2)):
                 project(unit, b)
-            gelu(units[2])
-            copy_p(1, 1, 1)
-            gelu(units[3])
-            quant_rounds(6)
-            quant_h((2, 0), (2, 1), (1, 0), (1, 1))
-            quant_p(1, 0)
-            quant_p(1, 1)
+                gelu(unit)
             gather(0, 5)
             emb_factor(0)
-            weave(8, nc.scalar, pair, 1)
+            quant_p(1, 1)
+            quant_h((2, 0), (2, 1), (1, 0), (1, 1))
+            quant_rounds(6)
+            pair = w_tile(2, "wg")
+            weave(7, nc.gpsimd, pair, 0)
+            weave(8, nc.scalar, pair, 1, slice(0, 1))
             tile = h_tile(4)
-            for n, b in enumerate((7, 0, 4, 3)):
+            for n, b in enumerate((3, 4)):
                 turn_h(units[n], b)
-            weigh_h(units[0], tile, 0)
             done = units
 
             for i in range(5):
                 r = 2 * i + 5
                 units = [(r + n, h) for n in range(2) for h in range(2)]
                 gather(2 * i + 1, 6)
-                weigh_h(done[1], tile, 1)
+                for n in range(2):
+                    weigh_h(done[n], tile, n)
+                if i:
+                    copy_emb(i - 1)
+                    weigh_emb(i - 1)
+                if i and r + 3 < NR:
+                    weave(r + 3, nc.scalar, pair, 1, slice(0, 1))
+                for n in range(2):
+                    project(units[n], 1 + n)
+                    gelu(units[n])
+                if r + 3 < NR:
+                    weave(r + 3, nc.scalar, pair, 1, slice(1, 2))
+                emb_product(i)
                 if i >= 2:
                     label_sums(i - 2)
-                emb_product(i)
-                weigh_h(done[2], tile, 2)
                 emb_sum(i)
-                weigh_h(done[3], tile, 3)
-                for unit, b in zip(units, (1, 2, 7, 1)):
-                    project(unit, b)
-                    gelu(unit)
+                for n in range(2):
+                    turn_h(done[2 + n], (0, 4)[n])
+                    weigh_h(done[2 + n], tile, 2 + n)
+                for n in range(2):
+                    project(units[2 + n], 1 + n)
+                    gelu(units[2 + n])
                 gather(2 * i + 2, 5)
                 emb_factor(i + 1)
+                if i == 4:
+                    copy_a(5)
                 quant_rounds(*range(r + 2, min(r + 4, NR)))
                 quant_h(*done)
-                turn_h(units[0], 0)
-                turn_emb(i, 7)
-                copy_emb(i)
                 if r + 4 < NR:
-                    rounds = range(r + 4, min(r + 6, NR))
-                    pair = w_tile(len(rounds), "wh")
-                    for n, q in enumerate(rounds):
-                        weave(q, nc.scalar if n else nc.gpsimd, pair, n)
-                weigh_emb(i)
+                    pair = w_tile(min(2, NR - r - 4), "wg")
+                    weave(r + 4, nc.gpsimd, pair, 0)
                 if i == 3:
                     nc.scalar.copy(out=vmat[0:64, 0:1], in_=cols[0:64, 3, NI - 1 : NI])
                     nc.scalar.copy(out=vmat[64:128, 1:2], in_=cols[64:128, 3, NI - 1 : NI])
-                turn_h(units[1], 3)
-                turn_h(units[2], 4)
-                tile = h_tile(4)
-                weigh_h(units[0], tile, 0)
-                turn_h(units[3], 0)
+                turn_h(units[0], 3)
+                turn_h(units[1], 4)
+                if i == 4:
+                    turn_h(units[2], 0)
+                turn_emb(i, 7)
+                tile = h_tile(4) if i < 4 else h_tile(4, "hm", 1)
                 done = units
 
             project((15, 0), 1)
-            gelu((15, 0))
             gather(11, 6)
             project((15, 1), 2)
+            copy_emb(4)
+            weigh_emb(4)
+            gelu((15, 0))
             gelu((15, 1))
-            weigh_h(done[1], tile, 1)
-            weigh_h(done[2], tile, 2)
+            for n in range(3):
+                weigh_h(done[n], tile, n)
+            turn_h(done[3], 3)
+            tpe[5] = bank_of(7)
+            turn_term(5, av[5], True)
             label_sums(3)
             emb_product(5)
             weigh_h(done[3], tile, 3)
-            gather(12, 7)
+            gather(12, 4)
             emb_factor(6)
             copy_a(6)
-            turn_h((15, 0), 3)
-            turn_h((15, 1), 4)
-            emb_sum(5)
+            turn_h((15, 0), 0)
+            turn_h((15, 1), 1)
+            turn_term(5, uv[5], False)
+            copy_emb(5)
             quant_h(*done)
             tile = h_tile(2, "hl", 1)
             weigh_h((15, 0), tile, 0)
             weigh_h((15, 1), tile, 1)
-            turn_emb(5, 6)
-            copy_emb(5)
             gather(14, 2)
-            gather(13, 0)
+            gather(13, 3)
             emb_factor(7)
             copy_a(7)
             tpe[6] = bank_of(5)
             turn_term(6, av[6], True)
-            label_sums(4)
             quant_h((15, 0), (15, 1))
             weigh_emb(5, "hl", 1)
             emb_product(6)
-            gather(15, 1)
-            tpe[7] = bank_of(7)
+            gather(15, 0)
+            tpe[7] = bank_of(6)
             turn_term(6, uv[6], False)
             turn_term(7, av[7], True)
+            label_sums(4)
             copy_emb(6)
             emb_product(7)
+            vv["bank"] = bank_of(4)
+            label_matmuls(7, av[7], first=True)
             turn_term(7, uv[7], False)
             copy_emb(7)
-            vv["bank"] = bank_of(3)
-            label_matmuls(7, av[7], first=True)
             label_matmuls(7, uv[7], last=True)
-            weigh_bank(6)
             label_sums(5)
+            weigh_bank(6)
             label_sums(6)
             add_offsets(vv["bank"][:, 0 : 4 * C].rearrange("p (st c) -> p st c", c=C), slice(2 * NV, C))
             add_offsets(sums, slice(0, 2 * NV))

@@ -19,6 +19,7 @@ P = 128
 NI = F // P
 NR = 2 * NI
 WCH = 256
+NS = 6
 NV = 7
 
 
@@ -48,9 +49,10 @@ def tile_endpoint_span_scoring_f4_kernel(
         rows = keep.tile([P, P], BF16, name="rows")
         rows32 = keep.tile([P, P], F32, name="rows32")
         cols = keep.tile([P, 4, NI], F32, name="cols")
+        vmat = keep.tile([P, 2], F32, name="vmat")
         sums = keep.tile([P, 4, C], F32, name="sums")
         vrow = keep.tile([P, NV * P], BF16, name="vrow")
-        vmat = keep.tile([P, 2], F32, name="vmat")
+        mixrow = keep.tile([P, NS * P], BF16, name="mixrow")
         dbias = keep.tile([P, C], BF16, name="dbias")
         score = keep.tile([P, 4, C], F32, name="score")
 
@@ -218,8 +220,71 @@ def tile_endpoint_span_scoring_f4_kernel(
         def gather(r, b):
             e = r % 2
             ab[r] = bank_of(b)
+            for st in range(4):
+                span = slice(P * st, P * (st + 1))
+                for h in range(2):
+                    cod, sca = hq[r, h]
+                    nc.tensor.matmul_mx(
+                        out=ab[r][:, span],
+                        lhsT=pcod[e, h][:, span].bitcast(FP8X4),
+                        lhsT_scale=psca[e, h][:, span],
+                        rhs=cod.bitcast(FP8X4),
+                        rhs_scale=sca,
+                        start=(h == 0),
+                        stop=(h == 1),
+                    )
+
+        def row_of(rows_tile, i, width=4):
+            return rows_tile[:, P * i : P * (i + 1)].unsqueeze(1).to_broadcast([P, width, P])
+
+        def mix_a(i):
+            tv[i] = stage.tile([P, 4, P], F32, name="tv", bufs=2)
+            src = ab[2 * i][:].rearrange("p (st f) -> p st f", st=4)
+            nc.vector.tensor_tensor(out=tv[i][:], in0=src, in1=row_of(mixrow, i), op=ALU.mult)
+
+        def times_b(i):
+            uv[i] = stage.tile([P, S], F32, name="uv", bufs=2)
+            nc.vector.scalar_tensor_tensor(
+                out=uv[i][:],
+                in0=tv.pop(i)[:].rearrange("p st f -> p (st f)"),
+                scalar=1.0,
+                in1=ab.pop(2 * i + 1)[:],
+                op0=ALU.add,
+                op1=ALU.mult,
+            )
+
+        def plus_a(i):
+            eo[i] = stage.tile([P, 4, P], F32, name="eo", bufs=4)
+            flat = eo[i][:].rearrange("p st f -> p (st f)")
+            nc.vector.tensor_tensor(out=flat, in0=ab.pop(2 * i)[:], in1=uv.pop(i)[:], op=ALU.add)
+            nc.sync.dma_start(out=out_0.rearrange("(r st) f -> r st f", st=4)[:, :, P * i : P * (i + 1)], in_=eo[i][:])
+
+        def weigh_emb(i, engine, name="vv", bufs=3):
+            vv[i] = stage.tile([P, 4, P], F32, name=name, align_bytes=64, bufs=bufs)
+            engine.tensor_tensor(out=vv[i][:], in0=eo[i][:], in1=row_of(vrow, i), op=ALU.mult)
+
+        def label_sums(i):
+            nc.vector.tensor_reduce(
+                out=sums[:, :, 2 * i : 2 * i + 2],
+                in_=vv.pop(i)[:].rearrange("p st (c f) -> p st c f", c=2),
+                op=ALU.add,
+                axis=mybir.AxisListType.X,
+            )
+
+        def label_accum(i):
+            src = vv.pop(i)
+            for st in range(4):
+                for c in range(2):
+                    part = src[:, st, 64 * c : 64 * (c + 1)]
+                    nc.scalar.activation(
+                        out=part, in_=part, func=ACT.Identity, accum_out=sums[:, st, 2 * i + c : 2 * i + c + 1]
+                    )
+
+        def gather_features(r, b):
+            e = r % 2
+            ab[r] = bank_of(b)
             for h in range(2):
-                cod, sca = hq.pop((r, h))
+                cod, sca = hq[r, h]
                 nc.tensor.matmul_mx(
                     out=ab[r][:],
                     lhsT=cod.bitcast(FP8X4),
@@ -231,28 +296,40 @@ def tile_endpoint_span_scoring_f4_kernel(
                 )
 
         def emb_factor(i):
-            tv[i] = stage.tile([P, S], F32, name="tv", bufs=2)
+            tv[i] = stage.tile([P, S], F32, name="tf", bufs=2)
             nc.scalar.activation(
                 out=tv[i][:], in_=ab[2 * i][:], func=ACT.Identity, bias=1.0, scale=cols[:, 2, i : i + 1]
             )
 
-        def emb_product(i):
-            uv[i] = stage.tile([P, S], F32, name="uv", bufs=3)
-            nc.vector.tensor_tensor(out=uv[i][:], in0=ab.pop(2 * i + 1)[:], in1=tv.pop(i)[:], op=ALU.mult)
+        def emb_product(i, parts=1):
+            uv[i] = stage.tile([P, S], F32, name="uf", bufs=2)
+            for n in range(parts):
+                span = slice(n * S // parts, (n + 1) * S // parts)
+                nc.vector.tensor_tensor(out=uv[i][:, span], in0=ab[2 * i + 1][:, span], in1=tv[i][:, span], op=ALU.mult)
 
-        def emb_sum(i):
-            ev[i] = stage.tile([P, S], F32, name="ev", bufs=2)
-            nc.vector.tensor_tensor(out=ev[i][:], in0=ab.pop(2 * i)[:], in1=uv.pop(i)[:], op=ALU.add)
+        def turn_half(i, half, term, first):
+            if first:
+                tpe[i, half] = bank_of((3, 7)[half])
+            for st in range(2):
+                o = P * (2 * half + st)
+                nc.tensor.matmul(
+                    out=tpe[i, half][:, P * st : P * (st + 1)],
+                    lhsT=term[:, o : o + P],
+                    rhs=ident[:],
+                    is_transpose=True,
+                    start=first and st == 0,
+                    stop=not first and st == 1,
+                )
+
+        def copy_half(i, half):
+            eo[i, half] = stage.tile([P, 2, P], F32, name="eh", bufs=2)
+            nc.scalar.copy(out=eo[i, half][:].rearrange("p st f -> p (st f)"), in_=tpe[i, half][:, 0 : 2 * P])
+            rows_out = out_0.rearrange("(r st) f -> r st f", st=4)[:, 2 * half : 2 * half + 2, P * i : P * (i + 1)]
+            nc.sync.dma_start(out=rows_out, in_=eo[i, half][:])
 
         def copy_a(i):
             av[i] = stage.tile([P, S], F32, name="av", bufs=3)
             nc.scalar.copy(out=av[i][:], in_=ab.pop(2 * i)[:])
-
-        def turn_emb(i, b):
-            tpe[i] = bank_of(b)
-            src = ev.pop(i)
-            for st in range(4):
-                nc.tensor.transpose(tpe[i][:, P * st : P * (st + 1)], src[:, P * st : P * (st + 1)], ident[:])
 
         def turn_term(i, term, first):
             for st in range(4):
@@ -266,28 +343,15 @@ def tile_endpoint_span_scoring_f4_kernel(
                 )
 
         def copy_emb(i):
-            eo[i] = stage.tile([P, 4, P], F32, name="eo", bufs=6)
+            eo[i] = stage.tile([P, 4, P], F32, name="eo", bufs=4)
             nc.scalar.copy(out=eo[i][:].rearrange("p st f -> p (st f)"), in_=tpe[i][:])
             nc.sync.dma_start(out=out_0.rearrange("(r st) f -> r st f", st=4)[:, :, P * i : P * (i + 1)], in_=eo[i][:])
-
-        def weigh_emb(i, name="vv", bufs=3):
-            vv[i] = stage.tile([P, 4, P], F32, name=name, align_bytes=64, bufs=bufs)
-            row = vrow[:, P * i : P * (i + 1)].unsqueeze(1).to_broadcast([P, 4, P])
-            nc.gpsimd.tensor_tensor(out=vv[i][:], in0=eo[i][:], in1=row, op=ALU.mult)
 
         def weigh_bank(i):
             vv[i] = stage.tile([P, 4, P], F32, name="vv", align_bytes=64, bufs=3)
             row = vrow[:, P * i : P * (i + 1)].unsqueeze(1).to_broadcast([P, 4, P])
             nc.vector.tensor_tensor(
                 out=vv[i][:], in0=tpe[i][:].rearrange("p (st f) -> p st f", st=4), in1=row, op=ALU.mult
-            )
-
-        def label_sums(i):
-            nc.vector.tensor_reduce(
-                out=sums[:, :, 2 * i : 2 * i + 2],
-                in_=vv.pop(i)[:].rearrange("p st (c f) -> p st c f", c=2),
-                op=ALU.add,
-                axis=mybir.AxisListType.X,
             )
 
         def label_matmuls(i, term, first=False, last=False):
@@ -333,6 +397,7 @@ def tile_endpoint_span_scoring_f4_kernel(
                 nc.sync.dma_start(out=sal[e][:], in_=gv.rearrange("(h m j) -> m h j", h=2, j=4))
             load_w(0, 1)
             load_w(1, 1)
+            nc.sync.dma_start(out=mixrow[:], in_=mix[0 : NS * P].partition_broadcast(P))
             for c in range(2, F // WCH):
                 load_w(0, c)
                 load_w(1, c)
@@ -408,114 +473,109 @@ def tile_endpoint_span_scoring_f4_kernel(
                 project(unit, b)
                 gelu(unit)
             gather(0, 5)
-            emb_factor(0)
             quant_p(1, 1)
             quant_h((2, 0), (2, 1), (1, 0), (1, 1))
             quant_rounds(6)
             pair = w_tile(2, "wg")
             weave(7, nc.gpsimd, pair, 0)
-            weave(8, nc.scalar, pair, 1, slice(0, 1))
-            tile = h_tile(4)
+            weave(8, nc.scalar, pair, 1)
+            tile = h_tile(2)
             for n, b in enumerate((3, 4)):
                 turn_h(units[n], b)
             done = units
 
+            waiting = []
             for i in range(5):
                 r = 2 * i + 5
                 units = [(r + n, h) for n in range(2) for h in range(2)]
+                turned = [(3, 4, 0)[(4 * i + n) % 3] for n in range(2, 6)]
+                base = len(waiting)
                 gather(2 * i + 1, 6)
-                for n in range(2):
-                    weigh_h(done[n], tile, n)
-                if i:
-                    copy_emb(i - 1)
-                    weigh_emb(i - 1)
-                if i and r + 3 < NR:
-                    weave(r + 3, nc.scalar, pair, 1, slice(0, 1))
+                weigh_h(done[0], tile, base)
+                mix_a(i)
+                weigh_h(done[1], tile, base + 1)
                 for n in range(2):
                     project(units[n], 1 + n)
                     gelu(units[n])
-                if r + 3 < NR:
-                    weave(r + 3, nc.scalar, pair, 1, slice(1, 2))
-                emb_product(i)
-                if i >= 2:
-                    label_sums(i - 2)
-                emb_sum(i)
+                if i:
+                    label_accum(i - 1)
+                times_b(i)
+                quant_rounds(*range(r + 2, min(r + 4, NR)))
+                quant_h(*waiting, *done[:2])
+                tile = h_tile(4)
                 for n in range(2):
-                    turn_h(done[2 + n], (0, 4)[n])
-                    weigh_h(done[2 + n], tile, 2 + n)
+                    turn_h(done[2 + n], turned[n])
+                weigh_h(done[2], tile, 0)
+                plus_a(i)
+                weigh_h(done[3], tile, 1)
+                waiting = done[2:]
                 for n in range(2):
                     project(units[2 + n], 1 + n)
                     gelu(units[2 + n])
-                gather(2 * i + 2, 5)
-                emb_factor(i + 1)
-                if i == 4:
-                    copy_a(5)
-                quant_rounds(*range(r + 2, min(r + 4, NR)))
-                quant_h(*done)
-                if r + 4 < NR:
-                    pair = w_tile(min(2, NR - r - 4), "wg")
-                    weave(r + 4, nc.gpsimd, pair, 0)
+                gather(2 * i + 2, (7, 5)[i % 2])
                 if i == 3:
                     nc.scalar.copy(out=vmat[0:64, 0:1], in_=cols[0:64, 3, NI - 1 : NI])
                     nc.scalar.copy(out=vmat[64:128, 1:2], in_=cols[64:128, 3, NI - 1 : NI])
-                turn_h(units[0], 3)
-                turn_h(units[1], 4)
-                if i == 4:
-                    turn_h(units[2], 0)
-                turn_emb(i, 7)
-                tile = h_tile(4) if i < 4 else h_tile(4, "hm", 1)
+                if r + 4 < NR:
+                    rounds = range(r + 4, min(r + 6, NR))
+                    pair = w_tile(len(rounds), "wg")
+                    for n, q in enumerate(rounds):
+                        weave(q, nc.scalar if n else nc.gpsimd, pair, n)
+                weigh_emb(i, nc.gpsimd)
+                for n in range(2):
+                    turn_h(units[n], turned[2 + n])
                 done = units
 
+            turn_h(done[2], 4)
             project((15, 0), 1)
             gather(11, 6)
             project((15, 1), 2)
-            copy_emb(4)
-            weigh_emb(4)
             gelu((15, 0))
+            label_accum(4)
             gelu((15, 1))
-            for n in range(3):
-                weigh_h(done[n], tile, n)
-            turn_h(done[3], 3)
-            tpe[5] = bank_of(7)
-            turn_term(5, av[5], True)
-            label_sums(3)
-            emb_product(5)
-            weigh_h(done[3], tile, 3)
-            gather(12, 4)
+            mix_a(5)
+            weigh_h(done[0], tile, 2)
+            weigh_h(done[1], tile, 3)
+            tile2 = h_tile(2)
+            weigh_h(done[2], tile2, 0)
+            quant_h(*waiting, *done[:2])
+            turn_h(done[3], 0)
+            turn_h((15, 0), 3)
+            times_b(5)
+            weigh_h(done[3], tile2, 1)
+            gather_features(12, 5)
+            turn_h((15, 1), 4)
             emb_factor(6)
             copy_a(6)
-            turn_h((15, 0), 0)
-            turn_h((15, 1), 1)
-            turn_term(5, uv[5], False)
-            copy_emb(5)
-            quant_h(*done)
-            tile = h_tile(2, "hl", 1)
-            weigh_h((15, 0), tile, 0)
-            weigh_h((15, 1), tile, 1)
-            gather(14, 2)
-            gather(13, 3)
+            last = h_tile(2)
+            weigh_h((15, 0), last, 0)
+            quant_h(*done[2:])
+            weigh_h((15, 1), last, 1)
+            gather_features(13, 1)
+            gather_features(14, 2)
             emb_factor(7)
             copy_a(7)
-            tpe[6] = bank_of(5)
-            turn_term(6, av[6], True)
-            quant_h((15, 0), (15, 1))
-            weigh_emb(5, "hl", 1)
             emb_product(6)
-            gather(15, 0)
-            tpe[7] = bank_of(6)
+            quant_h((15, 0), (15, 1))
+            plus_a(5)
+            weigh_emb(5, nc.gpsimd)
+            tpe[6] = bank_of(6)
+            turn_term(6, av[6], True)
             turn_term(6, uv[6], False)
-            turn_term(7, av[7], True)
-            label_sums(4)
-            copy_emb(6)
-            emb_product(7)
+            gather_features(15, 0)
+            for half in range(2):
+                turn_half(7, half, av[7], True)
             vv["bank"] = bank_of(4)
             label_matmuls(7, av[7], first=True)
-            turn_term(7, uv[7], False)
-            copy_emb(7)
-            label_matmuls(7, uv[7], last=True)
-            label_sums(5)
             weigh_bank(6)
+            copy_emb(6)
+            emb_product(7, 2)
+            for half in range(2):
+                turn_half(7, half, uv[7], False)
+                copy_half(7, half)
+            label_matmuls(7, uv[7], last=True)
             label_sums(6)
+            label_sums(5)
             add_offsets(vv["bank"][:, 0 : 4 * C].rearrange("p (st c) -> p st c", c=C), slice(2 * NV, C))
             add_offsets(sums, slice(0, 2 * NV))
             nc.sync.dma_start(out=out_1.rearrange("(r st) c -> r st c", st=4), in_=score[:])

@@ -50,6 +50,7 @@ def tile_endpoint_span_scoring_f4_kernel(
         rows32 = keep.tile([P, P], F32, name="rows32")
         cols = keep.tile([P, 4, NI], F32, name="cols")
         vmat = keep.tile([P, 2], F32, name="vmat")
+        unread = keep.tile([P, 1], F32, name="unread")
         sums = keep.tile([P, 4, C], F32, name="sums")
         vrow = keep.tile([P, NV * P], BF16, name="vrow")
         mixrow = keep.tile([P, NS * P], BF16, name="mixrow")
@@ -121,7 +122,7 @@ def tile_endpoint_span_scoring_f4_kernel(
 
         def copy_p(e, sp, h):
             if (e, h) not in pg:
-                pg[e, h] = stage.tile([P, S, 4], BF16, name="pg", align_bytes=64, bufs=4)
+                pg[e, h] = stage.tile([P, S, 4], BF16, name=f"pg{e}{h}", align_bytes=64, bufs=1)
             dst = pg[e, h][:, 256 * sp : 256 * (sp + 1), :]
             nc.scalar.copy(
                 out=dst.rearrange("p r q -> p (r q)").bitcast(F32).rearrange("p (r u) -> p r u", u=2),
@@ -131,18 +132,19 @@ def tile_endpoint_span_scoring_f4_kernel(
         def quant_p(e, h):
             quant(pcod[e, h][:], psca[e, h][:], pg.pop((e, h))[:].rearrange("p r q -> p (r q)"))
 
-        def weave_w(e, c):
-            wg[e, c] = stage.tile([P, 2, WCH, 4], BF16, name=("wg", "wh")[e], align_bytes=64, bufs=1)
-            src = wraw[e, c][:].rearrange("p g t f -> p g f t")
-            nc.gpsimd.tensor_scalar(out=wg[e, c][:], in0=src, scalar1=1.0, scalar2=0.0, op0=ALU.mult, op1=ALU.add)
+        def weave_pass(g):
+            if g == 0:
+                wg["first"] = stage.tile([P, 2, WCH, 4], BF16, name="wh", align_bytes=64, bufs=1)
+            src = wraw[0, 0][:, g].rearrange("p t f -> p f t")
+            nc.gpsimd.tensor_scalar(out=wg["first"][:, g], in0=src, scalar1=1.0, scalar2=0.0, op0=ALU.mult, op1=ALU.add)
 
-        def quant_w(e, c):
+        def quant_w():
             cod = stage.tile([P, 2, WCH], U32, name="wcod", align_bytes=64, bufs=4)
             sca = stage.tile([P, 2, WCH], U8, name="wsca", align_bytes=64, bufs=4)
             flat = "p g f -> p (g f)"
-            quant(cod[:].rearrange(flat), sca[:].rearrange(flat), wg.pop((e, c))[:].rearrange("p g f q -> p (g f q)"))
+            quant(cod[:].rearrange(flat), sca[:].rearrange(flat), wg.pop("first")[:].rearrange("p g f q -> p (g f q)"))
             for o in range(2):
-                wq[4 * c + 2 * o + e] = (cod[:, :, P * o : P * (o + 1)], sca[:, :, P * o : P * (o + 1)])
+                wq[2 * o] = (cod[:, :, P * o : P * (o + 1)], sca[:, :, P * o : P * (o + 1)])
 
         def w_tile(width, name="wg"):
             return stage.tile([P, width, 2, P, 4], BF16, name=name, align_bytes=64, bufs=1)
@@ -378,20 +380,21 @@ def tile_endpoint_span_scoring_f4_kernel(
             make_identity(nc, ident[:])
             nc.vector.memset(rows[:], 0.0)
             nc.vector.memset(vmat[:], 0.0)
+            nc.scalar.activation(out=unread[:], in_=vmat[:, 0:1], func=ACT.Gelu_apprx_tanh)
             load_x(0, 0)
             load_x(1, 0)
             nc.sync.dma_start(out=xs[:], in_=x_scale.rearrange("o (g p t) -> p (o g) t", p=P, t=4))
             load_x(0, 1)
             load_x(1, 1)
-            load_w(0, 0)
+            load_p(0, 0)
             load_x_rows(2)
             load_x_rows(3)
-            load_p(0, 0)
-            load_w(1, 0)
+            load_w(0, 0)
+            load_p(0, 1)
             for q, vec in enumerate((bs, be, mix, v)):
                 nc.sync.dma_start(out=rows[NI * q : NI * (q + 1), :], in_=vec.rearrange("(i f) -> i f", f=P))
-            load_p(0, 1)
             load_p(1, 0)
+            load_w(1, 0)
             load_p(1, 1)
             for e, gv in enumerate((gs, ge)):
                 nc.sync.dma_start(out=sal[e][:], in_=gv.rearrange("(h m j) -> m h j", h=2, j=4))
@@ -404,81 +407,108 @@ def tile_endpoint_span_scoring_f4_kernel(
             nc.sync.dma_start(out=vrow[:], in_=v[0 : NV * P].partition_broadcast(P))
             nc.sync.dma_start(out=dbias[:], in_=d.partition_broadcast(P))
 
-            pieces = [(0, 0), (1, 0), (0, 1), (1, 1), (2, 0), (3, 0), (2, 1), (3, 1)]
-            for n, (m, g) in enumerate(pieces):
+            def piece(m, g, b, second=nc.scalar):
                 cast_x(2 * m, g, nc.scalar)
-                cast_x(2 * m + 1, g, nc.vector if n < 2 else nc.scalar)
-                turn_x(m, g, n % 4)
-                if n == 3:
-                    weave_w(0, 0)
-                    weave_w(1, 0)
-                if n >= 1:
-                    scale_x(*pieces[n - 1])
-                if n in (5, 6):
-                    turn_p(0, 0, n - 5, n - 1)
+                cast_x(2 * m + 1, g, second)
+                turn_x(m, g, b)
+
+            piece(0, 0, 0, nc.vector)
+            piece(1, 0, 1, nc.vector)
+            piece(0, 1, 2, nc.vector)
+            scale_x(0, 0)
+            piece(1, 1, 3)
+            scale_x(1, 0)
+            weave_pass(0)
+            weave_pass(1)
+            turn_p(0, 0, 0, 4)
+            turn_p(0, 0, 1, 5)
+            piece(2, 0, 0)
+            scale_x(0, 1)
+            piece(3, 0, 1)
+            scale_x(1, 1)
+            piece(2, 1, 2)
+            turn_p(0, 1, 0, 6)
+            scale_x(2, 0)
+            piece(3, 1, 3)
+            turn_p(0, 1, 1, 7)
+            scale_x(3, 0)
+            quant_x(0, 0)
+            quant_w()
+            quant_x(0, 1)
+            both = w_tile(2, "xg01")
+            weave(1, nc.gpsimd, both, 0)
             nc.scalar.copy(out=rows32[:], in_=rows[:])
-            scale_x(*pieces[-1])
+            copy_p(0, 0, 0)
+            copy_p(0, 0, 1)
             small = bank_of(0)
             nc.tensor.transpose(small[:, 0:P], rows32[:], ident[:])
-            for h in range(2):
-                copy_p(0, 0, h)
-                turn_p(0, 1, h, 6 + h)
+            turn_p(1, 0, 0, 4)
+            turn_p(1, 0, 1, 5)
             nc.scalar.copy(out=cols[:].rearrange("p q i -> p (q i)"), in_=small[:, 0 : 4 * NI])
-            for h in range(2):
-                copy_p(0, 1, h)
-                turn_p(1, 0, h, (1, 4)[h])
-            turn_p(1, 1, 0, 5)
-            for h in range(2):
-                copy_p(1, 0, h)
-            copy_p(1, 1, 0)
-            quant_x(0, 0)
-            quant_w(0, 0)
-            quant_x(0, 1)
-            quant_x(1, 0)
-            quant_x(1, 1)
-            quant_w(1, 0)
-            quant_p(0, 0)
-            quant_p(0, 1)
-            quant_p(1, 0)
-            pair = w_tile(2, "wh")
-            weave(4, nc.gpsimd, pair, 0)
-            weave(5, nc.gpsimd, pair, 1)
+            copy_p(0, 1, 0)
+            copy_p(0, 1, 1)
+            scale_x(2, 1)
+            scale_x(3, 1)
             first = [(0, 0), (2, 0), (0, 1), (2, 1), (1, 0), (1, 1)]
-            for unit, b in zip(first[:4], (0, 2, 3, 6)):
-                project(unit, b)
-                gelu(unit)
             tiles = [h_tile(2), h_tile(4)]
             slots = [(0, 0), (1, 0), (0, 1), (1, 1), (1, 2), (1, 3)]
+
+            def weigh_first(n):
+                weigh_h(first[n], tiles[slots[n][0]], slots[n][1])
+
+            project(first[0], 1)
+            copy_p(1, 0, 0)
+            weave(3, nc.scalar, both, 1, slice(0, 1))
+            gelu(first[0])
+            copy_p(1, 0, 1)
+            turn_p(1, 1, 0, 6)
+            project(first[1], 0)
+            weave(3, nc.scalar, both, 1, slice(1, 2))
+            gelu(first[1])
             turn_p(1, 1, 1, 7)
-            turn_h(first[0], 1)
-            for unit, b in zip(first[4:], (4, 5)):
+            turn_h(first[0], 4)
+            copy_p(1, 1, 0)
+            quant_x(1, 0)
+            quant_x(1, 1)
+            quant_p(0, 0)
+            quant_rounds(1, 3)
+            quant_p(0, 1)
+            quant_p(1, 0)
+            weave(4, nc.gpsimd, w_tile(1, "pg10"), 0)
+            for unit, b in zip(first[2:4], (5, 1)):
                 project(unit, b)
                 gelu(unit)
-            for n, b in zip((1, 2, 3), (0, 2, 3)):
-                turn_h(first[n], b)
-            for n in range(4):
-                weigh_h(first[n], tiles[slots[n][0]], slots[n][1])
             copy_p(1, 1, 1)
-            weave(6, nc.scalar, w_tile(1, "wg"), 0)
-            units = [(r, h) for r in (3, 4) for h in range(2)]
-            for unit, b in zip(units[:2], (6, 1)):
+            turn_h(first[1], 2)
+            turn_h(first[2], 3)
+            for unit, b in zip(first[4:], (6, 0)):
                 project(unit, b)
                 gelu(unit)
-            quant_rounds(4, 5)
+            turn_h(first[3], 5)
+            for n in range(3):
+                weigh_first(n)
+            quant_rounds(4)
             quant_h((0, 0), (0, 1))
-            for n, b in zip((4, 5), (4, 7)):
+            quant_p(1, 1)
+            weave(5, nc.gpsimd, w_tile(1, "pg11"), 0)
+            weave(6, nc.scalar, w_tile(1, "wh"), 0)
+            units = [(r, h) for r in (3, 4) for h in range(2)]
+            for unit, b in zip(units[:2], (7, 1)):
+                project(unit, b)
+                gelu(unit)
+            weigh_first(3)
+            for n, b in zip((4, 5), (4, 6)):
                 turn_h(first[n], b)
-                weigh_h(first[n], tiles[slots[n][0]], slots[n][1])
+                weigh_first(n)
             for unit, b in zip(units[2:], (0, 2)):
                 project(unit, b)
                 gelu(unit)
             gather(0, 5)
-            quant_p(1, 1)
-            quant_h((2, 0), (2, 1), (1, 0), (1, 1))
             quant_rounds(6)
-            pair = w_tile(2, "wg")
-            weave(7, nc.gpsimd, pair, 0)
-            weave(8, nc.scalar, pair, 1)
+            quant_h((2, 0), (2, 1), (1, 0), (1, 1))
+            quant_rounds(5)
+            weave(7, nc.gpsimd, w_tile(1, "pg11"), 0)
+            weave(8, nc.scalar, w_tile(1, "wh"), 0)
             tile = h_tile(2)
             for n, b in enumerate((3, 4)):
                 turn_h(units[n], b)
@@ -500,7 +530,11 @@ def tile_endpoint_span_scoring_f4_kernel(
                 if i:
                     label_accum(i - 1)
                 times_b(i)
-                quant_rounds(*range(r + 2, min(r + 4, NR)))
+                if i:
+                    quant_rounds(*range(r + 2, min(r + 4, NR)))
+                else:
+                    quant_rounds(8)
+                    quant_rounds(7)
                 quant_h(*waiting, *done[:2])
                 tile = h_tile(4)
                 for n in range(2):
@@ -518,7 +552,7 @@ def tile_endpoint_span_scoring_f4_kernel(
                     nc.scalar.copy(out=vmat[64:128, 1:2], in_=cols[64:128, 3, NI - 1 : NI])
                 if r + 4 < NR:
                     rounds = range(r + 4, min(r + 6, NR))
-                    pair = w_tile(len(rounds), "wg")
+                    pair = w_tile(len(rounds), "pg11")
                     for n, q in enumerate(rounds):
                         weave(q, nc.scalar if n else nc.gpsimd, pair, n)
                 weigh_emb(i, nc.gpsimd)

@@ -20,6 +20,7 @@ NI = F // P
 NR = 2 * NI
 WCH = 256
 NS = 6
+HALF_BANKS = (3, 7)
 NV = 7
 
 
@@ -34,8 +35,7 @@ def tile_endpoint_span_scoring_f4_kernel(
 
         ident = keep.tile([P, P], F32, name="ident")
 
-        xb = {(m, g): keep.tile([P, 2, 512], U8, name=f"xb{m}{g}", align_bytes=64) for m in range(2) for g in range(2)}
-        xc = {m: keep.tile([P, 2, D], U8, name=f"xc{m}", align_bytes=64) for m in range(2, 4)}
+        xb = [keep.tile([P, 2, D], U8, name=f"xb{m}", align_bytes=64) for m in range(4)]
         xs = keep.tile([P, 2, 4], F32, name="xs")
         xcod = {(h, g): keep.tile([P, 512], U32, name=f"xcod{h}{g}", align_bytes=64) for h in range(2) for g in range(2)}
         xsca = {(h, g): keep.tile([P, 512], U8, name=f"xsca{h}{g}", align_bytes=64) for h in range(2) for g in range(2)}
@@ -55,20 +55,19 @@ def tile_endpoint_span_scoring_f4_kernel(
         vrow = keep.tile([P, NV * P], BF16, name="vrow")
         mixrow = keep.tile([P, NS * P], BF16, name="mixrow")
         dbias = keep.tile([P, C], BF16, name="dbias")
+        dshare = keep.tile([P, C], F32, name="dshare")
         score = keep.tile([P, 4, C], F32, name="score")
 
         xv = x_bytes.rearrange("(h p j) k -> h p j k", h=2, p=P, j=4)
         wv = [w.rearrange("(g p j) f -> g p j f", g=2, p=P, j=4) for w in (ws, we)]
         pv = [q.rearrange("(r st) t -> r st t", st=4) for q in (ps, pe)]
 
-        def load_x(m, g):
-            nc.sync.dma_start(out=xb[m, g][:], in_=xv[0][:, 2 * m : 2 * m + 2, 512 * g : 512 * (g + 1)])
+        def load_x(m):
+            h, jp = divmod(m, 2)
+            nc.sync.dma_start(out=xb[m][:], in_=xv[h][:, 2 * jp : 2 * jp + 2, :])
 
-        def load_x_rows(m):
-            nc.sync.dma_start(out=xc[m][:], in_=xv[1][:, 2 * m - 4 : 2 * m - 2, :])
-
-        def load_w(e, c):
-            for g in range(2):
+        def load_w(e, c, passes=range(2)):
+            for g in passes:
                 nc.sync.dma_start(out=wraw[e, c][:, g, :, :], in_=wv[e][g][:, :, c * WCH : (c + 1) * WCH])
 
         def load_p(e, sp):
@@ -82,7 +81,7 @@ def tile_endpoint_span_scoring_f4_kernel(
 
         def cast_x(n, g, engine):
             xw[n, g] = stage.tile([P, 512], BF16, name="xw", bufs=8)
-            raw = xb[n // 2, g][:, n % 2, :] if n < 4 else xc[n // 2][:, n % 2, 512 * g : 512 * (g + 1)]
+            raw = xb[n // 2][:, n % 2, 512 * g : 512 * (g + 1)]
             if engine is nc.vector:
                 nc.vector.tensor_copy(out=xw[n, g][:], in_=raw.bitcast(FP8))
             else:
@@ -98,7 +97,7 @@ def tile_endpoint_span_scoring_f4_kernel(
 
         def turn_x(m, g, b):
             xbank[m, g] = bank_of(b)
-            for half in range(2):
+            for half in (1, 0):
                 turn_words(xbank[m, g], half, xw.pop((2 * m + half, g))[:].bitcast(F32))
 
         def scale_x(m, g):
@@ -244,6 +243,15 @@ def tile_endpoint_span_scoring_f4_kernel(
             src = ab[2 * i][:].rearrange("p (st f) -> p st f", st=4)
             nc.vector.tensor_tensor(out=tv[i][:], in0=src, in1=row_of(mixrow, i), op=ALU.mult)
 
+        def copy_spans(i):
+            av[i] = stage.tile([P, S], F32, name="av", bufs=3)
+            nc.scalar.copy(out=av[i][:], in_=ab[2 * i][:])
+
+        def mix_copy(i):
+            tv[i] = stage.tile([P, 4, P], F32, name="tv", bufs=2)
+            src = av[i][:].rearrange("p (st f) -> p st f", st=4)
+            nc.gpsimd.tensor_tensor(out=tv[i][:], in0=src, in1=row_of(mixrow, i), op=ALU.mult)
+
         def times_b(i):
             uv[i] = stage.tile([P, S], F32, name="uv", bufs=2)
             nc.vector.scalar_tensor_tensor(
@@ -279,7 +287,11 @@ def tile_endpoint_span_scoring_f4_kernel(
                 for c in range(2):
                     part = src[:, st, 64 * c : 64 * (c + 1)]
                     nc.scalar.activation(
-                        out=part, in_=part, func=ACT.Identity, accum_out=sums[:, st, 2 * i + c : 2 * i + c + 1]
+                        out=part,
+                        in_=part,
+                        func=ACT.Identity,
+                        bias=dshare[:, 2 * i + c : 2 * i + c + 1],
+                        accum_out=score[:, st, 2 * i + c : 2 * i + c + 1],
                     )
 
         def gather_features(r, b):
@@ -311,7 +323,7 @@ def tile_endpoint_span_scoring_f4_kernel(
 
         def turn_half(i, half, term, first):
             if first:
-                tpe[i, half] = bank_of((3, 7)[half])
+                tpe[i, half] = bank_of(HALF_BANKS[half])
             for st in range(2):
                 o = P * (2 * half + st)
                 nc.tensor.matmul(
@@ -381,16 +393,15 @@ def tile_endpoint_span_scoring_f4_kernel(
             nc.vector.memset(rows[:], 0.0)
             nc.vector.memset(vmat[:], 0.0)
             nc.scalar.activation(out=unread[:], in_=vmat[:, 0:1], func=ACT.Gelu_apprx_tanh)
-            load_x(0, 0)
-            load_x(1, 0)
+            load_x(0)
             nc.sync.dma_start(out=xs[:], in_=x_scale.rearrange("o (g p t) -> p (o g) t", p=P, t=4))
-            load_x(0, 1)
-            load_x(1, 1)
+            load_x(1)
             load_p(0, 0)
-            load_x_rows(2)
-            load_x_rows(3)
-            load_w(0, 0)
+            load_x(2)
+            load_x(3)
+            load_w(0, 0, [0])
             load_p(0, 1)
+            load_w(0, 0, [1])
             for q, vec in enumerate((bs, be, mix, v)):
                 nc.sync.dma_start(out=rows[NI * q : NI * (q + 1), :], in_=vec.rearrange("(i f) -> i f", f=P))
             load_p(1, 0)
@@ -408,29 +419,29 @@ def tile_endpoint_span_scoring_f4_kernel(
             nc.sync.dma_start(out=dbias[:], in_=d.partition_broadcast(P))
 
             def piece(m, g, b, second=nc.scalar):
-                cast_x(2 * m, g, nc.scalar)
                 cast_x(2 * m + 1, g, second)
+                cast_x(2 * m, g, nc.scalar)
                 turn_x(m, g, b)
 
             piece(0, 0, 0, nc.vector)
-            piece(1, 0, 1, nc.vector)
-            piece(0, 1, 2, nc.vector)
+            piece(0, 1, 1, nc.vector)
+            piece(1, 0, 2, nc.vector)
             scale_x(0, 0)
             piece(1, 1, 3)
-            scale_x(1, 0)
+            scale_x(0, 1)
             weave_pass(0)
             weave_pass(1)
             turn_p(0, 0, 0, 4)
             turn_p(0, 0, 1, 5)
             piece(2, 0, 0)
-            scale_x(0, 1)
+            scale_x(1, 0)
             piece(3, 0, 1)
             scale_x(1, 1)
-            piece(2, 1, 2)
             turn_p(0, 1, 0, 6)
+            piece(2, 1, 2)
+            turn_p(0, 1, 1, 7)
             scale_x(2, 0)
             piece(3, 1, 3)
-            turn_p(0, 1, 1, 7)
             scale_x(3, 0)
             quant_x(0, 0)
             quant_w()
@@ -487,8 +498,8 @@ def tile_endpoint_span_scoring_f4_kernel(
             turn_h(first[3], 5)
             for n in range(3):
                 weigh_first(n)
-            quant_rounds(4)
             quant_h((0, 0), (0, 1))
+            quant_rounds(4)
             quant_p(1, 1)
             weave(5, nc.gpsimd, w_tile(1, "pg11"), 0)
             weave(6, nc.scalar, w_tile(1, "wh"), 0)
@@ -500,12 +511,13 @@ def tile_endpoint_span_scoring_f4_kernel(
             for n, b in zip((4, 5), (4, 6)):
                 turn_h(first[n], b)
                 weigh_first(n)
+            gather(0, 5)
             for unit, b in zip(units[2:], (0, 2)):
                 project(unit, b)
                 gelu(unit)
-            gather(0, 5)
-            quant_rounds(6)
+            mix_a(0)
             quant_h((2, 0), (2, 1), (1, 0), (1, 1))
+            quant_rounds(6)
             quant_rounds(5)
             weave(7, nc.gpsimd, w_tile(1, "pg11"), 0)
             weave(8, nc.scalar, w_tile(1, "wh"), 0)
@@ -522,11 +534,14 @@ def tile_endpoint_span_scoring_f4_kernel(
                 base = len(waiting)
                 gather(2 * i + 1, 6)
                 weigh_h(done[0], tile, base)
-                mix_a(i)
+                if i:
+                    mix_a(i)
                 weigh_h(done[1], tile, base + 1)
                 for n in range(2):
                     project(units[n], 1 + n)
                     gelu(units[n])
+                if i == 1:
+                    nc.scalar.mul(out=dshare[:], in_=dbias[:], mul=C / F)
                 if i:
                     label_accum(i - 1)
                 times_b(i)
@@ -565,8 +580,8 @@ def tile_endpoint_span_scoring_f4_kernel(
             gather(11, 6)
             project((15, 1), 2)
             gelu((15, 0))
-            label_accum(4)
             gelu((15, 1))
+            label_accum(4)
             mix_a(5)
             weigh_h(done[0], tile, 2)
             weigh_h(done[1], tile, 3)
@@ -587,8 +602,8 @@ def tile_endpoint_span_scoring_f4_kernel(
             weigh_h((15, 1), last, 1)
             gather_features(13, 1)
             gather_features(14, 2)
+            copy_spans(7)
             emb_factor(7)
-            copy_a(7)
             emb_product(6)
             quant_h((15, 0), (15, 1))
             plus_a(5)
@@ -611,5 +626,5 @@ def tile_endpoint_span_scoring_f4_kernel(
             label_sums(6)
             label_sums(5)
             add_offsets(vv["bank"][:, 0 : 4 * C].rearrange("p (st c) -> p st c", c=C), slice(2 * NV, C))
-            add_offsets(sums, slice(0, 2 * NV))
+            add_offsets(sums, slice(10, 14))
             nc.sync.dma_start(out=out_1.rearrange("(r st) c -> r st c", st=4), in_=score[:])

@@ -498,8 +498,8 @@ def tile_endpoint_span_scoring_f4_kernel(
             turn_h(first[3], 5)
             for n in range(3):
                 weigh_first(n)
-            quant_h((0, 0), (0, 1))
             quant_rounds(4)
+            quant_h((0, 0), (0, 1))
             quant_p(1, 1)
             weave(5, nc.gpsimd, w_tile(1, "pg11"), 0)
             weave(6, nc.scalar, w_tile(1, "wh"), 0)
@@ -511,13 +511,12 @@ def tile_endpoint_span_scoring_f4_kernel(
             for n, b in zip((4, 5), (4, 6)):
                 turn_h(first[n], b)
                 weigh_first(n)
-            gather(0, 5)
             for unit, b in zip(units[2:], (0, 2)):
                 project(unit, b)
                 gelu(unit)
-            mix_a(0)
-            quant_h((2, 0), (2, 1), (1, 0), (1, 1))
+            gather(0, 5)
             quant_rounds(6)
+            quant_h((2, 0), (2, 1), (1, 0), (1, 1))
             quant_rounds(5)
             weave(7, nc.gpsimd, w_tile(1, "pg11"), 0)
             weave(8, nc.scalar, w_tile(1, "wh"), 0)
@@ -534,8 +533,7 @@ def tile_endpoint_span_scoring_f4_kernel(
                 base = len(waiting)
                 gather(2 * i + 1, 6)
                 weigh_h(done[0], tile, base)
-                if i:
-                    mix_a(i)
+                mix_a(i)
                 weigh_h(done[1], tile, base + 1)
                 for n in range(2):
                     project(units[n], 1 + n)

@@ -35,7 +35,8 @@ def tile_endpoint_span_scoring_f4_kernel(
 
         ident = keep.tile([P, P], F32, name="ident")
 
-        xb = [keep.tile([P, 2, D], U8, name=f"xb{m}", align_bytes=64) for m in range(4)]
+        xb = {(m, g): keep.tile([P, 2, 512], U8, name=f"xb{m}{g}", align_bytes=64) for m in range(2) for g in range(2)}
+        xc = {m: keep.tile([P, 2, D], U8, name=f"xc{m}", align_bytes=64) for m in range(2, 4)}
         xs = keep.tile([P, 2, 4], F32, name="xs")
         xcod = {(h, g): keep.tile([P, 512], U32, name=f"xcod{h}{g}", align_bytes=64) for h in range(2) for g in range(2)}
         xsca = {(h, g): keep.tile([P, 512], U8, name=f"xsca{h}{g}", align_bytes=64) for h in range(2) for g in range(2)}
@@ -49,7 +50,7 @@ def tile_endpoint_span_scoring_f4_kernel(
         rows = keep.tile([P, P], BF16, name="rows")
         rows32 = keep.tile([P, P], F32, name="rows32")
         cols = keep.tile([P, 4, NI], F32, name="cols")
-        vmat = keep.tile([P, 2], F32, name="vmat")
+        dcol = keep.tile([P, 1], F32, name="dcol")
         unread = keep.tile([P, 1], F32, name="unread")
         sums = keep.tile([P, 4, C], F32, name="sums")
         vrow = keep.tile([P, NV * P], BF16, name="vrow")
@@ -62,9 +63,11 @@ def tile_endpoint_span_scoring_f4_kernel(
         wv = [w.rearrange("(g p j) f -> g p j f", g=2, p=P, j=4) for w in (ws, we)]
         pv = [q.rearrange("(r st) t -> r st t", st=4) for q in (ps, pe)]
 
-        def load_x(m):
-            h, jp = divmod(m, 2)
-            nc.sync.dma_start(out=xb[m][:], in_=xv[h][:, 2 * jp : 2 * jp + 2, :])
+        def load_x(m, g):
+            nc.sync.dma_start(out=xb[m, g][:], in_=xv[0][:, 2 * m : 2 * m + 2, 512 * g : 512 * (g + 1)])
+
+        def load_x_rows(m):
+            nc.sync.dma_start(out=xc[m][:], in_=xv[1][:, 2 * m - 4 : 2 * m - 2, :])
 
         def load_w(e, c, passes=range(2)):
             for g in passes:
@@ -81,7 +84,7 @@ def tile_endpoint_span_scoring_f4_kernel(
 
         def cast_x(n, g, engine):
             xw[n, g] = stage.tile([P, 512], BF16, name="xw", bufs=8)
-            raw = xb[n // 2][:, n % 2, 512 * g : 512 * (g + 1)]
+            raw = xb[n // 2, g][:, n % 2, :] if n < 4 else xc[n // 2][:, n % 2, 512 * g : 512 * (g + 1)]
             if engine is nc.vector:
                 nc.vector.tensor_copy(out=xw[n, g][:], in_=raw.bitcast(FP8))
             else:
@@ -97,7 +100,7 @@ def tile_endpoint_span_scoring_f4_kernel(
 
         def turn_x(m, g, b):
             xbank[m, g] = bank_of(b)
-            for half in (1, 0):
+            for half in range(2):
                 turn_words(xbank[m, g], half, xw.pop((2 * m + half, g))[:].bitcast(F32))
 
         def scale_x(m, g):
@@ -321,9 +324,9 @@ def tile_endpoint_span_scoring_f4_kernel(
                 span = slice(n * S // parts, (n + 1) * S // parts)
                 nc.vector.tensor_tensor(out=uv[i][:, span], in0=ab[2 * i + 1][:, span], in1=tv[i][:, span], op=ALU.mult)
 
-        def turn_half(i, half, term, first):
+        def turn_half(i, half, term, first, banks=HALF_BANKS):
             if first:
-                tpe[i, half] = bank_of(HALF_BANKS[half])
+                tpe[i, half] = bank_of(banks[half])
             for st in range(2):
                 o = P * (2 * half + st)
                 nc.tensor.matmul(
@@ -368,16 +371,25 @@ def tile_endpoint_span_scoring_f4_kernel(
                 out=vv[i][:], in0=tpe[i][:].rearrange("p (st f) -> p st f", st=4), in1=row, op=ALU.mult
             )
 
-        def label_matmuls(i, term, first=False, last=False):
-            for st in range(4):
-                o = C * st + 2 * i
-                nc.tensor.matmul(
-                    out=vv["bank"][:, o : o + 2],
-                    lhsT=term[:, P * st : P * (st + 1)],
-                    rhs=vmat[:],
-                    start=first and st == 0,
-                    stop=last and st == 3,
-                )
+        def weigh_a(i):
+            vv["a"] = stage.tile([P, S], F32, name="va", bufs=1)
+            nc.scalar.activation(
+                out=vv["a"][:], in_=ab[2 * i][:], func=ACT.Identity, scale=cols[:, 3, i : i + 1], bias=dcol[:]
+            )
+
+        def weigh_u(i, half):
+            if half == 0:
+                vv["u"] = stage.tile([P, S], F32, name="vu", bufs=1)
+            span = slice(256 * half, 256 * (half + 1))
+            nc.scalar.activation(out=vv["u"][:, span], in_=uv[i][:, span], func=ACT.Copy, scale=cols[:, 3, i : i + 1])
+
+        def label_half(i, half):
+            nc.vector.tensor_reduce(
+                out=score[:, 2 * half : 2 * half + 2, 2 * i : 2 * i + 2],
+                in_=tpe["v", half][:, 0 : 2 * P].rearrange("p (st c f) -> p st c f", st=2, c=2),
+                op=ALU.add,
+                axis=mybir.AxisListType.X,
+            )
 
         def add_offsets(src, labels):
             width = labels.stop - labels.start
@@ -391,17 +403,17 @@ def tile_endpoint_span_scoring_f4_kernel(
         with tc.manual_schedule():
             make_identity(nc, ident[:])
             nc.vector.memset(rows[:], 0.0)
-            nc.vector.memset(vmat[:], 0.0)
-            nc.scalar.activation(out=unread[:], in_=vmat[:, 0:1], func=ACT.Gelu_apprx_tanh)
-            load_x(0)
+            nc.scalar.activation(out=unread[:], in_=rows[:, 0:1], func=ACT.Gelu_apprx_tanh)
+            load_x(0, 0)
+            load_x(1, 0)
             nc.sync.dma_start(out=xs[:], in_=x_scale.rearrange("o (g p t) -> p (o g) t", p=P, t=4))
-            load_x(1)
+            load_x(0, 1)
+            load_x(1, 1)
             load_p(0, 0)
-            load_x(2)
-            load_x(3)
-            load_w(0, 0, [0])
+            load_x_rows(2)
+            load_x_rows(3)
+            load_w(0, 0)
             load_p(0, 1)
-            load_w(0, 0, [1])
             for q, vec in enumerate((bs, be, mix, v)):
                 nc.sync.dma_start(out=rows[NI * q : NI * (q + 1), :], in_=vec.rearrange("(i f) -> i f", f=P))
             load_p(1, 0)
@@ -419,29 +431,29 @@ def tile_endpoint_span_scoring_f4_kernel(
             nc.sync.dma_start(out=dbias[:], in_=d.partition_broadcast(P))
 
             def piece(m, g, b, second=nc.scalar):
-                cast_x(2 * m + 1, g, second)
                 cast_x(2 * m, g, nc.scalar)
+                cast_x(2 * m + 1, g, second)
                 turn_x(m, g, b)
 
             piece(0, 0, 0, nc.vector)
-            piece(0, 1, 1, nc.vector)
-            piece(1, 0, 2, nc.vector)
+            piece(1, 0, 1, nc.vector)
+            piece(0, 1, 2, nc.vector)
             scale_x(0, 0)
             piece(1, 1, 3)
-            scale_x(0, 1)
+            scale_x(1, 0)
             weave_pass(0)
             weave_pass(1)
             turn_p(0, 0, 0, 4)
             turn_p(0, 0, 1, 5)
             piece(2, 0, 0)
-            scale_x(1, 0)
+            scale_x(0, 1)
             piece(3, 0, 1)
             scale_x(1, 1)
-            turn_p(0, 1, 0, 6)
             piece(2, 1, 2)
-            turn_p(0, 1, 1, 7)
+            turn_p(0, 1, 0, 6)
             scale_x(2, 0)
             piece(3, 1, 3)
+            turn_p(0, 1, 1, 7)
             scale_x(3, 0)
             quant_x(0, 0)
             quant_w()
@@ -561,8 +573,8 @@ def tile_endpoint_span_scoring_f4_kernel(
                     gelu(units[2 + n])
                 gather(2 * i + 2, (7, 5)[i % 2])
                 if i == 3:
-                    nc.scalar.copy(out=vmat[0:64, 0:1], in_=cols[0:64, 3, NI - 1 : NI])
-                    nc.scalar.copy(out=vmat[64:128, 1:2], in_=cols[64:128, 3, NI - 1 : NI])
+                    nc.scalar.copy(out=dcol[0:64], in_=dshare[0:64, C - 2 : C - 1])
+                    nc.scalar.copy(out=dcol[64:128], in_=dshare[64:128, C - 1 : C])
                 if r + 4 < NR:
                     rounds = range(r + 4, min(r + 6, NR))
                     pair = w_tile(len(rounds), "pg11")
@@ -600,8 +612,9 @@ def tile_endpoint_span_scoring_f4_kernel(
             weigh_h((15, 1), last, 1)
             gather_features(13, 1)
             gather_features(14, 2)
-            copy_spans(7)
             emb_factor(7)
+            copy_spans(7)
+            weigh_a(7)
             emb_product(6)
             quant_h((15, 0), (15, 1))
             plus_a(5)
@@ -612,17 +625,21 @@ def tile_endpoint_span_scoring_f4_kernel(
             gather_features(15, 0)
             for half in range(2):
                 turn_half(7, half, av[7], True)
-            vv["bank"] = bank_of(4)
-            label_matmuls(7, av[7], first=True)
+            for half in range(2):
+                turn_half("v", half, vv["a"], True, (4, 1))
             weigh_bank(6)
-            copy_emb(6)
             emb_product(7, 2)
+            copy_emb(6)
+            weigh_u(7, 0)
+            weigh_u(7, 1)
             for half in range(2):
                 turn_half(7, half, uv[7], False)
+            for half in range(2):
+                turn_half("v", half, vv["u"], False)
                 copy_half(7, half)
-            label_matmuls(7, uv[7], last=True)
             label_sums(6)
             label_sums(5)
-            add_offsets(vv["bank"][:, 0 : 4 * C].rearrange("p (st c) -> p st c", c=C), slice(2 * NV, C))
+            label_half(7, 0)
             add_offsets(sums, slice(10, 14))
+            label_half(7, 1)
             nc.sync.dma_start(out=out_1.rearrange("(r st) c -> r st c", st=4), in_=score[:])

@@ -35,8 +35,8 @@ def tile_endpoint_span_scoring_f4_kernel(
 
         ident = keep.tile([P, P], F32, name="ident")
 
-        xb = {(m, g): keep.tile([P, 2, 512], U8, name=f"xb{m}{g}", align_bytes=64) for m in range(2) for g in range(2)}
-        xc = {m: keep.tile([P, 2, D], U8, name=f"xc{m}", align_bytes=64) for m in range(2, 4)}
+        xa = [keep.tile([P, D], U8, name=f"xa{n}", align_bytes=64) for n in range(2)]
+        xb = {m: keep.tile([P, 2, D], U8, name=f"xb{m}", align_bytes=64) for m in range(1, 4)}
         xs = keep.tile([P, 2, 4], F32, name="xs")
         xcod = {(h, g): keep.tile([P, 512], U32, name=f"xcod{h}{g}", align_bytes=64) for h in range(2) for g in range(2)}
         xsca = {(h, g): keep.tile([P, 512], U8, name=f"xsca{h}{g}", align_bytes=64) for h in range(2) for g in range(2)}
@@ -63,11 +63,9 @@ def tile_endpoint_span_scoring_f4_kernel(
         wv = [w.rearrange("(g p j) f -> g p j f", g=2, p=P, j=4) for w in (ws, we)]
         pv = [q.rearrange("(r st) t -> r st t", st=4) for q in (ps, pe)]
 
-        def load_x(m, g):
-            nc.sync.dma_start(out=xb[m, g][:], in_=xv[0][:, 2 * m : 2 * m + 2, 512 * g : 512 * (g + 1)])
-
-        def load_x_rows(m):
-            nc.sync.dma_start(out=xc[m][:], in_=xv[1][:, 2 * m - 4 : 2 * m - 2, :])
+        def load_x(m):
+            h, jp = divmod(m, 2)
+            nc.sync.dma_start(out=xb[m][:], in_=xv[h][:, 2 * jp : 2 * jp + 2, :])
 
         def load_w(e, c, passes=range(2)):
             for g in passes:
@@ -84,7 +82,8 @@ def tile_endpoint_span_scoring_f4_kernel(
 
         def cast_x(n, g, engine):
             xw[n, g] = stage.tile([P, 512], BF16, name="xw", bufs=8)
-            raw = xb[n // 2, g][:, n % 2, :] if n < 4 else xc[n // 2][:, n % 2, 512 * g : 512 * (g + 1)]
+            rows_n = xa[n][:] if n < 2 else xb[n // 2][:, n % 2]
+            raw = rows_n[:, 512 * g : 512 * (g + 1)]
             if engine is nc.vector:
                 nc.vector.tensor_copy(out=xw[n, g][:], in_=raw.bitcast(FP8))
             else:
@@ -111,6 +110,22 @@ def tile_endpoint_span_scoring_f4_kernel(
                 out=xg[h, g][:, 256 * jp : 256 * (jp + 1), :].rearrange("p r (u e) -> p r u e", e=2),
                 in0=xbank.pop((m, g))[:].bitcast(BF16).rearrange("p (u r e) -> p r u e", u=2, e=2),
                 in1=xs[:, g, :].unsqueeze(1).to_broadcast([P, 256, 4]).rearrange("p r (u e) -> p r u e", e=2),
+                op=ALU.mult,
+            )
+
+        def turn_tile(n, b):
+            xbank[n] = bank_of(b)
+            words = xw.pop((n, 0))[:].bitcast(F32)
+            for u in range(2):
+                nc.tensor.transpose(xbank[n][:, P * u : P * (u + 1)], words[:, u:256:2], ident[:])
+
+        def scale_tile(n):
+            if n == 0:
+                xg[0, 0] = stage.tile([P, 512, 4], BF16, name="xg00", align_bytes=64, bufs=1)
+            nc.vector.tensor_tensor(
+                out=xg[0, 0][:, P * n : P * (n + 1), :].rearrange("p r (u e) -> p r u e", e=2),
+                in0=xbank.pop(n)[:, 0 : 2 * P].bitcast(BF16).rearrange("p (u r e) -> p r u e", u=2, e=2),
+                in1=xs[:, 0, :].unsqueeze(1).to_broadcast([P, P, 4]).rearrange("p r (u e) -> p r u e", e=2),
                 op=ALU.mult,
             )
 
@@ -404,14 +419,13 @@ def tile_endpoint_span_scoring_f4_kernel(
             make_identity(nc, ident[:])
             nc.vector.memset(rows[:], 0.0)
             nc.scalar.activation(out=unread[:], in_=rows[:, 0:1], func=ACT.Gelu_apprx_tanh)
-            load_x(0, 0)
-            load_x(1, 0)
+            for n in range(2):
+                nc.sync.dma_start(out=xa[n][:], in_=xv[0][:, n, :])
             nc.sync.dma_start(out=xs[:], in_=x_scale.rearrange("o (g p t) -> p (o g) t", p=P, t=4))
-            load_x(0, 1)
-            load_x(1, 1)
+            load_x(1)
             load_p(0, 0)
-            load_x_rows(2)
-            load_x_rows(3)
+            load_x(2)
+            load_x(3)
             load_w(0, 0)
             load_p(0, 1)
             for q, vec in enumerate((bs, be, mix, v)):
@@ -435,25 +449,28 @@ def tile_endpoint_span_scoring_f4_kernel(
                 cast_x(2 * m + 1, g, second)
                 turn_x(m, g, b)
 
-            piece(0, 0, 0, nc.vector)
-            piece(1, 0, 1, nc.vector)
-            piece(0, 1, 2, nc.vector)
-            scale_x(0, 0)
+            for n in range(2):
+                cast_x(n, 0, nc.vector)
+                turn_tile(n, 4 + n)
+            piece(0, 1, 0, nc.vector)
+            scale_tile(0)
+            scale_tile(1)
+            piece(1, 0, 1)
+            scale_x(0, 1)
+            turn_p(0, 0, 0, 4)
             piece(1, 1, 3)
-            scale_x(1, 0)
             weave_pass(0)
             weave_pass(1)
-            turn_p(0, 0, 0, 4)
             turn_p(0, 0, 1, 5)
             piece(2, 0, 0)
-            scale_x(0, 1)
+            scale_x(1, 0)
             piece(3, 0, 1)
             scale_x(1, 1)
-            piece(2, 1, 2)
             turn_p(0, 1, 0, 6)
+            piece(2, 1, 2)
+            turn_p(0, 1, 1, 7)
             scale_x(2, 0)
             piece(3, 1, 3)
-            turn_p(0, 1, 1, 7)
             scale_x(3, 0)
             quant_x(0, 0)
             quant_w()
@@ -482,14 +499,13 @@ def tile_endpoint_span_scoring_f4_kernel(
             project(first[0], 1)
             copy_p(1, 0, 0)
             weave(3, nc.scalar, both, 1, slice(0, 1))
+            project(first[1], 0)
             gelu(first[0])
             copy_p(1, 0, 1)
             turn_p(1, 1, 0, 6)
-            project(first[1], 0)
+            turn_p(1, 1, 1, 7)
             weave(3, nc.scalar, both, 1, slice(1, 2))
             gelu(first[1])
-            turn_p(1, 1, 1, 7)
-            turn_h(first[0], 4)
             copy_p(1, 1, 0)
             quant_x(1, 0)
             quant_x(1, 1)
@@ -502,8 +518,8 @@ def tile_endpoint_span_scoring_f4_kernel(
                 project(unit, b)
                 gelu(unit)
             copy_p(1, 1, 1)
-            turn_h(first[1], 2)
-            turn_h(first[2], 3)
+            for n, b in enumerate((4, 2, 3)):
+                turn_h(first[n], b)
             for unit, b in zip(first[4:], (6, 0)):
                 project(unit, b)
                 gelu(unit)

@@ -425,8 +425,9 @@ def tile_endpoint_span_scoring_f4_kernel(
             load_x(1)
             load_p(0, 0)
             load_x(2)
+            load_w(0, 0, [0])
             load_x(3)
-            load_w(0, 0)
+            load_w(0, 0, [1])
             load_p(0, 1)
             for q, vec in enumerate((bs, be, mix, v)):
                 nc.sync.dma_start(out=rows[NI * q : NI * (q + 1), :], in_=vec.rearrange("(i f) -> i f", f=P))

@@ -438,12 +438,13 @@ def tile_endpoint_span_scoring_f4_kernel(
                 nc.sync.dma_start(out=sal[e][:], in_=gv.rearrange("(h m j) -> m h j", h=2, j=4))
             load_w(0, 1)
             load_w(1, 1)
+            load_w(0, 2)
             nc.sync.dma_start(out=mixrow[:], in_=mix[0 : NS * P].partition_broadcast(P))
-            for c in range(2, F // WCH):
-                load_w(0, c)
-                load_w(1, c)
+            load_w(1, 2)
             nc.sync.dma_start(out=vrow[:], in_=v[0 : NV * P].partition_broadcast(P))
             nc.sync.dma_start(out=dbias[:], in_=d.partition_broadcast(P))
+            load_w(0, 3)
+            load_w(1, 3)
 
             def piece(m, g, b, second=nc.scalar):
                 cast_x(2 * m, g, nc.scalar)

from contextlib import ExitStack

import concourse.mybir as mybir
from concourse.masks import make_identity

T, D, F, S, C = 1024, 1024, 1024, 512, 16
FLOPS = 2 * 2 * T * D * F + 2 * 2 * S * T * F

F32 = mybir.dt.float32
BF16 = mybir.dt.bfloat16
U32 = mybir.dt.uint32
U8 = mybir.dt.uint8
FP8 = mybir.dt.float8_e4m3fn
FP8X4 = mybir.dt.float8_e4m3fn_x4
ACT = mybir.ActivationFunctionType
ALU = mybir.AluOpType

P = 128
NI = F // P
NR = 2 * NI
WCH = 256
NS = 6
HALF_BANKS = (3, 7)
NV = 7


def tile_endpoint_span_scoring_f4_kernel(
    tc, x_bytes, x_scale, ws, we, bs, be, gs, ge, ps, pe, mix, v, d, out_0, out_1
):
    nc = tc.nc
    with ExitStack() as ctx:
        keep = ctx.enter_context(tc.tile_pool(name="keep", bufs=1))
        stage = ctx.enter_context(tc.tile_pool(name="stage", bufs=3))
        psum = ctx.enter_context(tc.psum_pool(name="psum", bufs=1))

        ident = keep.tile([P, P], F32, name="ident")

        xa = [keep.tile([P, D], U8, name=f"xa{n}", align_bytes=64) for n in range(2)]
        xb = {m: keep.tile([P, 2, D], U8, name=f"xb{m}", align_bytes=64) for m in range(1, 4)}
        xs = keep.tile([P, 2, 4], F32, name="xs")
        xcod = {(h, g): keep.tile([P, 512], U32, name=f"xcod{h}{g}", align_bytes=64) for h in range(2) for g in range(2)}
        xsca = {(h, g): keep.tile([P, 512], U8, name=f"xsca{h}{g}", align_bytes=64) for h in range(2) for g in range(2)}
        praw = {(e, sp): keep.tile([P, 2, T], BF16, name=f"praw{e}{sp}") for e in range(2) for sp in range(2)}
        pcod = {(e, h): keep.tile([P, S], U32, name=f"pcod{e}{h}", align_bytes=64) for e in range(2) for h in range(2)}
        psca = {(e, h): keep.tile([P, S], U8, name=f"psca{e}{h}", align_bytes=64) for e in range(2) for h in range(2)}
        wraw = {
            (e, c): keep.tile([P, 2, 4, WCH], BF16, name=f"wraw{e}{c}") for e in range(2) for c in range(F // WCH)
        }
        sal = [keep.tile([P, 2, 4], BF16, name=f"sal{e}") for e in range(2)]
        rows = keep.tile([P, P], BF16, name="rows")
        rows32 = keep.tile([P, P], F32, name="rows32")
        cols = keep.tile([P, 4, NI], F32, name="cols")
        dcol = keep.tile([P, 1], F32, name="dcol")
        unread = keep.tile([P, 1], F32, name="unread")
        sums = keep.tile([P, 4, C], F32, name="sums")
        vrow = keep.tile([P, NV * P], BF16, name="vrow")
        mixrow = keep.tile([P, NS * P], BF16, name="mixrow")
        dbias = keep.tile([P, C], BF16, name="dbias")
        dshare = keep.tile([P, C], F32, name="dshare")
        score = keep.tile([P, 4, C], F32, name="score")

        xv = x_bytes.rearrange("(h p j) k -> h p j k", h=2, p=P, j=4)
        wv = [w.rearrange("(g p j) f -> g p j f", g=2, p=P, j=4) for w in (ws, we)]
        pv = [q.rearrange("(r st) t -> r st t", st=4) for q in (ps, pe)]

        def load_x(m):
            h, jp = divmod(m, 2)
            nc.sync.dma_start(out=xb[m][:], in_=xv[h][:, 2 * jp : 2 * jp + 2, :])

        def load_w(e, c, passes=range(2)):
            for g in passes:
                nc.sync.dma_start(out=wraw[e, c][:, g, :, :], in_=wv[e][g][:, :, c * WCH : (c + 1) * WCH])

        def load_p(e, sp):
            nc.sync.dma_start(out=praw[e, sp][:], in_=pv[e][:, 2 * sp : 2 * sp + 2, :])

        def bank_of(b):
            return psum.tile([P, 512], F32, name=f"bank{b}")

        xw, xbank, xg, pbank, pg = {}, {}, {}, {}, {}
        wg, wq, z, gl, tph, hg, hq, ab, tv, uv, av, ev, tpe, eo, vv = ({} for n in range(15))

        def cast_x(n, g, engine):
            xw[n, g] = stage.tile([P, 512], BF16, name="xw", bufs=8)
            rows_n = xa[n][:] if n < 2 else xb[n // 2][:, n % 2]
            raw = rows_n[:, 512 * g : 512 * (g + 1)]
            if engine is nc.vector:
                nc.vector.tensor_copy(out=xw[n, g][:], in_=raw.bitcast(FP8))
            else:
                nc.scalar.copy(out=xw[n, g][:], in_=raw.bitcast(FP8))

        def turn_words(bank, half, words):
            for u in range(2):
                o = 256 * u + P * half
                nc.tensor.transpose(bank[:, o : o + P], words[:, u:256:2], ident[:])

        def quant(cod, sca, src):
            nc.vector.quantize_mx(out=cod.bitcast(FP8X4), scales=sca, in_=src)

        def turn_x(m, g, b):
            xbank[m, g] = bank_of(b)
            for half in range(2):
                turn_words(xbank[m, g], half, xw.pop((2 * m + half, g))[:].bitcast(F32))

        def scale_x(m, g):
            h, jp = divmod(m, 2)
            if jp == 0:
                xg[h, g] = stage.tile([P, 512, 4], BF16, name=f"xg{h}{g}", align_bytes=64, bufs=1)
            nc.vector.tensor_tensor(
                out=xg[h, g][:, 256 * jp : 256 * (jp + 1), :].rearrange("p r (u e) -> p r u e", e=2),
                in0=xbank.pop((m, g))[:].bitcast(BF16).rearrange("p (u r e) -> p r u e", u=2, e=2),
                in1=xs[:, g, :].unsqueeze(1).to_broadcast([P, 256, 4]).rearrange("p r (u e) -> p r u e", e=2),
                op=ALU.mult,
            )

        def turn_tile(n, b):
            xbank[n] = bank_of(b)
            words = xw.pop((n, 0))[:].bitcast(F32)
            for u in range(2):
                nc.tensor.transpose(xbank[n][:, P * u : P * (u + 1)], words[:, u:256:2], ident[:])

        def scale_tile(n):
            if n == 0:
                xg[0, 0] = stage.tile([P, 512, 4], BF16, name="xg00", align_bytes=64, bufs=1)
            nc.vector.tensor_tensor(
                out=xg[0, 0][:, P * n : P * (n + 1), :].rearrange("p r (u e) -> p r u e", e=2),
                in0=xbank.pop(n)[:, 0 : 2 * P].bitcast(BF16).rearrange("p (u r e) -> p r u e", u=2, e=2),
                in1=xs[:, 0, :].unsqueeze(1).to_broadcast([P, P, 4]).rearrange("p r (u e) -> p r u e", e=2),
                op=ALU.mult,
            )

        def quant_x(h, g):
            quant(xcod[h, g][:], xsca[h, g][:], xg.pop((h, g))[:].rearrange("p r q -> p (r q)"))

        def turn_p(e, sp, h, b):
            pbank[e, sp, h] = bank_of(b)
            for ss in range(2):
                turn_words(pbank[e, sp, h], ss, praw[e, sp][:, ss, 512 * h : 512 * (h + 1)].bitcast(F32))

        def copy_p(e, sp, h):
            if (e, h) not in pg:
                pg[e, h] = stage.tile([P, S, 4], BF16, name=f"pg{e}{h}", align_bytes=64, bufs=1)
            dst = pg[e, h][:, 256 * sp : 256 * (sp + 1), :]
            nc.scalar.copy(
                out=dst.rearrange("p r q -> p (r q)").bitcast(F32).rearrange("p (r u) -> p r u", u=2),
                in_=pbank.pop((e, sp, h))[:].rearrange("p (u r) -> p r u", u=2),
            )

        def quant_p(e, h):
            quant(pcod[e, h][:], psca[e, h][:], pg.pop((e, h))[:].rearrange("p r q -> p (r q)"))

        def weave_pass(g):
            if g == 0:
                wg["first"] = stage.tile([P, 2, WCH, 4], BF16, name="wh", align_bytes=64, bufs=1)
            src = wraw[0, 0][:, g].rearrange("p t f -> p f t")
            nc.gpsimd.tensor_scalar(out=wg["first"][:, g], in0=src, scalar1=1.0, scalar2=0.0, op0=ALU.mult, op1=ALU.add)

        def quant_w():
            cod = stage.tile([P, 2, WCH], U32, name="wcod", align_bytes=64, bufs=4)
            sca = stage.tile([P, 2, WCH], U8, name="wsca", align_bytes=64, bufs=4)
            flat = "p g f -> p (g f)"
            quant(cod[:].rearrange(flat), sca[:].rearrange(flat), wg.pop("first")[:].rearrange("p g f q -> p (g f q)"))
            for o in range(2):
                wq[2 * o] = (cod[:, :, P * o : P * (o + 1)], sca[:, :, P * o : P * (o + 1)])

        def w_tile(width, name="wg"):
            return stage.tile([P, width, 2, P, 4], BF16, name=name, align_bytes=64, bufs=1)

        def weave(r, engine, tile, slot, passes=slice(0, 2)):
            i, e = divmod(r, 2)
            c, o = divmod(i * P, WCH)
            wg[r] = (tile, slot)
            src = wraw[e, c][:, passes, :, o : o + P].rearrange("p g t f -> p g f t")
            if engine is nc.scalar:
                nc.scalar.copy(out=tile[:, slot, passes], in_=src)
            else:
                nc.gpsimd.tensor_scalar(out=tile[:, slot], in0=src, scalar1=1.0, scalar2=0.0, op0=ALU.mult, op1=ALU.add)

        def quant_rounds(*rounds):
            width = len(rounds)
            cod = stage.tile([P, width, 2, P], U32, name="wcod", align_bytes=64, bufs=4)
            sca = stage.tile([P, width, 2, P], U8, name="wsca", align_bytes=64, bufs=4)
            flat = "p e g f -> p (e g f)"
            quant(cod[:].rearrange(flat), sca[:].rearrange(flat), wg[rounds[0]][0][:].rearrange("p e g f q -> p (e g f q)"))
            for r in rounds:
                slot = wg.pop(r)[1]
                wq[r] = (cod[:, slot], sca[:, slot])

        def project(unit, b):
            r, h = unit
            cod, sca = wq[r]
            z[unit] = bank_of(b)
            for g in range(2):
                nc.tensor.matmul_mx(
                    out=z[unit][:],
                    lhsT=cod[:, g, :].bitcast(FP8X4),
                    lhsT_scale=sca[:, g, :],
                    rhs=xcod[h, g][:].bitcast(FP8X4),
                    rhs_scale=xsca[h, g][:],
                    start=(g == 0),
                    stop=(g == 1),
                )

        def gelu(unit):
            i, e = divmod(unit[0], 2)
            gl[unit] = stage.tile([P, 512], F32, name="gl", bufs=7)
            nc.scalar.activation(
                out=gl[unit][:], in_=z.pop(unit)[:], func=ACT.Gelu_apprx_tanh, bias=cols[:, e, i : i + 1]
            )

        def turn_h(unit, b):
            tph[unit] = bank_of(b)
            src = gl.pop(unit)
            for j in range(4):
                nc.tensor.transpose(tph[unit][:, P * j : P * (j + 1)], src[:, P * j : P * (j + 1)], ident[:])

        def weigh_h(unit, tile, slot):
            r, h = unit
            hg[unit] = (tile, slot)
            nc.vector.tensor_tensor(
                out=tile[:, slot],
                in0=tph.pop(unit)[:].rearrange("p (j f) -> p f j", j=4),
                in1=sal[r % 2][:, h, :].unsqueeze(1).to_broadcast([P, P, 4]),
                op=ALU.mult,
            )

        def h_tile(width, name="hg", bufs=3):
            return stage.tile([P, width, P, 4], BF16, name=name, align_bytes=64, bufs=bufs)

        def quant_h(*units):
            width = P * len(units)
            cod = stage.tile([P, width], U32, name="hcod", align_bytes=64, bufs=5)
            sca = stage.tile([P, width], U8, name="hsca", align_bytes=64, bufs=5)
            quant(cod[:], sca[:], hg[units[0]][0][:].rearrange("p s f q -> p (s f q)"))
            for unit in units:
                slot = hg.pop(unit)[1]
                hq[unit] = (cod[:, P * slot : P * (slot + 1)], sca[:, P * slot : P * (slot + 1)])

        def gather(r, b):
            e = r % 2
            ab[r] = bank_of(b)
            for st in range(4):
                span = slice(P * st, P * (st + 1))
                for h in range(2):
                    cod, sca = hq[r, h]
                    nc.tensor.matmul_mx(
                        out=ab[r][:, span],
                        lhsT=pcod[e, h][:, span].bitcast(FP8X4),
                        lhsT_scale=psca[e, h][:, span],
                        rhs=cod.bitcast(FP8X4),
                        rhs_scale=sca,
                        start=(h == 0),
                        stop=(h == 1),
                    )

        def row_of(rows_tile, i, width=4):
            return rows_tile[:, P * i : P * (i + 1)].unsqueeze(1).to_broadcast([P, width, P])

        def mix_a(i):
            tv[i] = stage.tile([P, 4, P], F32, name="tv", bufs=2)
            src = ab[2 * i][:].rearrange("p (st f) -> p st f", st=4)
            nc.vector.tensor_tensor(out=tv[i][:], in0=src, in1=row_of(mixrow, i), op=ALU.mult)

        def copy_spans(i):
            av[i] = stage.tile([P, S], F32, name="av", bufs=3)
            nc.scalar.copy(out=av[i][:], in_=ab[2 * i][:])

        def mix_copy(i):
            tv[i] = stage.tile([P, 4, P], F32, name="tv", bufs=2)
            src = av[i][:].rearrange("p (st f) -> p st f", st=4)
            nc.gpsimd.tensor_tensor(out=tv[i][:], in0=src, in1=row_of(mixrow, i), op=ALU.mult)

        def times_b(i):
            uv[i] = stage.tile([P, S], F32, name="uv", bufs=2)
            nc.vector.scalar_tensor_tensor(
                out=uv[i][:],
                in0=tv.pop(i)[:].rearrange("p st f -> p (st f)"),
                scalar=1.0,
                in1=ab.pop(2 * i + 1)[:],
                op0=ALU.add,
                op1=ALU.mult,
            )

        def plus_a(i):
            eo[i] = stage.tile([P, 4, P], F32, name="eo", bufs=4)
            flat = eo[i][:].rearrange("p st f -> p (st f)")
            nc.vector.tensor_tensor(out=flat, in0=ab.pop(2 * i)[:], in1=uv.pop(i)[:], op=ALU.add)
            nc.sync.dma_start(out=out_0.rearrange("(r st) f -> r st f", st=4)[:, :, P * i : P * (i + 1)], in_=eo[i][:])

        def weigh_emb(i, engine, name="vv", bufs=3):
            vv[i] = stage.tile([P, 4, P], F32, name=name, align_bytes=64, bufs=bufs)
            engine.tensor_tensor(out=vv[i][:], in0=eo[i][:], in1=row_of(vrow, i), op=ALU.mult)

        def label_sums(i):
            nc.vector.tensor_reduce(
                out=sums[:, :, 2 * i : 2 * i + 2],
                in_=vv.pop(i)[:].rearrange("p st (c f) -> p st c f", c=2),
                op=ALU.add,
                axis=mybir.AxisListType.X,
            )

        def label_accum(i):
            src = vv.pop(i)
            for st in range(4):
                for c in range(2):
                    part = src[:, st, 64 * c : 64 * (c + 1)]
                    nc.scalar.activation(
                        out=part,
                        in_=part,
                        func=ACT.Identity,
                        bias=dshare[:, 2 * i + c : 2 * i + c + 1],
                        accum_out=score[:, st, 2 * i + c : 2 * i + c + 1],
                    )

        def gather_features(r, b):
            e = r % 2
            ab[r] = bank_of(b)
            for h in range(2):
                cod, sca = hq[r, h]
                nc.tensor.matmul_mx(
                    out=ab[r][:],
                    lhsT=cod.bitcast(FP8X4),
                    lhsT_scale=sca,
                    rhs=pcod[e, h][:].bitcast(FP8X4),
                    rhs_scale=psca[e, h][:],
                    start=(h == 0),
                    stop=(h == 1),
                )

        def emb_factor(i):
            tv[i] = stage.tile([P, S], F32, name="tf", bufs=2)
            nc.scalar.activation(
                out=tv[i][:], in_=ab[2 * i][:], func=ACT.Identity, bias=1.0, scale=cols[:, 2, i : i + 1]
            )

        def emb_product(i, parts=1):
            uv[i] = stage.tile([P, S], F32, name="uf", bufs=2)
            for n in range(parts):
                span = slice(n * S // parts, (n + 1) * S // parts)
                nc.vector.tensor_tensor(out=uv[i][:, span], in0=ab[2 * i + 1][:, span], in1=tv[i][:, span], op=ALU.mult)

        def turn_half(i, half, term, first, banks=HALF_BANKS):
            if first:
                tpe[i, half] = bank_of(banks[half])
            for st in range(2):
                o = P * (2 * half + st)
                nc.tensor.matmul(
                    out=tpe[i, half][:, P * st : P * (st + 1)],
                    lhsT=term[:, o : o + P],
                    rhs=ident[:],
                    is_transpose=True,
                    start=first and st == 0,
                    stop=not first and st == 1,
                )

        def copy_half(i, half):
            eo[i, half] = stage.tile([P, 2, P], F32, name="eh", bufs=2)
            nc.scalar.copy(out=eo[i, half][:].rearrange("p st f -> p (st f)"), in_=tpe[i, half][:, 0 : 2 * P])
            rows_out = out_0.rearrange("(r st) f -> r st f", st=4)[:, 2 * half : 2 * half + 2, P * i : P * (i + 1)]
            nc.sync.dma_start(out=rows_out, in_=eo[i, half][:])

        def copy_a(i):
            av[i] = stage.tile([P, S], F32, name="av", bufs=3)
            nc.scalar.copy(out=av[i][:], in_=ab.pop(2 * i)[:])

        def turn_term(i, term, first):
            for st in range(4):
                nc.tensor.matmul(
                    out=tpe[i][:, P * st : P * (st + 1)],
                    lhsT=term[:, P * st : P * (st + 1)],
                    rhs=ident[:],
                    is_transpose=True,
                    start=first and st == 0,
                    stop=not first and st == 3,
                )

        def copy_emb(i):
            eo[i] = stage.tile([P, 4, P], F32, name="eo", bufs=4)
            nc.scalar.copy(out=eo[i][:].rearrange("p st f -> p (st f)"), in_=tpe[i][:])
            nc.sync.dma_start(out=out_0.rearrange("(r st) f -> r st f", st=4)[:, :, P * i : P * (i + 1)], in_=eo[i][:])

        def weigh_bank(i):
            vv[i] = stage.tile([P, 4, P], F32, name="vv", align_bytes=64, bufs=3)
            row = vrow[:, P * i : P * (i + 1)].unsqueeze(1).to_broadcast([P, 4, P])
            nc.vector.tensor_tensor(
                out=vv[i][:], in0=tpe[i][:].rearrange("p (st f) -> p st f", st=4), in1=row, op=ALU.mult
            )

        def weigh_a(i):
            vv["a"] = stage.tile([P, S], F32, name="va", bufs=1)
            nc.scalar.activation(
                out=vv["a"][:], in_=ab[2 * i][:], func=ACT.Identity, scale=cols[:, 3, i : i + 1], bias=dcol[:]
            )

        def weigh_u(i, half):
            if half == 0:
                vv["u"] = stage.tile([P, S], F32, name="vu", bufs=1)
            span = slice(256 * half, 256 * (half + 1))
            nc.scalar.activation(out=vv["u"][:, span], in_=uv[i][:, span], func=ACT.Copy, scale=cols[:, 3, i : i + 1])

        def label_half(i, half):
            nc.vector.tensor_reduce(
                out=score[:, 2 * half : 2 * half + 2, 2 * i : 2 * i + 2],
                in_=tpe["v", half][:, 0 : 2 * P].rearrange("p (st c f) -> p st c f", st=2, c=2),
                op=ALU.add,
                axis=mybir.AxisListType.X,
            )

        def add_offsets(src, labels):
            width = labels.stop - labels.start
            nc.vector.tensor_tensor(
                out=score[:, :, labels],
                in0=src[:, :, labels],
                in1=dbias[:, labels].unsqueeze(1).to_broadcast([P, 4, width]),
                op=ALU.add,
            )

        with tc.manual_schedule():
            make_identity(nc, ident[:])
            nc.vector.memset(rows[:], 0.0)
            nc.scalar.activation(out=unread[:], in_=rows[:, 0:1], func=ACT.Gelu_apprx_tanh)
            for n in range(2):
                nc.sync.dma_start(out=xa[n][:], in_=xv[0][:, n, :])
            nc.sync.dma_start(out=xs[:], in_=x_scale.rearrange("o (g p t) -> p (o g) t", p=P, t=4))
            load_x(1)
            load_p(0, 0)
            load_x(2)
            load_w(0, 0, [0])
            load_x(3)
            load_w(0, 0, [1])
            load_p(0, 1)
            for q, vec in enumerate((bs, be, mix, v)):
                nc.sync.dma_start(out=rows[NI * q : NI * (q + 1), :], in_=vec.rearrange("(i f) -> i f", f=P))
            load_p(1, 0)
            load_w(1, 0)
            load_p(1, 1)
            for e, gv in enumerate((gs, ge)):
                nc.sync.dma_start(out=sal[e][:], in_=gv.rearrange("(h m j) -> m h j", h=2, j=4))
            load_w(0, 1)
            load_w(1, 1)
            load_w(0, 2)
            nc.sync.dma_start(out=mixrow[:], in_=mix[0 : NS * P].partition_broadcast(P))
            load_w(1, 2)
            nc.sync.dma_start(out=vrow[:], in_=v[0 : NV * P].partition_broadcast(P))
            nc.sync.dma_start(out=dbias[:], in_=d.partition_broadcast(P))
            load_w(0, 3)
            load_w(1, 3)

            def piece(m, g, b, second=nc.scalar):
                cast_x(2 * m, g, nc.scalar)
                cast_x(2 * m + 1, g, second)
                turn_x(m, g, b)

            for n in range(2):
                cast_x(n, 0, nc.vector)
                turn_tile(n, 4 + n)
            piece(0, 1, 0, nc.vector)
            scale_tile(0)
            scale_tile(1)
            piece(1, 0, 1)
            scale_x(0, 1)
            turn_p(0, 0, 0, 4)
            piece(1, 1, 3)
            weave_pass(0)
            weave_pass(1)
            turn_p(0, 0, 1, 5)
            piece(2, 0, 0)
            scale_x(1, 0)
            piece(3, 0, 1)
            scale_x(1, 1)
            turn_p(0, 1, 0, 6)
            piece(2, 1, 2)
            turn_p(0, 1, 1, 7)
            scale_x(2, 0)
            piece(3, 1, 3)
            scale_x(3, 0)
            quant_x(0, 0)
            quant_w()
            quant_x(0, 1)
            both = w_tile(2, "xg01")
            weave(1, nc.gpsimd, both, 0)
            nc.scalar.copy(out=rows32[:], in_=rows[:])
            copy_p(0, 0, 0)
            copy_p(0, 0, 1)
            small = bank_of(0)
            nc.tensor.transpose(small[:, 0:P], rows32[:], ident[:])
            turn_p(1, 0, 0, 4)
            turn_p(1, 0, 1, 5)
            nc.scalar.copy(out=cols[:].rearrange("p q i -> p (q i)"), in_=small[:, 0 : 4 * NI])
            copy_p(0, 1, 0)
            copy_p(0, 1, 1)
            scale_x(2, 1)
            scale_x(3, 1)
            first = [(0, 0), (2, 0), (0, 1), (2, 1), (1, 0), (1, 1)]
            tiles = [h_tile(2), h_tile(4)]
            slots = [(0, 0), (1, 0), (0, 1), (1, 1), (1, 2), (1, 3)]

            def weigh_first(n):
                weigh_h(first[n], tiles[slots[n][0]], slots[n][1])

            project(first[0], 1)
            copy_p(1, 0, 0)
            weave(3, nc.scalar, both, 1, slice(0, 1))
            project(first[1], 0)
            gelu(first[0])
            copy_p(1, 0, 1)
            turn_p(1, 1, 0, 6)
            turn_p(1, 1, 1, 7)
            weave(3, nc.scalar, both, 1, slice(1, 2))
            gelu(first[1])
            copy_p(1, 1, 0)
            quant_x(1, 0)
            quant_x(1, 1)
            quant_p(0, 0)
            quant_rounds(1, 3)
            quant_p(0, 1)
            quant_p(1, 0)
            weave(4, nc.gpsimd, w_tile(1, "pg10"), 0)
            for unit, b in zip(first[2:4], (5, 1)):
                project(unit, b)
                gelu(unit)
            copy_p(1, 1, 1)
            for n, b in enumerate((4, 2, 3)):
                turn_h(first[n], b)
            for unit, b in zip(first[4:], (6, 0)):
                project(unit, b)
                gelu(unit)
            turn_h(first[3], 5)
            for n in range(3):
                weigh_first(n)
            quant_rounds(4)
            quant_h((0, 0), (0, 1))
            quant_p(1, 1)
            weave(5, nc.gpsimd, w_tile(1, "pg11"), 0)
            weave(6, nc.scalar, w_tile(1, "wh"), 0)
            units = [(r, h) for r in (3, 4) for h in range(2)]
            for unit, b in zip(units[:2], (7, 1)):
                project(unit, b)
                gelu(unit)
            weigh_first(3)
            for n, b in zip((4, 5), (4, 6)):
                turn_h(first[n], b)
                weigh_first(n)
            for unit, b in zip(units[2:], (0, 2)):
                project(unit, b)
                gelu(unit)
            gather(0, 5)
            quant_rounds(6)
            quant_h((2, 0), (2, 1), (1, 0), (1, 1))
            quant_rounds(5)
            weave(7, nc.gpsimd, w_tile(1, "pg11"), 0)
            weave(8, nc.scalar, w_tile(1, "wh"), 0)
            tile = h_tile(2)
            for n, b in enumerate((3, 4)):
                turn_h(units[n], b)
            done = units

            waiting = []
            for i in range(5):
                r = 2 * i + 5
                units = [(r + n, h) for n in range(2) for h in range(2)]
                turned = [(3, 4, 0)[(4 * i + n) % 3] for n in range(2, 6)]
                base = len(waiting)
                gather(2 * i + 1, 6)
                weigh_h(done[0], tile, base)
                mix_a(i)
                weigh_h(done[1], tile, base + 1)
                for n in range(2):
                    project(units[n], 1 + n)
                    gelu(units[n])
                if i == 1:
                    nc.scalar.mul(out=dshare[:], in_=dbias[:], mul=C / F)
                if i:
                    label_accum(i - 1)
                times_b(i)
                if i:
                    quant_rounds(*range(r + 2, min(r + 4, NR)))
                else:
                    quant_rounds(8)
                    quant_rounds(7)
                quant_h(*waiting, *done[:2])
                tile = h_tile(4)
                for n in range(2):
                    turn_h(done[2 + n], turned[n])
                weigh_h(done[2], tile, 0)
                plus_a(i)
                weigh_h(done[3], tile, 1)
                waiting = done[2:]
                for n in range(2):
                    project(units[2 + n], 1 + n)
                    gelu(units[2 + n])
                gather(2 * i + 2, (7, 5)[i % 2])
                if i == 3:
                    nc.scalar.copy(out=dcol[0:64], in_=dshare[0:64, C - 2 : C - 1])
                    nc.scalar.copy(out=dcol[64:128], in_=dshare[64:128, C - 1 : C])
                if r + 4 < NR:
                    rounds = range(r + 4, min(r + 6, NR))
                    pair = w_tile(len(rounds), "pg11")
                    for n, q in enumerate(rounds):
                        weave(q, nc.scalar if n else nc.gpsimd, pair, n)
                weigh_emb(i, nc.gpsimd)
                for n in range(2):
                    turn_h(units[n], turned[2 + n])
                done = units

            turn_h(done[2], 4)
            project((15, 0), 1)
            gather(11, 6)
            project((15, 1), 2)
            gelu((15, 0))
            gelu((15, 1))
            label_accum(4)
            mix_a(5)
            weigh_h(done[0], tile, 2)
            weigh_h(done[1], tile, 3)
            tile2 = h_tile(2)
            weigh_h(done[2], tile2, 0)
            quant_h(*waiting, *done[:2])
            turn_h(done[3], 0)
            turn_h((15, 0), 3)
            times_b(5)
            weigh_h(done[3], tile2, 1)
            gather_features(12, 5)
            turn_h((15, 1), 4)
            emb_factor(6)
            copy_a(6)
            last = h_tile(2)
            weigh_h((15, 0), last, 0)
            quant_h(*done[2:])
            weigh_h((15, 1), last, 1)
            gather_features(13, 1)
            gather_features(14, 2)
            emb_factor(7)
            copy_spans(7)
            weigh_a(7)
            emb_product(6)
            quant_h((15, 0), (15, 1))
            plus_a(5)
            weigh_emb(5, nc.gpsimd)
            tpe[6] = bank_of(6)
            turn_term(6, av[6], True)
            turn_term(6, uv[6], False)
            gather_features(15, 0)
            for half in range(2):
                turn_half(7, half, av[7], True)
            for half in range(2):
                turn_half("v", half, vv["a"], True, (4, 1))
            weigh_bank(6)
            emb_product(7, 2)
            copy_emb(6)
            weigh_u(7, 0)
            weigh_u(7, 1)
            for half in range(2):
                turn_half(7, half, uv[7], False)
            for half in range(2):
                turn_half("v", half, vv["u"], False)
                copy_half(7, half)
            label_sums(6)
            label_sums(5)
            label_half(7, 0)
            add_offsets(sums, slice(10, 14))
            label_half(7, 1)
            nc.sync.dma_start(out=out_1.rearrange("(r st) c -> r st c", st=4), in_=score[:])
